import numpy as np, ml_dtypes
CORES = [40,41,42,43,44,45,46,47]
N = 8
import mx_ref
BF = ml_dtypes.bfloat16
def cut(t, i, w=512):
    return t[:, w * i:w * i + w]
def pick(q, e):
    c = np.concatenate([q[0].reshape(128, -1, 4), np.zeros((128, 1, 4), np.uint8)], axis=1); s = np.concatenate([q[1], np.ones((16, 1), np.uint8)], axis=1)
    return (np.ascontiguousarray(c[:, e].reshape(128, -1)), np.ascontiguousarray(s[:, e]))
def join(*qs):
    return (np.concatenate([q[0] for q in qs], axis=1), np.concatenate([q[1] for q in qs], axis=1))
def put(q, e, v):
    c, s = q[0].reshape(128, -1, 4).copy(), q[1].copy(); c[:, e] = v[0].reshape(128, -1, 4); s[:, e] = v[1]
    return (c.reshape(128, -1), s)
def pk(c, s):
    return (np.ascontiguousarray(c), mx_ref.live(s))
def emit(q):
    return q[0], q[1]
def decode(q):
    o = []
    for b in range(4):
        e = np.zeros((128, 128, 4), np.float32); e[np.arange(128), np.arange(128), b] = 1
        o.append(mx_ref.matmul(mx_ref.quantize(e.reshape(128, 512).astype(BF)), q))
    return np.stack(o, axis=2).reshape(128, -1)
def f(rng, *shape):
    return mx_ref.flush((rng.standard_normal(shape, dtype=np.float32) * np.exp2(rng.integers(-2, 3, shape[:-1] + (1,)))).astype(BF))
def wide(rng, *shape, cols=0):
    v = rng.standard_normal(shape, dtype=np.float32) * np.exp2(rng.integers(-12, 13, shape)).astype(np.float32)
    if cols: v *= np.repeat(np.exp2(rng.integers(-cols, cols + 1, shape[:-2] + (1, shape[-1] // 4))) * (rng.random(shape[:-2] + (1, shape[-1] // 4)) > 0.0625), 4, axis=-1).astype(np.float32)
    return mx_ref.flush(v.astype(BF))
P, K, O = 256, 64, 1
def places(t, j):
    return (j + t * np.arange(N)[:, None]) % P
def checks(tab, u):
    return np.stack([mx_ref.matmul(mx_ref.quantize(np.ascontiguousarray(u[r])), tab[r])[:2] for r in range(N)], axis=1)
def judge(c, g, t):
    j = np.arange(P)
    p = (j + t) % N
    at = places(t, j)
    c, a = c[np.arange(N)[:, None], at], np.abs(g[np.arange(N)[:, None], at])
    s = c[p, j]
    for r in range(N):
        s = np.where(p == r, s, s - c[r])
    bad = np.argsort(-np.abs(s), kind="stable")[:K]
    a[p, j] = -1
    return bad, np.argmax(a, axis=0)[bad]
def rebuilt(tab, bad, lost, t):
    at = places(t, bad)
    v = decode(join(*[pick(tab[r], at[r]) for r in range(N)])).reshape(128, N, K, 4)
    new = np.zeros((128, K, 4), np.float32)
    for k in range(K):
        p = (bad[k] + t) % N
        x = v[:, p, k]
        for r in range(N):
            if r != p and r != lost[k]: x = x - v[:, r, k]
        new[:, k] = x
    return mx_ref.quantize(np.ascontiguousarray(new.reshape(128, -1).astype(BF)))
def data(rng):
    return f(rng, N, 128, 4 * P).astype(np.float32).reshape(N, 128, P, 4)
def striped(v):
    v = v.copy()
    for r in range(N):
        j = np.arange(r, P, N)
        v[r][:, j] = 0
        v[r][:, j] = np.sum(v[:, :, j], axis=0)
    return v
def harm(rng, v, stripes, size):
    for j in stripes:
        v[(j + rng.integers(1, N)) % N][:, j] = size * rng.standard_normal((128, 4))
def queries(rng):
    q = np.array(f(rng, 1, 128, 512))
    q[:, :, 8:] = 0
    return np.concatenate([q] * N)
def draw(rng, v, q=None):
    v = v.astype(np.float32).reshape(N, 128, 4 * P)
    v[np.abs(v) < np.float32(2.0 ** -16)] = 0
    return {"tb": v.astype(BF), "u": queries(rng) if q is None else q, "w": f(rng, N, 128, 512 * O)}
def setup_inputs(rng):
    v = striped(data(rng))
    harm(rng, v, rng.permutation(P)[:K + 6], 8)
    return draw(rng, v)
def setup_inputs_again(rng):
    v, q = striped(data(rng) * np.float32(2.0 ** -8)), queries(rng)
    s = np.where(q[0, :, 4:8].astype(np.float32) < 0, -1.0, 1.0)
    q[:, :, :4] = (np.abs(q[:, :, :4].astype(np.float32)) * s).astype(BF)
    q[:, :32, :4] = 0
    on = (np.arange(128) < 32)[:, None]
    at = N * rng.permutation(P // N)[:K // 2] + 2 * rng.integers(0, N // 2, K // 2) + np.arange(K // 2) % 2
    for j in at:
        p = int(j) % N
        m = (p + int(rng.integers(1, N))) % N
        if p % 2:
            m = ((p + 1) // 2 + N // 2 * int(rng.integers(0, 2))) % N
            if m == p: m = (m + N // 2) % N
        v[m][:, j] = 2.0 ** -4 * (1 + rng.random((128, 4))) * s * on
        v[p][:, j] = (2.0 ** 5 if p % 2 else -2.0 ** 5) * (1 + rng.random((128, 4))) * s
    return draw(rng, v, q)
def setup_inputs_one(rng):
    v, q = striped(data(rng)), queries(rng)
    s = np.where(q[0, :, :4].astype(np.float32) < 0, -1.0, 1.0)
    q[:, :, 4:8] = (np.abs(q[:, :, 4:8].astype(np.float32)) * s).astype(BF)
    m, i = int(rng.integers(0, N)), np.arange(P)
    at = rng.permutation(np.flatnonzero((i % N != m) & ((i - m + 1) % N != m)))[:2 * K]
    size = np.repeat([2.0 ** 16, 2.0 ** 11], K)
    v[m][:, at] = (1 + rng.random((128, 2 * K, 4))) * s[:, None] * size[:, None]
    return draw(rng, v, q)
def setup_inputs_spread(rng):
    q = (queries(rng).astype(np.float32) * np.float32(2.0 ** 20)).astype(BF)
    return draw(rng, wide(rng, N, 128, 4 * P, cols=6), q)
def setup_inputs_ties(rng):
    v, q = np.zeros((N, 128, P, 4), np.float32), queries(rng)
    s = np.where(q[0, :, 4:8].astype(np.float32) < 0, -1.0, 1.0)
    q[:, :32, :4] = 0
    on = (np.arange(128) < 32)[:, None]
    for p in range(N):
        at = p + N * rng.permutation(P // N)
        for g in range(P // N // 3):
            x = 2.0 ** -2 * rng.standard_normal((N, 128, 1, 4))
            a, b, m = (p + 1 + rng.permutation(N - 1)[:3]) % N
            x[p] *= 2.0 ** 22
            x[m] = x[p]
            x[a, :, 0] = np.where(on, 2.0 ** 23 * (1 + rng.random((128, 4))) * s, x[a, :, 0])
            x[b] = x[a] * rng.choice([-1.0, 1.0])
            v[:, :, at[3 * g:3 * g + 3]] = x * rng.choice([-1.0, 1.0], (3, 1))
    return draw(rng, v, q)
def setup_inputs_zero(rng):
    v = striped(data(rng))
    lo, hi = int(rng.integers(0, K // 4 + 1)), int(rng.integers(K // 2, P - K // 4 + 1))
    v[:, :, :hi] = 0
    v[:, :, hi + K // 4:] = 0
    for j in range(lo, lo + K // 4):
        m, n = (j + 1 + rng.permutation(N - 1)[:2]) % N
        v[m][:, j] = 4 * rng.standard_normal((128, 4))
        v[n][:, j] = -v[m][:, j]
    harm(rng, v, np.arange(hi, hi + K // 4), 8)
    return draw(rng, v)
def check_inputs(d):
    b = []
    for k, lo, hi in (("tb", -16, 24), ("u", -30, 30), ("w", -30, 30)):
        v = np.abs(d[k].astype(np.float32))
        if not (np.isfinite(v).all() and ((v == 0) | (v >= 2.0 ** lo) & (v <= 2.0 ** hi)).all()): b.append("a value of " + k)
    q = d["u"].astype(np.float32)
    if (q[:, :, 8:] != 0).any(): b.append("u has numbers behind its first 2 columns")
    if (q != q[:1]).any(): b.append("u isn't the same on all ranks")
    return b
def reference(tb, u, w):
    tab = [mx_ref.quantize(np.ascontiguousarray(tb[r])) for r in range(N)]
    bs = np.zeros((N, 4, K), np.float32)
    for t in range(2):
        c, g = checks(tab, u)
        bad, lost = judge(c, g, t)
        new = rebuilt(tab, bad, lost, t)
        at = places(t, bad)
        for r in range(N):
            e = np.flatnonzero(lost == r)
            tab[r] = put(tab[r], at[r, e], pick(new, e))
        bs[:, 2 * t] = bad
        bs[:, 2 * t + 1] = lost
    oc, osc, y = np.zeros((N, 128, 4 * P), np.uint8), np.zeros((N, 16, P), np.uint8), np.zeros((N, 128, O * P), np.float32)
    for r in range(N):
        oc[r], osc[r] = emit(tab[r])
        for o in range(O):
            y[r, :, o * P:o * P + P] = mx_ref.matmul(mx_ref.quantize(np.ascontiguousarray(cut(w[r], o))), tab[r])
    return {"oc": oc, "osc": osc, "bs": bs, "y": y}

@@ -1,0 +1,547 @@
+from concourse.bass import DstId, RemoteDMATransfer
+from concourse.mybir import dt, AluOpType, AxisListType, ActivationFunctionType
+
+OP = AluOpType
+AF = ActivationFunctionType
+X = AxisListType.X
+N, P, K, NO, KO = 8, 256, 64, 4, 16
+BIG = 1e29
+STEP = 1.0 - 2.0 ** -24
+TINY = 2.0 ** -118
+FR = 2.0 ** -8
+
+F4 = "float8_e4m3fn_x4"
+SCRATCH = {}
+VIEW = {}
+
+
+def _sb(name, n, ty="float32"):
+    SCRATCH[name] = ("sbuf", [128, n], ty)
+
+
+def _mx(name, n):
+    _sb(name, n, F4)
+    _sb(name + "s", n, "uint8")
+
+
+def _parts(buf, *parts):
+    c = 0
+    for name, n in parts:
+        VIEW[name] = (buf, c)
+        c += n + -n % 4
+    _sb(buf, c)
+
+
+for _n, _w in (("tbt", 4 * P), ("ut", 512), ("wt", 512), ("ee", 528), ("zt", 512)):
+    _sb(_n, _w, "bfloat16")
+_parts("con", ("rc", 40), ("hm", 32), ("jc", 1), ("hx", 32), ("hy", 32), ("rf", 40), ("dl0", 8), ("fb", 8), ("st", 2), ("sd32", 32),
+       ("sp", 16), ("one", 32), ("frc", 32), ("oc", 8), ("klc", 16), ("ng", 4), ("eq0", 32), ("eq1", 32), ("dm0", 32), ("dm1", 32),
+       ("gm0", 16), ("gm1", 16), ("lof", 4), ("vj0", 32), ("vj1", 32), ("pr", 64), ("l16", 64), ("t3", 64), ("t4", 64), ("t5", 64),
+       ("t6", 64), ("t7", 64), ("t8", 64))
+for _n, _w in (("nat", 528), ("x16", 272), ("xa0", 256), ("xa1", 256), ("xm0", 256), ("xm1", 256), ("md", 128),
+               ("sd", 256), ("dpat", 128), ("yb", 256), ("ya", P + K), ("lt", 64), ("wt01", 64), ("tab", 128)):
+    _sb(_n, _w)
+_sb("pi", 2, "int32")
+_sb("ib", 8, "int32")
+_sb("cl", 2, "uint16")
+_sb("lo", 4, "uint16")
+_sb("dl", 8, "uint16")
+_sb("gl", 2, "uint16")
+for _n, _w in (("tA", P), ("tB", P), ("F", P), ("uq", 128), ("wq", 128), ("eq", 512)):
+    _mx(_n, _w)
+for _t in "01":
+    _parts("jd" + _t, ("d1" + _t, 32), ("so" + _t, 32), ("du" + _t, 64), ("lw" + _t, 32), ("px" + _t, 16), ("tl" + _t, 64), ("rk" + _t, 4),
+           ("tt" + _t, 128), ("xs" + _t, 8), ("ys" + _t, 8), ("xb" + _t, 4), ("jf" + _t, 4), ("fr" + _t, 4), ("zz" + _t, 16),
+           ("zo" + _t, 8), ("nd" + _t, 1), ("wg" + _t, 64), ("wb" + _t, 64), ("wc" + _t, 64), ("wd" + _t, 64), ("we" + _t, 64),
+           ("wf" + _t, 64), ("th" + _t, 256), ("cm" + _t, 260), ("ca" + _t, 2), ("cb" + _t, 2), ("ls" + _t, 2), ("rl" + _t, 256),
+           ("cj" + _t, 256), ("lj" + _t, 16), ("mm" + _t, 256))
+    for _n, _w in (("L", 32), ("S", 256), ("Lz", 64), ("val", 32), ("D", 256), ("dd", 128), ("bk", 64), ("lk", 64), ("M", 256)):
+        _sb(_n + _t, _w)
+    for _n, _w in (("R", 2), ("of", 4), ("cd", 4), ("oo", 2), ("lc", 2), ("ml", 16), ("oi", 8)):
+        _sb(_n + _t, _w, "uint16")
+    _sb("h" + _t, 512, "bfloat16")
+    for _n, _w in (("slot", K), ("land", 256), ("ord", 128), ("new", 128), ("W", P + K)):
+        _mx(_n + _t, _w)
+SCRATCH["pc"] = ("psum", [128, 1024], "float32")
+SCRATCH["dec"] = ("psum", [128, 2048], "float32")
+SCRATCH["py"] = ("psum", [128, 1024], "float32")
+PSUM = ("pc", "dec", "py")
+
+SEMAPHORES = ["qv", "qs", "qt", "qg", "out", "ld_u", "ld_a", "ld_b", "ld_w", "st_c", "st_s", "st_y",
+              "st_b0", "st_b1", "ck0", "ck1", "col0", "col0s", "col1", "col1s", "new0", "new0s", "new1", "new1s"]
+
+
+def rank_program(g, core, T, topo):
+    rank = T.rank_of(core)
+    if rank is None:
+        return
+    eng = {"v": g.vector, "s": g.scalar, "t": g.tensor, "g": g, "y": g.sync}
+    count = {"v": 0, "s": 0, "t": 0, "g": 0}
+    seen = {e: {} for e in eng}
+    wrote, read = {}, {}
+    final = {}
+
+    def A(name, c0, c1, st=1, p0=0, p1=128):
+        if name in VIEW:
+            name, c = VIEW[name]
+            c0, c1 = c0 + c, c1 + c
+        ap = T[name][p0:p1, c0:c1] if st == 1 else T[name][p0:p1, c0:c1:st]
+        cols = frozenset(c // 512 for c in range(c0, c1, st)) if name in PSUM else frozenset(range(c0, c1, st))
+        return (name, p0, p1, cols, ap)
+
+    def hits(table, r):
+        for (p0, p1, cols, tok) in table.get(r[0], ()):
+            if p0 < r[2] and r[1] < p1 and not cols.isdisjoint(r[3]):
+                yield tok
+
+    def wait(e, sem, val):
+        if seen[e].get(sem, 0) < val:
+            eng[e].wait_ge(T.sem[sem], val)
+            seen[e][sem] = val
+
+    def order(e, ins, outs):
+        need = {}
+        for rs, table, same in ((ins, wrote, True), (outs, wrote, True), (outs, read, False)):
+            for r in rs:
+                for sem, val, src in hits(table, r):
+                    if src != e or (same and r[0] not in PSUM) or rs is ins:
+                        need[sem] = max(need.get(sem, 0), val)
+        for sem, val in need.items():
+            wait(e, sem, val)
+
+    def note(ins, outs, tok):
+        for r in ins:
+            read.setdefault(r[0], []).append((r[1], r[2], r[3], tok))
+        for r in outs:
+            wrote.setdefault(r[0], []).append((r[1], r[2], r[3], tok))
+
+    def op(e, outs, ins, call):
+        order(e, ins, outs)
+        inst = call()
+        count[e] += 1
+        inst.then_inc(T.sem["q" + e], 1)
+        final["q" + e] = count[e]
+        note(ins, outs, ("q" + e, count[e], e))
+
+    def dma(e, out, in_, sem, total, out_ap=None, in_ap=None):
+        order(e, [in_] if in_ else [], [out] if out else [])
+        o = out_ap if out_ap is not None else out[4]
+        i = in_ap if in_ap is not None else in_[4]
+        eng[e].dma_start(o, i).then_inc(T.sem[sem], 16)
+        final[sem] = total
+        note([in_] if in_ else [], [out] if out else [], (sem, total, "dma"))
+
+    def tt(out, a, b, o):
+        op("v", [out], [a, b], lambda: g.vector.tensor_tensor(out[4], a[4], b[4], o))
+
+    def ts(out, a, s1, s2, o0, o1=None):
+        ins = [a] + [s for s in (s1, s2) if isinstance(s, tuple)]
+        v1 = s1[4] if isinstance(s1, tuple) else s1
+        v2 = s2[4] if isinstance(s2, tuple) else s2
+        if o1 is None:
+            op("v", [out], ins, lambda: g.vector.tensor_scalar(out[4], a[4], v1, None, o0))
+        else:
+            op("v", [out], ins, lambda: g.vector.tensor_scalar(out[4], a[4], v1, v2, o0, o1))
+
+    def act(out, a, f, bias=None, scale=None, total=None):
+        ins = [a] + [s for s in (bias, scale) if isinstance(s, tuple)]
+        kw = {}
+        if bias is not None:
+            kw["bias"] = bias[4] if isinstance(bias, tuple) else bias
+        if scale is not None:
+            kw["scale"] = scale[4] if isinstance(scale, tuple) else scale
+        if total is not None:
+            kw["accum_out"] = total[4]
+        op("s", [out] if total is None else [out, total], ins, lambda: g.scalar.activation(out[4], a[4], f, **kw))
+
+    def cp(e, out, a):
+        if e == "v":
+            op("v", [out], [a], lambda: g.vector.tensor_copy(out[4], a[4]))
+        else:
+            act(out, a, AF.Copy)
+
+    def fill(out, x):
+        op("v", [out], [], lambda: g.vector.memset(out[4], x))
+
+    def const(out, x, like):
+        act(out, like, AF.Identity, bias=x, scale=0.0)
+
+    def red(out, a, o):
+        op("v", [out], [a], lambda: g.vector.tensor_reduce(out[4], a[4], X, o))
+
+    def scan(out, d0, d1, o0, o1, first=None):
+        op("v", [out], [d0, d1] + ([first] if first else []),
+           lambda: g.vector.tensor_tensor_scan(out[4], d0[4], d1[4], first[4] if first else 0.0, o0, o1))
+
+    def turn(out, a):
+        op("v", [out], [a], lambda: g.vector.transpose(out[4], a[4]))
+
+    def iota(out, pat, base, cm, flag=True):
+        kw = {"allow_small_or_imprecise_dtypes": True} if flag else {}
+        op("g", [out], [], lambda: g.iota(out[4], pat, base, cm, **kw))
+
+    def gather(e, out, win, off, f=AF.Copy):
+        if e == "v":
+            op("v", [out], [win, off], lambda: g.vector.tensor_copy(out[4], win[4].indirect(off[4])))
+        else:
+            op("s", [out], [win, off], lambda: g.scalar.activation(out[4], win[4].indirect(off[4]), f))
+
+    def gather_tt(out, win, off, b, o):
+        op("v", [out], [win, off, b], lambda: g.vector.tensor_tensor(out[4], win[4].indirect(off[4]), b[4], o))
+
+    def scatter(win, off, val):
+        op("v", [win], [val, off], lambda: g.vector.tensor_copy(win[4].indirect(off[4]), val[4]))
+
+    def pickc(dst, c0, c1, src, n, off):
+        o, i = A(dst, c0, c1), A(src, 0, n)
+        op("v", [o], [i, off], lambda: g.vector.tensor_copy(o[4].bitcast(dt.uint32), i[4].bitcast(dt.uint32).indirect(off[4])))
+
+    def picks(e, dst, c0, c1, src, n, off):
+        gather(e, A(dst + "s", c0, c1), A(src + "s", 0, n), off)
+
+    def pick(dst, c0, c1, src, n, off):
+        pickc(dst, c0, c1, src, n, off)
+        picks("s", dst, c0, c1, src, n, off)
+
+    def pick2(dst, n1, src, n, off, k):
+        for h in range(2):
+            pickc(dst, n1 * h, n1 * h + n1, src, n, A(off, k * h, k * h + k))
+        for h, e in ((0, "s"), (1, "v")):
+            picks(e, dst, n1 * h, n1 * h + n1, src, n, A(off, k * h, k * h + k))
+
+    def quant(dst, c0, c1, tile, at):
+        o, s, i = A(dst, c0, c1), A(dst + "s", c0, c1), A(tile, at, at + 4 * (c1 - c0))
+        op("v", [o, s], [i], lambda: g.vector.quantize_mx(o[4], s[4], i[4]))
+
+    def mm(out, lhs, a, rhs, b0, b1):
+        l, ls, r, rs = A(lhs, a, a + 128), A(lhs + "s", a, a + 128), A(rhs, b0, b1), A(rhs + "s", b0, b1)
+        op("t", [out], [l, ls, r, rs], lambda: g.tensor.matmul_mx(out[4], l[4], ls[4], r[4], rs[4], True, True))
+
+    peers = [c for c in T.cores if c != core]
+
+    def dest(c):
+        rid, pid, _s = topo.addr(c)
+        return DstId(rid=rid, pnc=pid)
+
+    def raw(r, codes):
+        return r[4].bitcast(dt.uint8) if codes else r[4]
+
+    def spread(ref, sem, codes=False):
+        order("g", [ref], [])
+        m = topo.mask(core, peers[0])
+        for c in peers:
+            m &= topo.mask(core, c)
+        g.remote_dma_fused([RemoteDMATransfer(dst_ids=[dest(c) for c in peers], dma_engine_mask=m, remote_sem=T.sem[sem],
+                                              srcs=[raw(ref, codes)], dsts=[raw(ref, codes) for _ in peers])],
+                           local_sem=T.sem["out"])
+        final["out"] = final.get("out", 0) + bin(m).count("1")
+
+    full = len(topo.engines(core, peers[0]))
+
+    def landed(refs, sem, total):
+        note([], refs, (sem, total, "remote"))
+        final[sem] = total
+
+    def deal(t, codes):
+        tr = []
+        for o in range(NO):
+            c = T.cores[2 * o + t]
+            if c == core:
+                continue
+            es = topo.engines(core, c)
+            w = len(es) // NO
+            s = "" if codes else "s"
+            src = A("slot%d" % t + s, KO * o, KO * o + KO)
+            order("g", [src], [])
+            d = A("land%d" % t + s, KO * rank, KO * rank + KO)
+            tr.append(RemoteDMATransfer(dst_ids=[dest(c)], dma_engine_mask=sum(1 << e for e in es[w * o:w * o + w]),
+                                        remote_sem=T.sem["col%d" % t + s], srcs=[raw(src, codes)], dsts=[raw(d, codes)]))
+            final["out"] = final.get("out", 0) + w
+        g.remote_dma_fused(tr, local_sem=T.sem["out"])
+
+    own = rank % 2
+    o_ = rank // 2
+    a0 = KO * o_
+
+    dma("y", A("tbt", 0, 512), None, "ld_a", 16, in_ap=T.tb[:, 0:512])
+    dma("s", A("ut", 0, 8), None, "ld_u", 16, in_ap=T.u[:, 0:8])
+    dma("s", A("tbt", 512, 1024), None, "ld_b", 16, in_ap=T.tb[:, 512:1024])
+    wait("y", "ld_b", 16)
+    dma("y", A("wt", 0, 512), None, "ld_w", 16, in_ap=T.w[:])
+
+    iota(A("pi", 0, 2), [[1, 2]], 0, 1, False)
+    iota(A("nat", 0, 128), [[1, 128]], 0, 0)
+    iota(A("rc", 0, 40), [[0, 5], [1, 8]], 0, 0)
+    iota(A("hm", 0, 32), [[0, 2], [1, 2], [0, 8]], 0, 0)
+    iota(A("jc", 0, 1), [[1, 1]], 0, 1)
+    iota(A("lt", 0, 64), [[0, 8], [1, 8]], 0, 0)
+    iota(A("pr", 0, 64), [[16, 8], [0, 8]], 0, 0)
+    iota(A("hx", 0, 32), [[128, 2], [1, 16]], 0, 0)
+    iota(A("dl0", 0, 8), [[16, 4], [0, 2]], 0, 0)
+    fill(A("ut", 8, 512), 0.0)
+    fill(A("one", 0, 32), 1.0)
+    fill(A("frc", 0, 32), FR)
+    for col, (src, bits) in enumerate(((0, 7), (1, 7), (0, 31), (0, 15), (0, 8), (0, 112), (0, 64), (0, 32))):
+        ts(A("ib", col, col + 1), A("pi", src, src + 1), bits, None, OP.bitwise_and)
+    cp("v", A("fb", 0, 8), A("ib", 0, 8))
+
+    def masks(t):
+        n = str(t)
+        ts(A("eq" + n, 0, 32), A("rc", 0, 32), A("fb", t, t + 1), -1.0, OP.is_equal, OP.mult)
+        ts(A("gm" + n, 0, 16), A("rc", 0, 16), A("fb", t, t + 1), BIG, OP.is_equal, OP.mult)
+        tt(A("dm" + n, 0, 32), A("eq" + n, 0, 32), A("hm", 0, 32), OP.add)
+
+    masks(0)
+    quant("uq", 0, 128, "ut", 0)
+    act(A("nat", 128, 256), A("nat", 0, 128), AF.Identity, bias=128.0)
+    act(A("nat", 256, 512), A("nat", 0, 256), AF.Identity, bias=256.0)
+    act(A("nat", 512, 528), A("nat", 0, 16), AF.Identity, bias=512.0)
+    act(A("ng", 0, 1), A("jc", 0, 1), AF.Identity, bias=4.0, scale=4.0)
+
+    def checks(t, tab, half, e0):
+        for h in range(2):
+            half(h)
+            mm(A("pc", 512 * h, 512 * h + 128), tab, 128 * h, "uq", 0, 128)
+        for h, e in ((0, e0), (1, "v")):
+            cp(e, A("L%d" % t, 4 * rank + 2 * h, 4 * rank + 2 * h + 2), A("pc", 512 * h, 512 * h + 2))
+        spread(A("L%d" % t, 4 * rank, 4 * rank + 4), "ck%d" % t)
+        landed([A("L%d" % t, 4 * r, 4 * r + 4) for r in range(N) if r != rank], "ck%d" % t, 7 * full)
+
+    checks(0, "tA", lambda h: quant("tA", 128 * h, 128 * h + 128, "tbt", 512 * h), "v")
+
+    iota(A("D0", 0, 256), [[0, 256]], 0, 0)
+    iota(A("x16", 0, 272), [[0, 17], [1, 16]], 0, 0)
+    iota(A("D1", 0, 256), [[0, 256]], 0, 0)
+    ts(A("lo", 0, 1), A("fb", 0, 1), 4.0, None, OP.mult)
+    ts(A("lo", 1, 2), A("fb", 0, 1), 4.0, 2.0, OP.mult, OP.add)
+    act(A("lof", 0, 1), A("fb", 4, 5), AF.Identity, bias=1.0, scale=0.25)
+    act(A("lof", 1, 2), A("fb", 0, 1), AF.Identity, bias=A("lof", 0, 1), scale=4.0)
+    cp("s", A("sd32", 0, 32), A("one", 0, 32))
+    const(A("sd32", 0, 32, 16), 0.0, A("nat", 0, 2))
+    const(A("sp", 0, 16), 0.0, A("nat", 0, 16))
+    const(A("sp", 0, 16, 8), -BIG, A("nat", 0, 2))
+    act(A("rf", 0, 40), A("rc", 0, 40), AF.Copy, scale=8.0 * FR)
+    for t in "01":
+        const(A("cm" + t, 256, 257), 128.0, A("nat", 0, 1))
+
+    def owner():
+        act(A("oc", 0, 1), A("fb", 0, 1), AF.Identity, bias=-16.0, scale=16.0)
+        act(A("oc", 1, 2), A("fb", 0, 1), AF.Relu, bias=-16.0, scale=16.0)
+        act(A("oc", 2, 3), A("fb", 0, 1), AF.Relu, bias=1.0, scale=-1.0)
+        act(A("oc", 3, 4), A("fb", 4, 5), AF.Copy, scale=0.125)
+        act(A("oc", 4, 5), A("fb", 4, 5), AF.Identity, bias=1.0, scale=-0.125)
+        act(A("oc", 5, 6), A("fb", 4, 5), AF.Copy, scale=8.0)
+        act(A("oc", 6, 7), A("fb", 4, 5), AF.Identity, bias=7.0)
+        act(A("klc", 0, 8), A("nat", 0, 8), AF.Copy, scale=A("oc", 4, 5))
+        act(A("klc", 8, 16), A("nat", 8, 16), AF.Copy, scale=A("oc", 3, 4))
+        act(A("l16", 0, 64), A("lt", 0, 64), AF.Copy, scale=16.0)
+        act(A("t4", 0, 64), A("pr", 0, 64), AF.Identity, bias=A("oc", 1, 2), scale=A("oc", 2, 3))
+        const(A("dpat", 0, 128), 1.0, A("nat", 0, 128))
+        const(A("dpat", 0, 128, 8), 0.0, A("nat", 0, 16))
+        const(A("dpat", 1, 128, 8), -1.0, A("nat", 0, 16))
+
+    def owner_v():
+        fill(A("zt", 0, 512), 0.0)
+        ts(A("ee", 0, 528), A("nat", 0, 528), A("ng", 0, 1), None, OP.is_equal)
+        quant("land%d" % own, 128, 256, "zt", 0)
+        for b in range(4):
+            quant("eq", 128 * b, 128 * b + 128, "ee", 4 - b)
+        ts(A("cl", 0, 1), A("fb", 0, 1), 16.0, A("oc", 6, 7), OP.mult, OP.add)
+
+    def owner_t():
+        ts(A("t3", 0, 64), A("pr", 0, 64), A("oc", 0, 1), 16.0, OP.is_le, OP.mult)
+        tt(A("t5", 0, 64), A("t3", 0, 64), A("t4", 0, 64), OP.add)
+        tt(A("t6", 0, 64), A("t5", 0, 64), A("l16", 0, 64), OP.is_equal)
+        act(A("t7", 0, 64), A("t6", 0, 64), AF.Copy, scale=128.0)
+        tt(A("t8", 0, 64), A("t5", 0, 64), A("t7", 0, 64), OP.add)
+        act(A("tab", 0, 64), A("t8", 0, 64), AF.Copy, scale=A("oc", 4, 5))
+        act(A("tab", 64, 128), A("t8", 0, 64), AF.Copy, scale=A("oc", 3, 4))
+
+    cp("v", A("lo", 2, 3), A("lof", 1, 2))
+    ts(A("gl", 0, 1), A("fb", 2, 3), 0.0, None, OP.add)
+    ts(A("gl", 1, 2), A("fb", 2, 3), 32.0, None, OP.add)
+    if own == 0:
+        owner()
+        owner_v()
+    else:
+        quant("W0", 0, 256, "tbt", 0)
+    act(A("st", 0, 1), A("fb", 6, 7), AF.Identity, bias=1.0, scale=(STEP - 1.0) / 64)
+    act(A("st", 1, 2), A("fb", 7, 8), AF.Identity, bias=1.0, scale=(STEP - 1.0) / 32)
+    for s, c in ((1, 0), (2, 1), (3, 0)):
+        act(A("md", 32 * s, 32 * s + 32), A("one", 0, 32), AF.Copy, scale=A("st", c, c + 1))
+    ts(A("md", 0, 32), A("nat", 0, 32), A("fb", 2, 3), STEP, OP.is_ge, OP.max)
+    ts(A("dl", 0, 8), A("dl0", 0, 8), A("fb", 3, 4), None, OP.add)
+    ts(A("hy", 0, 32), A("hx", 0, 32), A("fb", 5, 6), None, OP.add)
+    for t in range(2):
+        tt(A("vj%d" % t, 0, 32), A("hy", 0, 32), A("rf", t, t + 32), OP.add)
+    if own == 0:
+        owner_t()
+    ts(A("wt01", 0, 64), A("lt", 0, 64), float(rank), None, OP.is_equal)
+
+    def shift(t):
+        return rank if t == 0 else -rank % P
+
+    def lanes(t):
+        n, c = str(t), -shift(t) % 16
+        act(A("xa" + n, 0, 256), A("x16", c, c + 256), AF.Abs, bias=A("ng", 1, 2))
+        act(A("xm" + n, 0, 256), A("xa" + n, 0, 256), AF.Relu, bias=1.0, scale=-1.0)
+
+    def judge(t, tab):
+        n = lambda s: s + str(t)
+        L, d1, so, du, S, lw, px, tl = n("L"), n("d1"), n("so"), n("du"), n("S"), n("lw"), n("px"), n("tl")
+        th, cm, cj, rl, ca, cb, ls, rk, R = n("th"), n("cm"), n("cj"), n("rl"), n("ca"), n("cb"), n("ls"), n("rk"), n("R")
+        i = A(L, 0, 32)
+        gather_tt(A(d1, 0, 32), i, A("lo", 0, 2), A(n("dm"), 0, 32), OP.mult)
+        gather("s", A(lw, 0, 16), i, A("lo", 2, 3), AF.Abs)
+        scan(A(so, 0, 32), A("sd32", 0, 32), A(d1, 0, 32), OP.mult, OP.subtract)
+        for h in range(2):
+            act(A(du, 32 * h, 32 * h + 32), A("one", 0, 32), AF.Abs, bias=TINY, scale=A(so, 16 * h + 15, 16 * h + 16))
+        tt(A(lw, 16, 32), A(lw, 0, 16), A(n("gm"), 0, 16), OP.subtract)
+        scan(A(px, 0, 16), A("sp", 0, 16), A(lw, 16, 32), OP.add, OP.max)
+        for h in range(2):
+            turn(A(S, 128 * h, 128 * h + 32), A(du, 32 * h, 32 * h + 32))
+        for h in range(2):
+            act(A(n("lj"), 8 * h, 8 * h + 8), A(px, 8 * h, 8 * h + 8), AF.Sign, bias=A(px, 8 * h + 7, 8 * h + 8), scale=-1.0,
+                total=A(ls, h, h + 1))
+        for h in range(2):
+            act(A(tl, 32 * h, 32 * h + 32), A("frc", 0, 32), AF.Copy, scale=A(ls, h, h + 1))
+        for h in (0, 128):
+            cp("v", A(S, h + 32, h + 64, 1, 0, 64), A(S, h, h + 32, 1, 64, 128))
+            cp("s", A(S, h + 32, h + 64, 1, 64, 128), A(S, h, h + 32, 1, 0, 64))
+        ts(A(th, 128, 256), A("md", 0, 128), A(du, 32, 33), None, OP.mult)
+        for h in (0, 128):
+            for a, e in ((0, "v"), (2, "s"), (1, "v"), (3, "s")):
+                b = a ^ 1
+                cp(e, A(S, h + 64, h + 128, 1, 32 * a, 32 * a + 32), A(S, h, h + 64, 1, 32 * b, 32 * b + 32))
+        turn(A(n("Lz"), 0, 64), A(tl, 0, 64))
+        gather_tt(A(n("val"), 0, 32), A(n("Lz"), 0, 64), A("gl", 0, 2), A("vj%d" % t, 0, 32), OP.add)
+        act(A(th, 0, 128), A("md", 0, 128), AF.Copy, scale=A(du, 0, 1))
+        act(A(n("nd"), 0, 1), A(du, 0, 1), AF.Copy, scale=-1.0)
+        act(A(rl, 128, 256), A(S, 0, 128), AF.Relu, bias=A(du, 32, 33), scale=-1.0)
+        act(A(rl, 0, 128), A(S, 128, 256), AF.Relu, bias=A(n("nd"), 0, 1))
+        act(A(cj, 128, 256), A(rl, 128, 256), AF.Sign, scale=-1.0, total=A(ca, 1, 2))
+        act(A(cj, 0, 128), A(rl, 0, 128), AF.Sign, total=A(ca, 0, 1))
+        for h in (1, 0):
+            tt(A(cm, 128 * h, 128 * h + 128), A(S, 128 * h, 128 * h + 128), A(th, 128 * h, 128 * h + 128), OP.is_gt)
+        red(A(cb, 1, 2), A(cm, 128, 257), OP.add)
+        red(A(cb, 0, 1), A(cm, 0, 128), OP.add)
+        tt(A(rk, 0, 2), A(ca, 0, 2), A(cb, 0, 2), OP.add)
+        cp("v", A(R, 0, 2), A(rk, 0, 2))
+        scatter(A(n("D"), 0, 256), A(R, 0, 2), A(n("val"), 0, 32))
+        gather("v", A(n("dd"), 0, 128), A(n("D"), 0, 64), A("dl", 0, 8))
+        turn(A(n("tt"), 0, 128), A(n("dd"), 0, 128))
+        xs, ys, xb, of = n("xs"), n("ys"), n("xb"), n("of")
+        tt(A(xs, 0, 4), A(n("tt"), 0, 128, 32), A(n("tt"), 16, 128, 32), OP.add)
+        cp("v", A(xs, 4, 8, 1, 0, 64), A(xs, 0, 4, 1, 64, 128))
+        cp("s", A(xs, 4, 8, 1, 64, 128), A(xs, 0, 4, 1, 0, 64))
+        tt(A(ys, 0, 4), A(xs, 0, 4), A(xs, 4, 8), OP.add)
+        for a, e in ((0, "v"), (2, "s"), (1, "v"), (3, "s")):
+            b = a ^ 1
+            cp(e, A(ys, 4, 8, 1, 32 * a, 32 * a + 32), A(ys, 0, 4, 1, 32 * b, 32 * b + 32))
+        tt(A(xb, 0, 4), A(ys, 0, 4), A(ys, 4, 8), OP.add)
+        cp("v", A(of, 0, 4), A(xb, 0, 4))
+        pick(n("slot"), 0, K, tab, P, A(of, 0, 4))
+        deal(t, True)
+        deal(t, False)
+        cp("v", A(n("jf"), 0, 4), A(of, 0, 4))
+        if own == t:
+            cp("v", A(n("oo"), 0, 1), A(xb, o_, o_ + 1))
+            pick(n("land"), KO * rank, KO * rank + KO, tab, P, A(n("oo"), 0, 1))
+        tt(A(n("fr"), 0, 4), A(xb, 0, 4), A(n("jf"), 0, 4), OP.subtract)
+        if own == t:
+            ts(A(n("lc"), 0, 1), A(n("fr"), o_, o_ + 1), 1.0 / FR, A("oc", 5, 6), OP.mult, OP.add)
+            gather_tt(A(n("zz"), 0, 16), A("tab", 0, 128), A(n("lc"), 0, 1), A("klc", 0, 16), OP.add)
+            tt(A(n("zo"), 0, 8), A(n("zz"), 0, 8), A(n("zz"), 8, 16), OP.add)
+            cp("v", A(n("oi"), 0, 8), A(n("zo"), 0, 8))
+        ts(A(n("cd"), 0, 4), A(n("fr"), 0, 4), 1.0 / FR, None, OP.mult)
+        gather("s", A(n("bk"), 0, 64), A("nat", 0, 256), A(of, 0, 4))
+        gather("s", A(n("wd"), 0, 64), A("wt01", 0, 64), A(n("cd"), 0, 4))
+
+    def lists(t):
+        n = lambda s: s + str(t)
+        gather("s", A(n("lk"), 0, 64), A("lt", 0, 64), A(n("cd"), 0, 4))
+        dma("y", None, A(n("bk"), 0, 64, 1, 0, 1), "st_b%d" % t, 32, out_ap=T.bs[2 * t:2 * t + 1, :])
+        dma("y", None, A(n("lk"), 0, 64, 1, 0, 1), "st_b%d" % t, 32, out_ap=T.bs[2 * t + 1:2 * t + 2, :])
+
+    def rebuild(t):
+        n = lambda s: s + str(t)
+        for s in ("", "s"):
+            landed([A(n("land") + s, KO * r, KO * r + KO) for r in range(N) if r != rank], "col%d" % t + s, 7 * (full // NO))
+        pick2(n("ord"), 64, n("land"), 256, n("oi"), 4)
+        for b in range(4):
+            mm(A("dec", 512 * b, 512 * b + 128), "eq", 128 * b, n("ord"), 0, 128)
+        for b in range(4):
+            scan(A(n("h"), b, 512, 4), A("dpat", 0, 128), A("dec", 512 * b, 512 * b + 128), OP.mult, OP.subtract)
+        quant(n("new"), 0, 128, n("h"), 0)
+        pick(n("W"), P + a0, P + a0 + KO, n("new"), 128, A("cl", 0, 1))
+        spread(A(n("W"), P + a0, P + a0 + KO), "new%d" % t, True)
+        spread(A(n("W") + "s", P + a0, P + a0 + KO), "new%ds" % t)
+
+    def newcols(t):
+        n = lambda s: s + str(t)
+        tt(A(n("wb"), 0, 64), A("nat", P, P + K), A(n("bk"), 0, 64), OP.subtract)
+        tt(A(n("wc"), 0, 64), A(n("wd"), 0, 64), A(n("wb"), 0, 64), OP.mult)
+        tt(A(n("we"), 0, 64), A(n("wc"), 0, 64), A(n("bk"), 0, 64), OP.add)
+
+    def newlist(t):
+        n = lambda s: s + str(t)
+        gather("s", A(n("wg"), 0, 64), A(n("xm"), 0, 256), A(n("of"), 0, 4))
+        tt(A(n("wf"), 0, 64), A(n("we"), 0, 64), A(n("wg"), 0, 64), OP.mult)
+        scatter(A(n("M"), 0, 256), A(n("of"), 0, 4), A(n("wf"), 0, 64))
+        m, mmx, c = n("M"), n("mm"), shift(t)
+        scan(A(mmx, 0, P - c), A("sd", 0, P - c), A(m, c, P), OP.mult, OP.add)
+        if c:
+            scan(A(mmx, P - c, P), A("sd", P - c, P), A(m, 0, c), OP.mult, OP.add, A(mmx, P - c - 1, P - c))
+        cp("v", A(n("ml"), 0, 16), A(mmx, 15, 256, 16))
+
+    def finish(t):
+        n = lambda s: s + str(t)
+        if t == 0:
+            if own == 0:
+                quant("W0", 0, 256, "tbt", 0)
+            act(A("ng", 1, 2), A("fb", 3, 4), AF.Copy, scale=-1.0)
+            lanes(0)
+        if own == t:
+            rebuild(t)
+        newcols(t)
+        if t == 0:
+            tt(A("M0", 0, P), A("xm0", 0, P), A("nat", 0, P), OP.mult)
+            act(A("sd", 0, 256), A("x16", 0, 256), AF.Sign)
+        newlist(t)
+        lists(t)
+        if t == 0 and own:
+            owner()
+            owner_v()
+            owner_t()
+        others = [o for o in range(NO) if 2 * o + t != rank]
+        for s in ("", "s"):
+            landed([A(n("W") + s, P + KO * o, P + KO * o + KO) for o in others], "new%d" % t + s, len(others) * full)
+
+    judge(0, "tA")
+    finish(0)
+    pick2("tB", 128, "W0", P + K, "ml0", 8)
+    checks(1, "tB", lambda h: None, "s")
+    pick("W1", 0, P, "W0", P + K, A("ml0", 0, 16))
+    masks(1)
+    quant("wq", 0, 128, "wt", 0)
+    lanes(1)
+    tt(A("M1", 0, P), A("xm1", 0, P), A("nat", 0, P), OP.mult)
+    judge(1, "tB")
+    finish(1)
+    for h in range(2):
+        mm(A("py", 512 * h, 512 * h + 128), "wq", 0, "W1", 128 * h, 128 * h + 128)
+        cp("s", A("ya", 128 * h, 128 * h + 128), A("py", 512 * h, 512 * h + 128))
+    pick2("F", 128, "W1", P + K, "ml1", 8)
+    mm(A("pc", 0, 128), "wq", 0, "W1", P + K - 128, P + K)
+    cp("v", A("ya", P, P + K), A("pc", 128 - K, 128))
+    for h, e in ((0, "v"), (1, "s")):
+        gather(e, A("yb", 128 * h, 128 * h + 128), A("ya", 0, P + K), A("ml1", 8 * h, 8 * h + 8))
+    for h in range(2):
+        dma("y", None, A("F", 128 * h, 128 * h + 128), "st_c", 32, out_ap=T.oc[:, 512 * h:512 * h + 512],
+            in_ap=T.F[:, 128 * h:128 * h + 128].bitcast(dt.uint8))
+    for k in range(4):
+        dma("y", None, A("Fs", 0, P, 1, 32 * k, 32 * k + 4), "st_s", 64, out_ap=T.osc[4 * k:4 * k + 4, :])
+    dma("y", None, A("yb", 0, 128), "st_y", 32, out_ap=T.y[:, 0:128])
+    dma("s", None, A("yb", 128, 256), "st_y", 32, out_ap=T.y[:, 128:256])
+    for sem, val in final.items():
+        wait("g", sem, val)

@@ -9,6 +9,7 @@ BIG = 1e29
 STEP = 1.0 - 2.0 ** -24
 TINY = 2.0 ** -118
 FR = 2.0 ** -8
+CY, HAND, LOAD = 1.04e-3, 0.16, 1.3
 
 F4 = "float8_e4m3fn_x4"
 SCRATCH = {}
@@ -32,26 +33,31 @@ def _parts(buf, *parts):
     _sb(buf, c)
 
 
-for _n, _w in (("tbt", 4 * P), ("ut", 512), ("wt", 512), ("ee", 528), ("zt", 512)):
+for _n, _w in (("tbt", 4 * P + 4 * N), ("ut", 512), ("wt", 512), ("ee", 528), ("zt", 512)):
     _sb(_n, _w, "bfloat16")
 _parts("con", ("rc", 40), ("hm", 32), ("jc", 1), ("hx", 32), ("hy", 32), ("rf", 40), ("dl0", 8), ("fb", 8), ("st", 2), ("sd32", 32),
        ("sp", 16), ("one", 32), ("frc", 32), ("oc", 8), ("klc", 16), ("ng", 4), ("eq0", 32), ("eq1", 32), ("dm0", 32), ("dm1", 32),
        ("gm0", 16), ("gm1", 16), ("lof", 4), ("vj0", 32), ("vj1", 32), ("pr", 64), ("l16", 64), ("t3", 64), ("t4", 64), ("t5", 64),
-       ("t6", 64), ("t7", 64), ("t8", 64))
+       ("t6", 64), ("t7", 64), ("t8", 64), ("mc", 4), ("jm", 4), ("wa", 8), ("r8", 32))
 for _n, _w in (("nat", 528), ("x16", 272), ("xa0", 256), ("xa1", 256), ("xm0", 256), ("xm1", 256), ("md", 128),
-               ("sd", 256), ("dpat", 128), ("yb", 256), ("ya", P + K), ("lt", 64), ("wt01", 64), ("tab", 128)):
+               ("sd", 256), ("dpat", 128), ("yb", 256), ("ya", P + K), ("lt", 64), ("wt01", 64), ("tab", 128),
+               ("Z", 256), ("Wn", N * P), ("Tn", 256), ("cv", K)):
     _sb(_n, _w)
 _sb("pi", 2, "int32")
 _sb("ib", 8, "int32")
+_sb("iw", 24, "int32")
 _sb("cl", 2, "uint16")
-_sb("lo", 4, "uint16")
+_sb("lo0", 4, "uint16")
+_sb("lo1", 4, "uint16")
 _sb("dl", 8, "uint16")
 _sb("gl", 2, "uint16")
-for _n, _w in (("tA", P), ("tB", P), ("F", P), ("uq", 128), ("wq", 128), ("eq", 512)):
+_sb("ul", 8, "uint16")
+_sb("wo", 4, "uint16")
+for _n, _w in (("tA", P + 128), ("tB", P), ("tR", P), ("F", P), ("uq", 128), ("ua", 128), ("wq", 128), ("eq", 512)):
     _mx(_n, _w)
 for _t in "01":
-    _parts("jd" + _t, ("d1" + _t, 32), ("so" + _t, 32), ("du" + _t, 64), ("lw" + _t, 32), ("px" + _t, 16), ("tl" + _t, 64), ("rk" + _t, 4),
-           ("tt" + _t, 128), ("xs" + _t, 8), ("ys" + _t, 8), ("xb" + _t, 4), ("jf" + _t, 4), ("fr" + _t, 4), ("zz" + _t, 16),
+    _parts("jd" + _t, ("d1" + _t, 32), ("so" + _t, 32), ("du" + _t, 64), ("lw" + _t, 32), ("px" + _t, 16), ("tl" + _t, 64),
+           ("tt" + _t, 128), ("xs" + _t, 32), ("xb" + _t, 32), ("jf" + _t, 4), ("fr" + _t, 4), ("zz" + _t, 16),
            ("zo" + _t, 8), ("nd" + _t, 1), ("wg" + _t, 64), ("wb" + _t, 64), ("wc" + _t, 64), ("wd" + _t, 64), ("we" + _t, 64),
            ("wf" + _t, 64), ("th" + _t, 256), ("cm" + _t, 260), ("ca" + _t, 2), ("cb" + _t, 2), ("ls" + _t, 2), ("rl" + _t, 256),
            ("cj" + _t, 256), ("lj" + _t, 16), ("mm" + _t, 256))
@@ -87,7 +93,7 @@ def rank_program(g, core, T, topo):
             c0, c1 = c0 + c, c1 + c
         ap = T[name][p0:p1, c0:c1] if st == 1 else T[name][p0:p1, c0:c1:st]
         cols = frozenset(c // 512 for c in range(c0, c1, st)) if name in PSUM else frozenset(range(c0, c1, st))
-        return (name, p0, p1, cols, ap)
+        return (name, p0, p1, cols, ap, len(range(c0, c1, st)))
 
     def hits(table, r):
         for (p0, p1, cols, tok) in table.get(r[0], ()):
@@ -115,24 +121,64 @@ def rank_program(g, core, T, topo):
         for r in outs:
             wrote.setdefault(r[0], []).append((r[1], r[2], r[3], tok))
 
-    def op(e, outs, ins, call):
-        order(e, ins, outs)
-        inst = call()
-        count[e] += 1
-        inst.then_inc(T.sem["q" + e], 1)
-        final["q" + e] = count[e]
-        note(ins, outs, ("q" + e, count[e], e))
+    jobs, jw, jr, sent = [], {}, {}, []
 
-    def dma(e, out, in_, sem, total, out_ap=None, in_ap=None):
-        order(e, [in_] if in_ else [], [out] if out else [])
-        o = out_ap if out_ap is not None else out[4]
-        i = in_ap if in_ap is not None else in_[4]
-        eng[e].dma_start(o, i).then_inc(T.sem[sem], 16)
-        final[sem] = total
-        note([in_] if in_ else [], [out] if out else [], (sem, total, "dma"))
+    def job(e, outs, ins, run, cost, lag, after=()):
+        need = set(after)
+        for rs, table in ((ins, jw), (outs, jw), (outs, jr)):
+            for r in rs:
+                need.update(hits(table, r))
+        k = len(jobs)
+        jobs.append((e, run, cost, lag, need))
+        for rs, table in ((ins, jr), (outs, jw)):
+            for r in rs:
+                table.setdefault(r[0], []).append((r[1], r[2], r[3], k))
+        return k
+
+    def op(e, outs, ins, call, cost=None):
+        def run():
+            order(e, ins, outs)
+            inst = call()
+            count[e] += 1
+            inst.then_inc(T.sem["q" + e], 1)
+            final["q" + e] = count[e]
+            note(ins, outs, ("q" + e, count[e], e))
+        job(e, outs, ins, run, max(64, max(r[5] for r in outs[:1] + ins[:1])) * CY if cost is None else cost, HAND)
+
+    def dma(e, out, in_, sem, total, out_ap=None, in_ap=None, behind=None):
+        ins, outs = [in_] if in_ else [], [out] if out else []
+
+        def run():
+            order(e, ins + ([behind] if behind else []), outs)
+            o = out_ap if out_ap is not None else out[4]
+            i = in_ap if in_ap is not None else in_[4]
+            eng[e].dma_start(o, i).then_inc(T.sem[sem], 16)
+            final[sem] = total
+            note(ins, outs, (sem, total, "dma"))
+        job(e, outs, ins + ([behind] if behind else []), run, 0.1, LOAD)
+
+    def emit():
+        tail = [0.0] * len(jobs)
+        for k in range(len(jobs) - 1, -1, -1):
+            tail[k] += jobs[k][2] + jobs[k][3]
+            for d in jobs[k][4]:
+                tail[d] = max(tail[d], tail[k])
+        busy, start = {}, {}
+        for k in sorted(range(len(jobs)), key=lambda k: (-tail[k], k)):
+            e, run, cost, lag, need = jobs[k]
+            t = max([start[d] + jobs[d][2] + jobs[d][3] for d in need], default=0.0)
+            if e:
+                for a, b in sorted(busy.setdefault(e, [])):
+                    if t + cost <= a + 1e-9:
+                        break
+                    t = max(t, b)
+                busy[e].append((t, t + cost))
+            start[k] = t
+        for k in sorted(start, key=lambda k: (start[k], k)):
+            jobs[k][1]()
 
     def tt(out, a, b, o):
-        op("v", [out], [a, b], lambda: g.vector.tensor_tensor(out[4], a[4], b[4], o))
+        op("v", [out], [a, b], lambda: g.vector.tensor_tensor(out[4], a[4], b[4], o), max(64, 2 * out[5]) * CY)
 
     def ts(out, a, s1, s2, o0, o1=None):
         ins = [a] + [s for s in (s1, s2) if isinstance(s, tuple)]
@@ -161,7 +207,7 @@ def rank_program(g, core, T, topo):
             act(out, a, AF.Copy)
 
     def fill(out, x):
-        op("v", [out], [], lambda: g.vector.memset(out[4], x))
+        op("v", [out], [], lambda: g.vector.memset(out[4], x), max(64, out[5] // 2) * CY)
 
     def const(out, x, like):
         act(out, like, AF.Identity, bias=x, scale=0.0)
@@ -178,23 +224,27 @@ def rank_program(g, core, T, topo):
 
     def iota(out, pat, base, cm, flag=True):
         kw = {"allow_small_or_imprecise_dtypes": True} if flag else {}
-        op("g", [out], [], lambda: g.iota(out[4], pat, base, cm, **kw))
+        op("g", [out], [], lambda: g.iota(out[4], pat, base, cm, **kw), 0.16 + 2 * CY * out[5])
+
+    def by(out):
+        return 0.07 + 1.5 * CY * out[5]
 
     def gather(e, out, win, off, f=AF.Copy):
         if e == "v":
-            op("v", [out], [win, off], lambda: g.vector.tensor_copy(out[4], win[4].indirect(off[4])))
+            op("v", [out], [win, off], lambda: g.vector.tensor_copy(out[4], win[4].indirect(off[4])), by(out))
         else:
-            op("s", [out], [win, off], lambda: g.scalar.activation(out[4], win[4].indirect(off[4]), f))
+            op("s", [out], [win, off], lambda: g.scalar.activation(out[4], win[4].indirect(off[4]), f), by(out))
 
     def gather_tt(out, win, off, b, o):
-        op("v", [out], [win, off, b], lambda: g.vector.tensor_tensor(out[4], win[4].indirect(off[4]), b[4], o))
+        op("v", [out], [win, off, b], lambda: g.vector.tensor_tensor(out[4], win[4].indirect(off[4]), b[4], o), by(out))
 
     def scatter(win, off, val):
-        op("v", [win], [val, off], lambda: g.vector.tensor_copy(win[4].indirect(off[4]), val[4]))
+        op("v", [win], [val, off], lambda: g.vector.tensor_copy(win[4].indirect(off[4]), val[4]), 0.06 + 3.5 * CY * val[5])
 
     def pickc(dst, c0, c1, src, n, off):
         o, i = A(dst, c0, c1), A(src, 0, n)
-        op("v", [o], [i, off], lambda: g.vector.tensor_copy(o[4].bitcast(dt.uint32), i[4].bitcast(dt.uint32).indirect(off[4])))
+        op("v", [o], [i, off], lambda: g.vector.tensor_copy(o[4].bitcast(dt.uint32), i[4].bitcast(dt.uint32).indirect(off[4])),
+           by(o))
 
     def picks(e, dst, c0, c1, src, n, off):
         gather(e, A(dst + "s", c0, c1), A(src + "s", 0, n), off)
@@ -211,11 +261,11 @@ def rank_program(g, core, T, topo):
 
     def quant(dst, c0, c1, tile, at):
         o, s, i = A(dst, c0, c1), A(dst + "s", c0, c1), A(tile, at, at + 4 * (c1 - c0))
-        op("v", [o, s], [i], lambda: g.vector.quantize_mx(o[4], s[4], i[4]))
+        op("v", [o, s], [i], lambda: g.vector.quantize_mx(o[4], s[4], i[4]), 0.015 + 0.27 * CY * i[5])
 
     def mm(out, lhs, a, rhs, b0, b1):
         l, ls, r, rs = A(lhs, a, a + 128), A(lhs + "s", a, a + 128), A(rhs, b0, b1), A(rhs + "s", b0, b1)
-        op("t", [out], [l, ls, r, rs], lambda: g.tensor.matmul_mx(out[4], l[4], ls[4], r[4], rs[4], True, True))
+        op("t", [out], [l, ls, r, rs], lambda: g.tensor.matmul_mx(out[4], l[4], ls[4], r[4], rs[4], True, True), 144 * 1.5 * CY)
 
     peers = [c for c in T.cores if c != core]
 
@@ -227,37 +277,44 @@ def rank_program(g, core, T, topo):
         return r[4].bitcast(dt.uint8) if codes else r[4]
 
     def spread(ref, sem, codes=False):
-        order("g", [ref], [])
-        m = topo.mask(core, peers[0])
-        for c in peers:
-            m &= topo.mask(core, c)
-        g.remote_dma_fused([RemoteDMATransfer(dst_ids=[dest(c) for c in peers], dma_engine_mask=m, remote_sem=T.sem[sem],
-                                              srcs=[raw(ref, codes)], dsts=[raw(ref, codes) for _ in peers])],
-                           local_sem=T.sem["out"])
-        final["out"] = final.get("out", 0) + bin(m).count("1")
+        def run():
+            order("g", [ref], [])
+            m = topo.mask(core, peers[0])
+            for c in peers:
+                m &= topo.mask(core, c)
+            g.remote_dma_fused([RemoteDMATransfer(dst_ids=[dest(c) for c in peers], dma_engine_mask=m, remote_sem=T.sem[sem],
+                                                  srcs=[raw(ref, codes)], dsts=[raw(ref, codes) for _ in peers])],
+                               local_sem=T.sem["out"])
+            final["out"] = final.get("out", 0) + bin(m).count("1")
+        sent.append(job("g", [], [ref], run, 0.5, 0.0, sent[-1:]))
 
     full = len(topo.engines(core, peers[0]))
 
-    def landed(refs, sem, total):
-        note([], refs, (sem, total, "remote"))
-        final[sem] = total
+    def landed(refs, sem, total, lag):
+        def run():
+            note([], refs, (sem, total, "remote"))
+            final[sem] = total
+        job(None, refs, [], run, 0.0, lag, sent[-1:])
 
     def deal(t, codes):
-        tr = []
-        for o in range(NO):
-            c = T.cores[2 * o + t]
-            if c == core:
-                continue
-            es = topo.engines(core, c)
-            w = len(es) // NO
-            s = "" if codes else "s"
-            src = A("slot%d" % t + s, KO * o, KO * o + KO)
-            order("g", [src], [])
-            d = A("land%d" % t + s, KO * rank, KO * rank + KO)
-            tr.append(RemoteDMATransfer(dst_ids=[dest(c)], dma_engine_mask=sum(1 << e for e in es[w * o:w * o + w]),
-                                        remote_sem=T.sem["col%d" % t + s], srcs=[raw(src, codes)], dsts=[raw(d, codes)]))
-            final["out"] = final.get("out", 0) + w
-        g.remote_dma_fused(tr, local_sem=T.sem["out"])
+        s = "" if codes else "s"
+
+        def run():
+            tr = []
+            for o in range(NO):
+                c = T.cores[2 * o + t]
+                if c == core:
+                    continue
+                es = topo.engines(core, c)
+                w = len(es) // NO
+                src = A("slot%d" % t + s, KO * o, KO * o + KO)
+                order("g", [src], [])
+                d = A("land%d" % t + s, KO * rank, KO * rank + KO)
+                tr.append(RemoteDMATransfer(dst_ids=[dest(c)], dma_engine_mask=sum(1 << e for e in es[w * o:w * o + w]),
+                                            remote_sem=T.sem["col%d" % t + s], srcs=[raw(src, codes)], dsts=[raw(d, codes)]))
+                final["out"] = final.get("out", 0) + w
+            g.remote_dma_fused(tr, local_sem=T.sem["out"])
+        sent.append(job("g", [], [A("slot%d" % t + s, 0, K)], run, 0.4, 0.0, sent[-1:]))
 
     own = rank % 2
     o_ = rank // 2
@@ -266,8 +323,7 @@ def rank_program(g, core, T, topo):
     dma("y", A("tbt", 0, 512), None, "ld_a", 16, in_ap=T.tb[:, 0:512])
     dma("s", A("ut", 0, 8), None, "ld_u", 16, in_ap=T.u[:, 0:8])
     dma("s", A("tbt", 512, 1024), None, "ld_b", 16, in_ap=T.tb[:, 512:1024])
-    wait("y", "ld_b", 16)
-    dma("y", A("wt", 0, 512), None, "ld_w", 16, in_ap=T.w[:])
+    dma("y", A("wt", 0, 512), None, "ld_w", 16, in_ap=T.w[:], behind=A("tbt", 512, 1024))
 
     iota(A("pi", 0, 2), [[1, 2]], 0, 1, False)
     iota(A("nat", 0, 128), [[1, 128]], 0, 0)
@@ -298,31 +354,45 @@ def rank_program(g, core, T, topo):
     act(A("nat", 512, 528), A("nat", 0, 16), AF.Identity, bias=512.0)
     act(A("ng", 0, 1), A("jc", 0, 1), AF.Identity, bias=4.0, scale=4.0)
 
-    def checks(t, tab, half, e0):
+    def share(t, bank, e):
         for h in range(2):
-            half(h)
-            mm(A("pc", 512 * h, 512 * h + 128), tab, 128 * h, "uq", 0, 128)
-        for h, e in ((0, e0), (1, "v")):
-            cp(e, A("L%d" % t, 4 * rank + 2 * h, 4 * rank + 2 * h + 2), A("pc", 512 * h, 512 * h + 2))
+            cp(e, A("L%d" % t, 4 * rank + 2 * h, 4 * rank + 2 * h + 2), A(bank, 512 * h, 512 * h + 2))
         spread(A("L%d" % t, 4 * rank, 4 * rank + 4), "ck%d" % t)
-        landed([A("L%d" % t, 4 * r, 4 * r + 4) for r in range(N) if r != rank], "ck%d" % t, 7 * full)
+        landed([A("L%d" % t, 4 * r, 4 * r + 4) for r in range(N) if r != rank], "ck%d" % t, 7 * full, 1.2 if t else 2.4)
 
-    checks(0, "tA", lambda h: quant("tA", 128 * h, 128 * h + 128, "tbt", 512 * h), "v")
+    for h in range(2):
+        quant("tA", 128 * h, 128 * h + 128, "tbt", 512 * h)
+        mm(A("pc", 512 * h, 512 * h + 128), "tA", 128 * h, "uq", 0, 128)
+    share(0, "pc", "v")
 
     iota(A("D0", 0, 256), [[0, 256]], 0, 0)
     iota(A("x16", 0, 272), [[0, 17], [1, 16]], 0, 0)
     iota(A("D1", 0, 256), [[0, 256]], 0, 0)
-    ts(A("lo", 0, 1), A("fb", 0, 1), 4.0, None, OP.mult)
-    ts(A("lo", 1, 2), A("fb", 0, 1), 4.0, 2.0, OP.mult, OP.add)
+    iota(A("Z", 0, 256), [[0, 256]], 0, 0)
+    ts(A("lo0", 0, 1), A("fb", 0, 1), 4.0, None, OP.mult)
+    ts(A("lo0", 1, 2), A("fb", 0, 1), 4.0, 2.0, OP.mult, OP.add)
+    if own == 0:
+        if rank:
+            quant("tA", P, P + 128, "tbt", 0)
+        for h in range(2):
+            mm(A("py", 512 * h, 512 * h + 128), "tA", rank + 128 * h, "uq", 0, 128)
+    else:
+        cp("s", A("tbt", 4 * P, 4 * P + 4 * N), A("tbt", 0, 4 * N))
+        quant("tR", 0, P, "tbt", 4 * rank)
+        for h in range(2):
+            mm(A("py", 512 * h, 512 * h + 128), "tR", 128 * h, "uq", 0, 128)
     act(A("lof", 0, 1), A("fb", 4, 5), AF.Identity, bias=1.0, scale=0.25)
     act(A("lof", 1, 2), A("fb", 0, 1), AF.Identity, bias=A("lof", 0, 1), scale=4.0)
     cp("s", A("sd32", 0, 32), A("one", 0, 32))
     const(A("sd32", 0, 32, 16), 0.0, A("nat", 0, 2))
+    cp("s", A("r8", 0, 32), A("one", 0, 32))
+    const(A("r8", 0, 32, 8), 0.0, A("nat", 0, 4))
     const(A("sp", 0, 16), 0.0, A("nat", 0, 16))
     const(A("sp", 0, 16, 8), -BIG, A("nat", 0, 2))
     act(A("rf", 0, 40), A("rc", 0, 40), AF.Copy, scale=8.0 * FR)
     for t in "01":
         const(A("cm" + t, 256, 257), 128.0, A("nat", 0, 1))
+    share(1, "py", "s")
 
     def owner():
         act(A("oc", 0, 1), A("fb", 0, 1), AF.Identity, bias=-16.0, scale=16.0)
@@ -342,7 +412,8 @@ def rank_program(g, core, T, topo):
 
     def owner_v():
         fill(A("zt", 0, 512), 0.0)
-        ts(A("ee", 0, 528), A("nat", 0, 528), A("ng", 0, 1), None, OP.is_equal)
+        for h in range(0, 528, 132):
+            ts(A("ee", h, h + 132), A("nat", h, h + 132), A("ng", 0, 1), None, OP.is_equal)
         quant("land%d" % own, 128, 256, "zt", 0)
         for b in range(4):
             quant("eq", 128 * b, 128 * b + 128, "ee", 4 - b)
@@ -357,14 +428,14 @@ def rank_program(g, core, T, topo):
         act(A("tab", 0, 64), A("t8", 0, 64), AF.Copy, scale=A("oc", 4, 5))
         act(A("tab", 64, 128), A("t8", 0, 64), AF.Copy, scale=A("oc", 3, 4))
 
-    cp("v", A("lo", 2, 3), A("lof", 1, 2))
+    cp("v", A("lo0", 2, 3), A("lof", 1, 2))
     ts(A("gl", 0, 1), A("fb", 2, 3), 0.0, None, OP.add)
     ts(A("gl", 1, 2), A("fb", 2, 3), 32.0, None, OP.add)
     if own == 0:
         owner()
         owner_v()
-    else:
-        quant("W0", 0, 256, "tbt", 0)
+    for h in (0, 128):
+        quant("W0", h, h + 128, "tbt", 4 * h)
     act(A("st", 0, 1), A("fb", 6, 7), AF.Identity, bias=1.0, scale=(STEP - 1.0) / 64)
     act(A("st", 1, 2), A("fb", 7, 8), AF.Identity, bias=1.0, scale=(STEP - 1.0) / 32)
     for s, c in ((1, 0), (2, 1), (3, 0)):
@@ -385,14 +456,15 @@ def rank_program(g, core, T, topo):
         n, c = str(t), -shift(t) % 16
         act(A("xa" + n, 0, 256), A("x16", c, c + 256), AF.Abs, bias=A("ng", 1, 2))
         act(A("xm" + n, 0, 256), A("xa" + n, 0, 256), AF.Relu, bias=1.0, scale=-1.0)
+        for h in range(0, P, 64):
+            tt(A("M" + n, h, h + 64), A("xm" + n, h, h + 64), A("nat", h, h + 64), OP.mult)
 
-    def judge(t, tab):
+    def judge(t, tab, i):
         n = lambda s: s + str(t)
-        L, d1, so, du, S, lw, px, tl = n("L"), n("d1"), n("so"), n("du"), n("S"), n("lw"), n("px"), n("tl")
-        th, cm, cj, rl, ca, cb, ls, rk, R = n("th"), n("cm"), n("cj"), n("rl"), n("ca"), n("cb"), n("ls"), n("rk"), n("R")
-        i = A(L, 0, 32)
-        gather_tt(A(d1, 0, 32), i, A("lo", 0, 2), A(n("dm"), 0, 32), OP.mult)
-        gather("s", A(lw, 0, 16), i, A("lo", 2, 3), AF.Abs)
+        d1, so, du, S, lw, px, tl = n("d1"), n("so"), n("du"), n("S"), n("lw"), n("px"), n("tl")
+        th, cm, cj, rl, ca, cb, ls, R = n("th"), n("cm"), n("cj"), n("rl"), n("ca"), n("cb"), n("ls"), n("R")
+        gather_tt(A(d1, 0, 32), i, A(n("lo"), 0, 2), A(n("dm"), 0, 32), OP.mult)
+        gather("s", A(lw, 0, 16), i, A(n("lo"), 2, 3), AF.Abs)
         scan(A(so, 0, 32), A("sd32", 0, 32), A(d1, 0, 32), OP.mult, OP.subtract)
         for h in range(2):
             act(A(du, 32 * h, 32 * h + 32), A("one", 0, 32), AF.Abs, bias=TINY, scale=A(so, 16 * h + 15, 16 * h + 16))
@@ -425,29 +497,29 @@ def rank_program(g, core, T, topo):
             tt(A(cm, 128 * h, 128 * h + 128), A(S, 128 * h, 128 * h + 128), A(th, 128 * h, 128 * h + 128), OP.is_gt)
         red(A(cb, 1, 2), A(cm, 128, 257), OP.add)
         red(A(cb, 0, 1), A(cm, 0, 128), OP.add)
-        tt(A(rk, 0, 2), A(ca, 0, 2), A(cb, 0, 2), OP.add)
-        cp("v", A(R, 0, 2), A(rk, 0, 2))
+        for h in range(2):
+            ts(A(R, h, h + 1), A(ca, h, h + 1), A(cb, h, h + 1), None, OP.add)
         scatter(A(n("D"), 0, 256), A(R, 0, 2), A(n("val"), 0, 32))
         gather("v", A(n("dd"), 0, 128), A(n("D"), 0, 64), A("dl", 0, 8))
         turn(A(n("tt"), 0, 128), A(n("dd"), 0, 128))
-        xs, ys, xb, of = n("xs"), n("ys"), n("xb"), n("of")
-        tt(A(xs, 0, 4), A(n("tt"), 0, 128, 32), A(n("tt"), 16, 128, 32), OP.add)
-        cp("v", A(xs, 4, 8, 1, 0, 64), A(xs, 0, 4, 1, 64, 128))
-        cp("s", A(xs, 4, 8, 1, 64, 128), A(xs, 0, 4, 1, 0, 64))
-        tt(A(ys, 0, 4), A(xs, 0, 4), A(xs, 4, 8), OP.add)
-        for a, e in ((0, "v"), (2, "s"), (1, "v"), (3, "s")):
-            b = a ^ 1
-            cp(e, A(ys, 4, 8, 1, 32 * a, 32 * a + 32), A(ys, 0, 4, 1, 32 * b, 32 * b + 32))
-        tt(A(xb, 0, 4), A(ys, 0, 4), A(ys, 4, 8), OP.add)
-        cp("v", A(of, 0, 4), A(xb, 0, 4))
+        xs, xb, of = n("xs"), n("xb"), n("of")
+        cp("v", A(xs, 0, 32, 4), A(n("tt"), 0, 128, 16))
+        for a, e in ((0, "s"), (64, "v")):
+            cp(e, A(xs, 2, 32, 4, a, a + 64), A(n("tt"), 0, 128, 16, 64 - a, 128 - a))
+        for x in (1, 3):
+            for a in range(4):
+                b = a ^ x
+                cp("sv"[a & 1], A(xs, x, 32, 4, 32 * a, 32 * a + 32), A(n("tt"), 0, 128, 16, 32 * b, 32 * b + 32))
+        scan(A(xb, 0, 32), A("r8", 0, 32), A(xs, 0, 32), OP.mult, OP.add)
+        cp("v", A(of, 0, 4), A(xb, 7, 32, 8))
         pick(n("slot"), 0, K, tab, P, A(of, 0, 4))
         deal(t, True)
         deal(t, False)
         cp("v", A(n("jf"), 0, 4), A(of, 0, 4))
         if own == t:
-            cp("v", A(n("oo"), 0, 1), A(xb, o_, o_ + 1))
+            cp("v", A(n("oo"), 0, 1), A(xb, 8 * o_ + 7, 8 * o_ + 8))
             pick(n("land"), KO * rank, KO * rank + KO, tab, P, A(n("oo"), 0, 1))
-        tt(A(n("fr"), 0, 4), A(xb, 0, 4), A(n("jf"), 0, 4), OP.subtract)
+        tt(A(n("fr"), 0, 4), A(xb, 7, 32, 8), A(n("jf"), 0, 4), OP.subtract)
         if own == t:
             ts(A(n("lc"), 0, 1), A(n("fr"), o_, o_ + 1), 1.0 / FR, A("oc", 5, 6), OP.mult, OP.add)
             gather_tt(A(n("zz"), 0, 16), A("tab", 0, 128), A(n("lc"), 0, 1), A("klc", 0, 16), OP.add)
@@ -466,7 +538,8 @@ def rank_program(g, core, T, topo):
     def rebuild(t):
         n = lambda s: s + str(t)
         for s in ("", "s"):
-            landed([A(n("land") + s, KO * r, KO * r + KO) for r in range(N) if r != rank], "col%d" % t + s, 7 * (full // NO))
+            landed([A(n("land") + s, KO * r, KO * r + KO) for r in range(N) if r != rank], "col%d" % t + s, 7 * (full // NO),
+                   0.9 if s else 0.6)
         pick2(n("ord"), 64, n("land"), 256, n("oi"), 4)
         for b in range(4):
             mm(A("dec", 512 * b, 512 * b + 128), "eq", 128 * b, n("ord"), 0, 128)
@@ -494,19 +567,49 @@ def rank_program(g, core, T, topo):
             scan(A(mmx, P - c, P), A("sd", P - c, P), A(m, 0, c), OP.mult, OP.add, A(mmx, P - c - 1, P - c))
         cp("v", A(n("ml"), 0, 16), A(mmx, 15, 256, 16))
 
+    def places():
+        act(A("mc", 0, 1), A("fb", 5, 6), AF.Identity, bias=2048.0, scale=-64.0)
+        act(A("mc", 1, 2), A("fb", 6, 7), AF.Identity, bias=A("mc", 0, 1), scale=56.0)
+        act(A("mc", 2, 3), A("fb", 7, 8), AF.Identity, bias=A("mc", 1, 2), scale=56.0)
+        act(A("jm", 0, 4), A("jf0", 0, 4), AF.Identity, bias=A("mc", 2, 3), scale=8.0)
+        ts(A("iw", 0, 4), A("fr0", 0, 4), 32.0 / FR, None, OP.mult)
+        ts(A("iw", 8, 12), A("iw", 0, 4), 2, 56, OP.logical_shift_right, OP.bitwise_and)
+        ts(A("iw", 4, 8), A("iw", 0, 4), 224, None, OP.bitwise_and)
+        tt(A("iw", 12, 16), A("jm", 0, 4), A("iw", 8, 12), OP.subtract)
+        ts(A("iw", 16, 20), A("iw", 12, 16), 3, 31, OP.logical_shift_right, OP.bitwise_and)
+        ts(A("iw", 20, 24), A("iw", 12, 16), 1792, None, OP.bitwise_and)
+        tt(A("wa", 0, 4), A("iw", 4, 8), A("iw", 16, 20), OP.add)
+        tt(A("wa", 4, 8), A("wa", 0, 4), A("iw", 20, 24), OP.add)
+        cp("v", A("wo", 0, 4), A("wa", 4, 8))
+
+    def turned():
+        for c in range(2):
+            cp("s", A("Z", 8 * c, 256, 16), A("L1", c, 32, 2))
+        ts(A("ul", 0, 8), A("one", 0, 8), A("fb", 4, 5), 0.125, OP.mult, OP.mult)
+        turn(A("Wn", 0, 256), A("Z", 0, 256))
+        pick("ua", 0, 128, "uq", 128, A("ul", 0, 8))
+        ts(A("lo1", 0, 3), A("lo0", 0, 3), 8.0, None, OP.mult)
+        masks(1)
+
+    def table(dst):
+        for h in range(4):
+            pick(dst, 64 * h, 64 * h + 64, "W0", P + K, A("ml0", 4 * h, 4 * h + 4))
+
     def finish(t):
         n = lambda s: s + str(t)
         if t == 0:
-            if own == 0:
-                quant("W0", 0, 256, "tbt", 0)
+            places()
             act(A("ng", 1, 2), A("fb", 3, 4), AF.Copy, scale=-1.0)
-            lanes(0)
+            act(A("sd", 0, 256), A("x16", 0, 256), AF.Sign)
+        else:
+            table("W1")
+            quant("wq", 0, 128, "wt", 0)
+        lanes(t)
         if own == t:
             rebuild(t)
-        newcols(t)
         if t == 0:
-            tt(A("M0", 0, P), A("xm0", 0, P), A("nat", 0, P), OP.mult)
-            act(A("sd", 0, 256), A("x16", 0, 256), AF.Sign)
+            turned()
+        newcols(t)
         newlist(t)
         lists(t)
         if t == 0 and own:
@@ -515,18 +618,17 @@ def rank_program(g, core, T, topo):
             owner_t()
         others = [o for o in range(NO) if 2 * o + t != rank]
         for s in ("", "s"):
-            landed([A(n("W") + s, P + KO * o, P + KO * o + KO) for o in others], "new%d" % t + s, len(others) * full)
+            landed([A(n("W") + s, P + KO * o, P + KO * o + KO) for o in others], "new%d" % t + s, len(others) * full,
+                   (1.2 if s else 0.7) + (0.0 if own == t else 4.5))
 
-    judge(0, "tA")
+    judge(0, "tA", A("L0", 0, 32))
     finish(0)
-    pick2("tB", 128, "W0", P + K, "ml0", 8)
-    checks(1, "tB", lambda h: None, "s")
-    pick("W1", 0, P, "W0", P + K, A("ml0", 0, 16))
-    masks(1)
-    quant("wq", 0, 128, "wt", 0)
-    lanes(1)
-    tt(A("M1", 0, P), A("xm1", 0, P), A("nat", 0, P), OP.mult)
-    judge(1, "tB")
+    table("tB")
+    mm(A("pc", 0, 128), "ua", 0, "W0", P + K - 128, P + K)
+    cp("v", A("cv", 0, K), A("pc", 128 - K, 128))
+    scatter(A("Wn", 0, N * P), A("wo", 0, 4), A("cv", 0, K))
+    turn(A("Tn", 0, 256), A("Wn", 0, 256))
+    judge(1, "tB", A("Tn", 0, 256))
     finish(1)
     for h in range(2):
         mm(A("py", 512 * h, 512 * h + 128), "wq", 0, "W1", 128 * h, 128 * h + 128)
@@ -543,5 +645,6 @@ def rank_program(g, core, T, topo):
         dma("y", None, A("Fs", 0, P, 1, 32 * k, 32 * k + 4), "st_s", 64, out_ap=T.osc[4 * k:4 * k + 4, :])
     dma("y", None, A("yb", 0, 128), "st_y", 32, out_ap=T.y[:, 0:128])
     dma("s", None, A("yb", 128, 256), "st_y", 32, out_ap=T.y[:, 128:256])
+    emit()
     for sem, val in final.items():
         wait("g", sem, val)

@@ -8,8 +8,11 @@ N, P, K, NO, KO = 8, 256, 64, 4, 16
 BIG = 1e29
 STEP = 1.0 - 2.0 ** -24
 TINY = 2.0 ** -118
-FR = 2.0 ** -8
+FR = 2.0 ** -7
+FZ = 2.0 ** -15
+HALF = 127.5 / 256
 CY, HAND, LOAD = 1.04e-3, 0.16, 1.3
+NB = 32 * (N + 1)
 
 F4 = "float8_e4m3fn_x4"
 SCRATCH = {}
@@ -35,38 +38,35 @@ def _parts(buf, *parts):
 
 for _n, _w in (("tbt", 4 * P + 4 * N), ("ut", 512), ("wt", 512), ("ee", 528), ("zt", 512)):
     _sb(_n, _w, "bfloat16")
-_parts("con", ("rc", 40), ("hm", 32), ("jc", 1), ("hx", 32), ("hy", 32), ("rf", 40), ("dl0", 8), ("fb", 8), ("st", 2), ("sd32", 32),
-       ("sp", 16), ("one", 32), ("frc", 32), ("oc", 8), ("klc", 16), ("ng", 4), ("eq0", 32), ("eq1", 32), ("dm0", 32), ("dm1", 32),
+_parts("con", ("rc", 40), ("hm", 32), ("jc", 1), ("hx", 32), ("hy", 32), ("rf", 40), ("fb", 8), ("sd32", 32),
+       ("sp", 16), ("one", 32), ("frc", 32), ("oc", 8), ("klc", 16), ("ng", 4), ("eq0", 32), ("dm0", 32),
        ("gm0", 16), ("gm1", 16), ("lof", 4), ("vj0", 32), ("vj1", 32), ("pr", 64), ("l16", 64), ("t3", 64), ("t4", 64), ("t5", 64),
-       ("t6", 64), ("t7", 64), ("t8", 64), ("mc", 4), ("jm", 4), ("wa", 8), ("r8", 32))
-for _n, _w in (("nat", 528), ("x16", 272), ("xa0", 256), ("xa1", 256), ("xm0", 256), ("xm1", 256), ("md", 128),
-               ("sd", 256), ("dpat", 128), ("yb", 256), ("ya", P + K), ("lt", 64), ("wt01", 64), ("tab", 128),
-               ("Z", 256), ("Wn", N * P), ("Tn", 256), ("cv", K)):
+       ("t6", 64), ("t7", 64), ("t8", 64), ("mc", 4), ("jm", 8), ("wa", 24), ("r8", 40), ("r2", 16), ("e1", 16), ("n1", 16),
+       ("pz", 16), ("pj", 16), ("sr", 32), ("sq", 32), ("vz", 32), ("hz", 32))
+for _n, _w in (("nat", 528), ("x16", 288), ("xa", 272), ("xm", 272), ("md", 68), ("Mu", 272), ("M", 272), ("mm", P),
+               ("sd", 256), ("dpat", 128), ("yb", 256), ("ya", P + 2 * K), ("lt", 64), ("wt01", 64), ("tab", 128),
+               ("Z", NB), ("Wn", 4096), ("Tn", NB), ("cv", K)):
     _sb(_n, _w)
 _sb("pi", 2, "int32")
 _sb("ib", 8, "int32")
-_sb("iw", 24, "int32")
-_sb("cl", 2, "uint16")
-_sb("lo0", 4, "uint16")
-_sb("lo1", 4, "uint16")
-_sb("dl", 8, "uint16")
-_sb("gl", 2, "uint16")
-_sb("ul", 8, "uint16")
-_sb("wo", 4, "uint16")
-for _n, _w in (("tA", P + 128), ("tB", P), ("tR", P), ("F", P), ("uq", 128), ("ua", 128), ("wq", 128), ("eq", 512)):
+_sb("iw", 28, "int32")
+_sb("iz", 8, "int32")
+for _n, _w in (("cl", 2), ("lo0", 4), ("sl", 2), ("zl", 2), ("gl", 2), ("ul", 8), ("wo", 4), ("oz", 4), ("os0", 4), ("ml", 16)):
+    _sb(_n, _w, "uint16")
+for _n, _w in (("tR", P), ("F", P), ("uq", 128), ("ua", 128), ("wq", 128), ("eq", 512), ("W", P + 2 * K)):
     _mx(_n, _w)
 for _t in "01":
     _parts("jd" + _t, ("d1" + _t, 32), ("so" + _t, 32), ("du" + _t, 64), ("lw" + _t, 32), ("px" + _t, 16), ("tl" + _t, 64),
-           ("tt" + _t, 128), ("xs" + _t, 32), ("xb" + _t, 32), ("jf" + _t, 4), ("fr" + _t, 4), ("zz" + _t, 16),
-           ("zo" + _t, 8), ("nd" + _t, 1), ("wg" + _t, 64), ("wb" + _t, 64), ("wc" + _t, 64), ("wd" + _t, 64), ("we" + _t, 64),
-           ("wf" + _t, 64), ("th" + _t, 256), ("cm" + _t, 260), ("ca" + _t, 2), ("cb" + _t, 2), ("ls" + _t, 2), ("rl" + _t, 256),
-           ("cj" + _t, 256), ("lj" + _t, 16), ("mm" + _t, 256))
-    for _n, _w in (("L", 32), ("S", 256), ("Lz", 64), ("val", 32), ("D", 256), ("dd", 128), ("bk", 64), ("lk", 64), ("M", 256)):
+           ("tt" + _t, 160), ("jf" + _t, 4), ("fr" + _t, 4), ("zz" + _t, 16), ("lf" + _t, 16),
+           ("zo" + _t, 8), ("wg" + _t, 64), ("wb" + _t, 64), ("wc" + _t, 64), ("wd" + _t, 64), ("we" + _t, 64),
+           ("wf" + _t, 64), ("th" + _t, 136), ("cm" + _t, 256), ("cs" + _t, 128), ("ca" + _t, 2), ("ls" + _t, 2), ("rl" + _t, 256),
+           ("cj" + _t, 256), ("lj" + _t, 16), ("bi" + _t, 64))
+    for _n, _w in (("L", 32), ("S", 256), ("Lz", 64), ("val", 32), ("D", 272), ("xb", 40), ("bk", 64), ("lk", 64)):
         _sb(_n + _t, _w)
-    for _n, _w in (("R", 2), ("of", 4), ("cd", 4), ("oo", 2), ("lc", 2), ("ml", 16), ("oi", 8)):
+    for _n, _w in (("R", 2), ("of", 16), ("cd", 4), ("lc", 2), ("oi", 8)):
         _sb(_n + _t, _w, "uint16")
     _sb("h" + _t, 512, "bfloat16")
-    for _n, _w in (("slot", K), ("land", 256), ("ord", 128), ("new", 128), ("W", P + K)):
+    for _n, _w in (("slot", K), ("land", 256), ("ord", 128), ("new", 128)):
         _mx(_n + _t, _w)
 SCRATCH["pc"] = ("psum", [128, 1024], "float32")
 SCRATCH["dec"] = ("psum", [128, 2048], "float32")
@@ -121,10 +121,10 @@ def rank_program(g, core, T, topo):
         for r in outs:
             wrote.setdefault(r[0], []).append((r[1], r[2], r[3], tok))
 
-    jobs, jw, jr, sent = [], {}, {}, []
+    jobs, jw, jr, sent, gate = [], {}, {}, [], []
 
     def job(e, outs, ins, run, cost, lag, after=()):
-        need = set(after)
+        need = set(after) | set(gate)
         for rs, table in ((ins, jw), (outs, jw), (outs, jr)):
             for r in rs:
                 need.update(hits(table, r))
@@ -212,12 +212,10 @@ def rank_program(g, core, T, topo):
     def const(out, x, like):
         act(out, like, AF.Identity, bias=x, scale=0.0)
 
-    def red(out, a, o):
-        op("v", [out], [a], lambda: g.vector.tensor_reduce(out[4], a[4], X, o))
-
-    def scan(out, d0, d1, o0, o1, first=None):
-        op("v", [out], [d0, d1] + ([first] if first else []),
-           lambda: g.vector.tensor_tensor_scan(out[4], d0[4], d1[4], first[4] if first else 0.0, o0, o1))
+    def scan(out, d0, d1, o0, o1, first=0.0):
+        col = isinstance(first, tuple)
+        op("v", [out], [d0, d1] + ([first] if col else []),
+           lambda: g.vector.tensor_tensor_scan(out[4], d0[4], d1[4], first[4] if col else first, o0, o1))
 
     def turn(out, a):
         op("v", [out], [a], lambda: g.vector.transpose(out[4], a[4]))
@@ -266,6 +264,15 @@ def rank_program(g, core, T, topo):
     def mm(out, lhs, a, rhs, b0, b1):
         l, ls, r, rs = A(lhs, a, a + 128), A(lhs + "s", a, a + 128), A(rhs, b0, b1), A(rhs + "s", b0, b1)
         op("t", [out], [l, ls, r, rs], lambda: g.tensor.matmul_mx(out[4], l[4], ls[4], r[4], rs[4], True, True), 144 * 1.5 * CY)
+
+    def around(buf, src, step, end, places):
+        k = 0
+        for x, c in places:
+            for a in ((0, 2) if x == 2 else range(4)):
+                w = 64 if x == 2 else 32
+                b = a ^ x
+                cp("sv"[k & 1], A(buf, c, end, step, 32 * a, 32 * a + w), A(buf, src, end, step, 32 * b, 32 * b + w))
+                k += 1
 
     peers = [c for c in T.cores if c != core]
 
@@ -333,7 +340,6 @@ def rank_program(g, core, T, topo):
     iota(A("lt", 0, 64), [[0, 8], [1, 8]], 0, 0)
     iota(A("pr", 0, 64), [[16, 8], [0, 8]], 0, 0)
     iota(A("hx", 0, 32), [[128, 2], [1, 16]], 0, 0)
-    iota(A("dl0", 0, 8), [[16, 4], [0, 2]], 0, 0)
     fill(A("ut", 8, 512), 0.0)
     fill(A("one", 0, 32), 1.0)
     fill(A("frc", 0, 32), FR)
@@ -341,13 +347,9 @@ def rank_program(g, core, T, topo):
         ts(A("ib", col, col + 1), A("pi", src, src + 1), bits, None, OP.bitwise_and)
     cp("v", A("fb", 0, 8), A("ib", 0, 8))
 
-    def masks(t):
-        n = str(t)
-        ts(A("eq" + n, 0, 32), A("rc", 0, 32), A("fb", t, t + 1), -1.0, OP.is_equal, OP.mult)
-        ts(A("gm" + n, 0, 16), A("rc", 0, 16), A("fb", t, t + 1), BIG, OP.is_equal, OP.mult)
-        tt(A("dm" + n, 0, 32), A("eq" + n, 0, 32), A("hm", 0, 32), OP.add)
-
-    masks(0)
+    ts(A("eq0", 0, 32), A("rc", 0, 32), A("fb", 0, 1), -1.0, OP.is_equal, OP.mult)
+    ts(A("gm0", 0, 16), A("rc", 0, 16), A("fb", 0, 1), BIG, OP.is_equal, OP.mult)
+    tt(A("dm0", 0, 32), A("eq0", 0, 32), A("hm", 0, 32), OP.add)
     quant("uq", 0, 128, "ut", 0)
     act(A("nat", 128, 256), A("nat", 0, 128), AF.Identity, bias=128.0)
     act(A("nat", 256, 512), A("nat", 0, 256), AF.Identity, bias=256.0)
@@ -361,37 +363,38 @@ def rank_program(g, core, T, topo):
         landed([A("L%d" % t, 4 * r, 4 * r + 4) for r in range(N) if r != rank], "ck%d" % t, 7 * full, 1.2 if t else 2.4)
 
     for h in range(2):
-        quant("tA", 128 * h, 128 * h + 128, "tbt", 512 * h)
-        mm(A("pc", 512 * h, 512 * h + 128), "tA", 128 * h, "uq", 0, 128)
+        quant("W", 128 * h, 128 * h + 128, "tbt", 512 * h)
+        mm(A("pc", 512 * h, 512 * h + 128), "W", 128 * h, "uq", 0, 128)
     share(0, "pc", "v")
 
-    iota(A("D0", 0, 256), [[0, 256]], 0, 0)
-    iota(A("x16", 0, 272), [[0, 17], [1, 16]], 0, 0)
-    iota(A("D1", 0, 256), [[0, 256]], 0, 0)
-    iota(A("Z", 0, 256), [[0, 256]], 0, 0)
+    iota(A("D0", 0, 272), [[0, 272]], 0, 0)
+    iota(A("x16", 0, 288), [[0, 18], [1, 16]], 0, 0)
+    iota(A("D1", 0, 272), [[0, 272]], 0, 0)
+    iota(A("Z", 0, NB), [[0, NB]], 0, 0)
+    iota(A("r2", 0, 16), [[1, 8], [0, 2]], 0, 0)
+    iota(A("sr", 0, 16), [[0, 4], [8, 2], [24, 2]], 7, 0)
+    iota(A("sr", 16, 32), [[0, 4], [8, 2], [-16, 2]], 23, 0)
+    const(A("sr", 4, 5), 7.0 + 8 * (o_ >> 1) + 24 * (o_ & 1), A("one", 0, 1))
+    const(A("sr", 20, 21), 23.0 + 8 * (o_ >> 1) - 16 * (o_ & 1), A("one", 0, 1))
+    turn(A("sq", 0, 32), A("sr", 0, 32))
+    cp("v", A("sl", 0, 2), A("sq", 0, 2))
     ts(A("lo0", 0, 1), A("fb", 0, 1), 4.0, None, OP.mult)
     ts(A("lo0", 1, 2), A("fb", 0, 1), 4.0, 2.0, OP.mult, OP.add)
-    if own == 0:
-        if rank:
-            quant("tA", P, P + 128, "tbt", 0)
-        for h in range(2):
-            mm(A("py", 512 * h, 512 * h + 128), "tA", rank + 128 * h, "uq", 0, 128)
-    else:
+    if rank:
         cp("s", A("tbt", 4 * P, 4 * P + 4 * N), A("tbt", 0, 4 * N))
-        quant("tR", 0, P, "tbt", 4 * rank)
         for h in range(2):
-            mm(A("py", 512 * h, 512 * h + 128), "tR", 128 * h, "uq", 0, 128)
+            quant("tR", 128 * h, 128 * h + 128, "tbt", 4 * rank + 512 * h)
+    for h in range(2):
+        mm(A("py", 512 * h, 512 * h + 128), "tR" if rank else "W", 128 * h, "uq", 0, 128)
     act(A("lof", 0, 1), A("fb", 4, 5), AF.Identity, bias=1.0, scale=0.25)
     act(A("lof", 1, 2), A("fb", 0, 1), AF.Identity, bias=A("lof", 0, 1), scale=4.0)
     cp("s", A("sd32", 0, 32), A("one", 0, 32))
     const(A("sd32", 0, 32, 16), 0.0, A("nat", 0, 2))
-    cp("s", A("r8", 0, 32), A("one", 0, 32))
-    const(A("r8", 0, 32, 8), 0.0, A("nat", 0, 4))
+    const(A("r8", 0, 40), 1.0, A("nat", 0, 40))
+    const(A("r8", 0, 40, 8), 0.0, A("nat", 0, 5))
     const(A("sp", 0, 16), 0.0, A("nat", 0, 16))
     const(A("sp", 0, 16, 8), -BIG, A("nat", 0, 2))
     act(A("rf", 0, 40), A("rc", 0, 40), AF.Copy, scale=8.0 * FR)
-    for t in "01":
-        const(A("cm" + t, 256, 257), 128.0, A("nat", 0, 1))
     share(1, "py", "s")
 
     def owner():
@@ -400,7 +403,7 @@ def rank_program(g, core, T, topo):
         act(A("oc", 2, 3), A("fb", 0, 1), AF.Relu, bias=1.0, scale=-1.0)
         act(A("oc", 3, 4), A("fb", 4, 5), AF.Copy, scale=0.125)
         act(A("oc", 4, 5), A("fb", 4, 5), AF.Identity, bias=1.0, scale=-0.125)
-        act(A("oc", 5, 6), A("fb", 4, 5), AF.Copy, scale=8.0)
+        act(A("oc", 5, 6), A("fb", 4, 5), AF.Identity, bias=-HALF, scale=8.0)
         act(A("oc", 6, 7), A("fb", 4, 5), AF.Identity, bias=7.0)
         act(A("klc", 0, 8), A("nat", 0, 8), AF.Copy, scale=A("oc", 4, 5))
         act(A("klc", 8, 16), A("nat", 8, 16), AF.Copy, scale=A("oc", 3, 4))
@@ -434,99 +437,85 @@ def rank_program(g, core, T, topo):
     if own == 0:
         owner()
         owner_v()
-    for h in (0, 128):
-        quant("W0", h, h + 128, "tbt", 4 * h)
-    act(A("st", 0, 1), A("fb", 6, 7), AF.Identity, bias=1.0, scale=(STEP - 1.0) / 64)
-    act(A("st", 1, 2), A("fb", 7, 8), AF.Identity, bias=1.0, scale=(STEP - 1.0) / 32)
-    for s, c in ((1, 0), (2, 1), (3, 0)):
-        act(A("md", 32 * s, 32 * s + 32), A("one", 0, 32), AF.Copy, scale=A("st", c, c + 1))
-    ts(A("md", 0, 32), A("nat", 0, 32), A("fb", 2, 3), STEP, OP.is_ge, OP.max)
-    ts(A("dl", 0, 8), A("dl0", 0, 8), A("fb", 3, 4), None, OP.add)
+    ts(A("md", 0, 64, 2), A("nat", 0, 32), A("fb", 2, 3), STEP, OP.is_ge, OP.max)
+    act(A("md", 65, 66), A("fb", 7, 8), AF.Identity, bias=1.0, scale=(STEP - 1.0) / 32)
+    act(A("md", 64, 65), A("fb", 6, 7), AF.Identity, bias=1.0, scale=(STEP - 1.0) / 64)
+    act(A("md", 1, 64, 2), A("one", 0, 32), AF.Copy, scale=A("md", 65, 66))
     ts(A("hy", 0, 32), A("hx", 0, 32), A("fb", 5, 6), None, OP.add)
-    for t in range(2):
-        tt(A("vj%d" % t, 0, 32), A("hy", 0, 32), A("rf", t, t + 32), OP.add)
+    tt(A("vj0", 0, 32), A("hy", 0, 32), A("rf", 0, 32), OP.add)
     if own == 0:
         owner_t()
     ts(A("wt01", 0, 64), A("lt", 0, 64), float(rank), None, OP.is_equal)
 
-    def shift(t):
-        return rank if t == 0 else -rank % P
-
-    def lanes(t):
-        n, c = str(t), -shift(t) % 16
-        act(A("xa" + n, 0, 256), A("x16", c, c + 256), AF.Abs, bias=A("ng", 1, 2))
-        act(A("xm" + n, 0, 256), A("xa" + n, 0, 256), AF.Relu, bias=1.0, scale=-1.0)
-        for h in range(0, P, 64):
-            tt(A("M" + n, h, h + 64), A("xm" + n, h, h + 64), A("nat", h, h + 64), OP.mult)
-
-    def judge(t, tab, i):
+    def judge(t, i):
         n = lambda s: s + str(t)
         d1, so, du, S, lw, px, tl = n("d1"), n("so"), n("du"), n("S"), n("lw"), n("px"), n("tl")
-        th, cm, cj, rl, ca, cb, ls, R = n("th"), n("cm"), n("cj"), n("rl"), n("ca"), n("cb"), n("ls"), n("R")
-        gather_tt(A(d1, 0, 32), i, A(n("lo"), 0, 2), A(n("dm"), 0, 32), OP.mult)
-        gather("s", A(lw, 0, 16), i, A(n("lo"), 2, 3), AF.Abs)
-        scan(A(so, 0, 32), A("sd32", 0, 32), A(d1, 0, 32), OP.mult, OP.subtract)
+        th, cm, cs, cj, rl, ca, ls, R = n("th"), n("cm"), n("cs"), n("cj"), n("rl"), n("ca"), n("ls"), n("R")
+        if t == 0:
+            gather_tt(A(d1, 0, 32), A(i, 0, 32), A("lo0", 0, 2), A("dm0", 0, 32), OP.mult)
+            gather("s", A(lw, 0, 16), A(i, 0, 32), A("lo0", 2, 3), AF.Abs)
+            scan(A(so, 0, 32), A("sd32", 0, 32), A(d1, 0, 32), OP.mult, OP.subtract)
+        else:
+            for h in range(2):
+                scan(A(so, 16 * h + 8, 16 * h + 16), A("one", 0, 8), A(i, 32 + 16 * h, NB, 32), OP.mult, OP.subtract,
+                     A(i, 16 * h, 16 * h + 1))
+                act(A(lw, 8 * h, 8 * h + 8), A(i, 40 + 16 * h, NB, 32), AF.Abs)
         for h in range(2):
             act(A(du, 32 * h, 32 * h + 32), A("one", 0, 32), AF.Abs, bias=TINY, scale=A(so, 16 * h + 15, 16 * h + 16))
         tt(A(lw, 16, 32), A(lw, 0, 16), A(n("gm"), 0, 16), OP.subtract)
         scan(A(px, 0, 16), A("sp", 0, 16), A(lw, 16, 32), OP.add, OP.max)
+        turn(A(S, 0, 256, 4), A(du, 0, 64))
         for h in range(2):
-            turn(A(S, 128 * h, 128 * h + 32), A(du, 32 * h, 32 * h + 32))
+            act(A(th, 68 * h, 68 * h + 65), A("md", 0, 65), AF.Copy, scale=A(du, 32 * h, 32 * h + 1))
+        around(S, 0, 4, 256, ((1, 2), (2, 1), (3, 3)))
         for h in range(2):
             act(A(n("lj"), 8 * h, 8 * h + 8), A(px, 8 * h, 8 * h + 8), AF.Sign, bias=A(px, 8 * h + 7, 8 * h + 8), scale=-1.0,
                 total=A(ls, h, h + 1))
         for h in range(2):
-            act(A(tl, 32 * h, 32 * h + 32), A("frc", 0, 32), AF.Copy, scale=A(ls, h, h + 1))
-        for h in (0, 128):
-            cp("v", A(S, h + 32, h + 64, 1, 0, 64), A(S, h, h + 32, 1, 64, 128))
-            cp("s", A(S, h + 32, h + 64, 1, 64, 128), A(S, h, h + 32, 1, 0, 64))
-        ts(A(th, 128, 256), A("md", 0, 128), A(du, 32, 33), None, OP.mult)
-        for h in (0, 128):
-            for a, e in ((0, "v"), (2, "s"), (1, "v"), (3, "s")):
-                b = a ^ 1
-                cp(e, A(S, h + 64, h + 128, 1, 32 * a, 32 * a + 32), A(S, h, h + 64, 1, 32 * b, 32 * b + 32))
+            ts(A(tl, 32 * h, 32 * h + 32), A("frc", 0, 32), A(ls, h, h + 1), None, OP.mult)
         turn(A(n("Lz"), 0, 64), A(tl, 0, 64))
         gather_tt(A(n("val"), 0, 32), A(n("Lz"), 0, 64), A("gl", 0, 2), A("vj%d" % t, 0, 32), OP.add)
-        act(A(th, 0, 128), A("md", 0, 128), AF.Copy, scale=A(du, 0, 1))
-        act(A(n("nd"), 0, 1), A(du, 0, 1), AF.Copy, scale=-1.0)
-        act(A(rl, 128, 256), A(S, 0, 128), AF.Relu, bias=A(du, 32, 33), scale=-1.0)
-        act(A(rl, 0, 128), A(S, 128, 256), AF.Relu, bias=A(n("nd"), 0, 1))
-        act(A(cj, 128, 256), A(rl, 128, 256), AF.Sign, scale=-1.0, total=A(ca, 1, 2))
-        act(A(cj, 0, 128), A(rl, 0, 128), AF.Sign, total=A(ca, 0, 1))
-        for h in (1, 0):
-            tt(A(cm, 128 * h, 128 * h + 128), A(S, 128 * h, 128 * h + 128), A(th, 128 * h, 128 * h + 128), OP.is_gt)
-        red(A(cb, 1, 2), A(cm, 128, 257), OP.add)
-        red(A(cb, 0, 1), A(cm, 0, 128), OP.add)
         for h in range(2):
-            ts(A(R, h, h + 1), A(ca, h, h + 1), A(cb, h, h + 1), None, OP.add)
-        scatter(A(n("D"), 0, 256), A(R, 0, 2), A(n("val"), 0, 32))
-        gather("v", A(n("dd"), 0, 128), A(n("D"), 0, 64), A("dl", 0, 8))
-        turn(A(n("tt"), 0, 128), A(n("dd"), 0, 128))
-        xs, xb, of = n("xs"), n("xb"), n("of")
-        cp("v", A(xs, 0, 32, 4), A(n("tt"), 0, 128, 16))
-        for a, e in ((0, "s"), (64, "v")):
-            cp(e, A(xs, 2, 32, 4, a, a + 64), A(n("tt"), 0, 128, 16, 64 - a, 128 - a))
-        for x in (1, 3):
-            for a in range(4):
-                b = a ^ x
-                cp("sv"[a & 1], A(xs, x, 32, 4, 32 * a, 32 * a + 32), A(n("tt"), 0, 128, 16, 32 * b, 32 * b + 32))
-        scan(A(xb, 0, 32), A("r8", 0, 32), A(xs, 0, 32), OP.mult, OP.add)
-        cp("v", A(of, 0, 4), A(xb, 7, 32, 8))
-        pick(n("slot"), 0, K, tab, P, A(of, 0, 4))
+            act(A(rl, 128 * h, 128 * h + 128), A(S, 128 - 128 * h, 256 - 128 * h), AF.Sign, bias=A(du, 32 * h, 32 * h + 1), scale=-1.0)
+        for h in range(2):
+            act(A(cj, 128 * h, 128 * h + 128), A(rl, 128 * h, 128 * h + 128), AF.Relu, scale=2.0 * h - 1.0, total=A(ca, h, h + 1))
+        for h in range(2):
+            c = 128 * h
+            tt(A(cm, c, c + 64), A(S, c, c + 128, 2), A(th, 68 * h, 68 * h + 64), OP.is_gt)
+            ts(A(cm, c + 64, c + 128), A(S, c + 1, c + 128, 2), A(th, 68 * h + 64, 68 * h + 65), None, OP.is_gt)
+            scan(A(cs, 64 * h, 64 * h + 64), A(cm, c, c + 64), A(cm, c + 64, c + 128), OP.add, OP.add, float(c))
+        for h, o in ((0, OP.add), (1, OP.subtract)):
+            ts(A(R, h, h + 1), A(cs, 64 * h + 63, 64 * h + 64), A(ca, h, h + 1), None, o)
+        scatter(A(n("D"), 16, 272), A(R, 0, 2), A(n("val"), 0, 32))
+        tr, xb, of, lf = n("tt"), n("xb"), n("of"), n("lf")
+        turn(A(tr, 64, 160), A(n("D"), 0, 96))
+        turn(A(tr, 0, 64), A(n("D"), 16, 80))
+        around(tr, 0, 16, 160, ((1, 4), (2, 8), (3, 12)))
+        scan(A(xb, 0, 40), A("r8", 0, 40), A(tr, 0, 160, 4), OP.mult, OP.add)
+        gather("v", A(of, 0, 16), A(xb, 0, 40), A("sl", 0, 1))
+        gather("s", A(lf, 0, 16), A(xb, 0, 40), A("sl", 0, 1))
+        pick(n("slot"), 0, K, "W", P + K * t, A(of, 0, 4))
         deal(t, True)
         deal(t, False)
         cp("v", A(n("jf"), 0, 4), A(of, 0, 4))
         if own == t:
-            cp("v", A(n("oo"), 0, 1), A(xb, 8 * o_ + 7, 8 * o_ + 8))
-            pick(n("land"), KO * rank, KO * rank + KO, tab, P, A(n("oo"), 0, 1))
-        tt(A(n("fr"), 0, 4), A(xb, 7, 32, 8), A(n("jf"), 0, 4), OP.subtract)
+            pick(n("land"), KO * rank, KO * rank + KO, "W", P + K * t, A(of, 4, 5))
+        tt(A(n("fr"), 0, 4), A(lf, 0, 4), A(n("jf"), 0, 4), OP.subtract)
         if own == t:
             ts(A(n("lc"), 0, 1), A(n("fr"), o_, o_ + 1), 1.0 / FR, A("oc", 5, 6), OP.mult, OP.add)
             gather_tt(A(n("zz"), 0, 16), A("tab", 0, 128), A(n("lc"), 0, 1), A("klc", 0, 16), OP.add)
             tt(A(n("zo"), 0, 8), A(n("zz"), 0, 8), A(n("zz"), 8, 16), OP.add)
             cp("v", A(n("oi"), 0, 8), A(n("zo"), 0, 8))
-        ts(A(n("cd"), 0, 4), A(n("fr"), 0, 4), 1.0 / FR, None, OP.mult)
-        gather("s", A(n("bk"), 0, 64), A("nat", 0, 256), A(of, 0, 4))
+        ts(A(n("cd"), 0, 4), A(n("fr"), 0, 4), 1.0 / FR, -HALF, OP.mult, OP.add)
+        if t == 0:
+            ts(A("os0", 0, 4), A("jf0", 0, 4), 8.0 - rank, None, OP.add)
+            gather("s", A("bk0", 0, 64), A("nat", 0, P), A(of, 0, 4))
+        else:
+            ts(A("iz", 0, 4), A("fr1", 0, 4), 1.0 / FZ, None, OP.mult)
+            ts(A("iz", 4, 8), A("iz", 0, 4), 255, None, OP.bitwise_and)
+            cp("v", A("oz", 0, 4), A("iz", 4, 8))
+            gather("s", A("bk1", 0, 64), A("nat", 0, P), A("oz", 0, 4))
+            gather("s", A("bi1", 0, 64), A("nat", 0, P + K), A(of, 0, 4))
         gather("s", A(n("wd"), 0, 64), A("wt01", 0, 64), A(n("cd"), 0, 4))
 
     def lists(t):
@@ -537,6 +526,7 @@ def rank_program(g, core, T, topo):
 
     def rebuild(t):
         n = lambda s: s + str(t)
+        c = P + K * t + a0
         for s in ("", "s"):
             landed([A(n("land") + s, KO * r, KO * r + KO) for r in range(N) if r != rank], "col%d" % t + s, 7 * (full // NO),
                    0.9 if s else 0.6)
@@ -546,70 +536,93 @@ def rank_program(g, core, T, topo):
         for b in range(4):
             scan(A(n("h"), b, 512, 4), A("dpat", 0, 128), A("dec", 512 * b, 512 * b + 128), OP.mult, OP.subtract)
         quant(n("new"), 0, 128, n("h"), 0)
-        pick(n("W"), P + a0, P + a0 + KO, n("new"), 128, A("cl", 0, 1))
-        spread(A(n("W"), P + a0, P + a0 + KO), "new%d" % t, True)
-        spread(A(n("W") + "s", P + a0, P + a0 + KO), "new%ds" % t)
+        pick("W", c, c + KO, n("new"), 128, A("cl", 0, 1))
+        spread(A("W", c, c + KO), "new%d" % t, True)
+        spread(A("Ws", c, c + KO), "new%ds" % t)
 
-    def newcols(t):
-        n = lambda s: s + str(t)
-        tt(A(n("wb"), 0, 64), A("nat", P, P + K), A(n("bk"), 0, 64), OP.subtract)
-        tt(A(n("wc"), 0, 64), A(n("wd"), 0, 64), A(n("wb"), 0, 64), OP.mult)
-        tt(A(n("we"), 0, 64), A(n("wc"), 0, 64), A(n("bk"), 0, 64), OP.add)
+    def tables():
+        c = (rank - 8) % 16
+        act(A("ng", 1, 2), A("fb", 3, 4), AF.Copy, scale=-1.0)
+        act(A("Mu", 0, 272), A("nat", 0, 272), AF.Identity, bias=rank - 8.0)
+        act(A("xa", 0, 272), A("x16", c, c + 272), AF.Abs, bias=A("ng", 1, 2))
+        act(A("xm", 0, 272), A("xa", 0, 272), AF.Relu, bias=1.0, scale=-1.0)
+        for h in range(0, 272, 68):
+            tt(A("M", h, h + 68), A("xm", h, h + 68), A("Mu", h, h + 68), OP.mult)
+        act(A("sd", 0, 256), A("x16", 0, 256), AF.Sign)
 
     def newlist(t):
         n = lambda s: s + str(t)
-        gather("s", A(n("wg"), 0, 64), A(n("xm"), 0, 256), A(n("of"), 0, 4))
-        tt(A(n("wf"), 0, 64), A(n("we"), 0, 64), A(n("wg"), 0, 64), OP.mult)
-        scatter(A(n("M"), 0, 256), A(n("of"), 0, 4), A(n("wf"), 0, 64))
-        m, mmx, c = n("M"), n("mm"), shift(t)
-        scan(A(mmx, 0, P - c), A("sd", 0, P - c), A(m, c, P), OP.mult, OP.add)
+        old, lo, hi, off = (A("bi1", 0, 64), 8, 264, A("oz", 0, 4)) if t else (A("bk0", 0, 64), 0, 272, A("os0", 0, 4))
+        tt(A(n("wb"), 0, 64), A("nat", P + K * t, P + K * t + K), old, OP.subtract)
+        tt(A(n("wc"), 0, 64), A(n("wd"), 0, 64), A(n("wb"), 0, 64), OP.mult)
+        tt(A(n("we"), 0, 64), A(n("wc"), 0, 64), old, OP.add)
+        gather_tt(A(n("wf"), 0, 64), A("xm", lo, hi), off, A(n("we"), 0, 64), OP.mult)
+        if t == 0:
+            scatter(A("Mu", lo, hi), off, A("we0", 0, 64))
+            if rank:
+                cp("s", A("Mu", 264 - rank, 264), A("Mu", 8 - rank, 8))
+            act(A("hz", 0, 32), A("hy", 0, 32), AF.Copy, scale=FZ)
+            tt(A("vz", 0, 32), A("hz", 0, 32), A("rf", 1, 33), OP.add)
+            ts(A("zl", 0, 1), A("jc", 0, 1), 0.0, None, OP.add)
+            ts(A("zl", 1, 2), A("jc", 0, 1), 128.0, None, OP.add)
+            gather_tt(A("vj1", 0, 32), A("Mu", 8, 264), A("zl", 0, 2), A("vz", 0, 32), OP.add)
+        scatter(A("M", lo, hi), off, A(n("wf"), 0, 64))
+        if t == 0:
+            if rank:
+                cp("s", A("M", 264 - rank, 264), A("M", 8 - rank, 8))
+            return
+        c = -rank % P
+        scan(A("mm", 0, P - c), A("sd", 0, P - c), A("M", 8 + c, 8 + P), OP.mult, OP.add)
         if c:
-            scan(A(mmx, P - c, P), A("sd", P - c, P), A(m, 0, c), OP.mult, OP.add, A(mmx, P - c - 1, P - c))
-        cp("v", A(n("ml"), 0, 16), A(mmx, 15, 256, 16))
+            scan(A("mm", P - c, P), A("sd", P - c, P), A("M", 8, 8 + c), OP.mult, OP.add, A("mm", P - c - 1, P - c))
+        cp("v", A("ml", 0, 16), A("mm", 15, 256, 16))
 
     def places():
-        act(A("mc", 0, 1), A("fb", 5, 6), AF.Identity, bias=2048.0, scale=-64.0)
-        act(A("mc", 1, 2), A("fb", 6, 7), AF.Identity, bias=A("mc", 0, 1), scale=56.0)
-        act(A("mc", 2, 3), A("fb", 7, 8), AF.Identity, bias=A("mc", 1, 2), scale=56.0)
-        act(A("jm", 0, 4), A("jf0", 0, 4), AF.Identity, bias=A("mc", 2, 3), scale=8.0)
+        act(A("mc", 0, 1), A("fb", 5, 6), AF.Identity, bias=8192.0, scale=-256.0)
+        act(A("mc", 1, 2), A("fb", 6, 7), AF.Identity, bias=A("mc", 0, 1), scale=224.0)
+        act(A("mc", 2, 3), A("fb", 7, 8), AF.Identity, bias=A("mc", 1, 2), scale=224.0)
+        act(A("mc", 3, 4), A("mc", 2, 3), AF.Identity, bias=32.0)
+        act(A("jm", 0, 4), A("jf0", 0, 4), AF.Identity, bias=A("mc", 2, 3), scale=32.0)
+        act(A("jm", 4, 8), A("jf0", 0, 4), AF.Identity, bias=A("mc", 3, 4), scale=32.0)
         ts(A("iw", 0, 4), A("fr0", 0, 4), 32.0 / FR, None, OP.mult)
-        ts(A("iw", 8, 12), A("iw", 0, 4), 2, 56, OP.logical_shift_right, OP.bitwise_and)
         ts(A("iw", 4, 8), A("iw", 0, 4), 224, None, OP.bitwise_and)
-        tt(A("iw", 12, 16), A("jm", 0, 4), A("iw", 8, 12), OP.subtract)
-        ts(A("iw", 16, 20), A("iw", 12, 16), 3, 31, OP.logical_shift_right, OP.bitwise_and)
-        ts(A("iw", 20, 24), A("iw", 12, 16), 1792, None, OP.bitwise_and)
-        tt(A("wa", 0, 4), A("iw", 4, 8), A("iw", 16, 20), OP.add)
-        tt(A("wa", 4, 8), A("wa", 0, 4), A("iw", 20, 24), OP.add)
-        cp("v", A("wo", 0, 4), A("wa", 4, 8))
+        tt(A("iw", 8, 12), A("jm", 0, 4), A("iw", 4, 8), OP.subtract)
+        tt(A("iw", 12, 16), A("jm", 4, 8), A("iw", 4, 8), OP.subtract)
+        ts(A("wa", 0, 4), A("iw", 4, 8), 32.0, None, OP.add)
+        ts(A("iw", 16, 20), A("iw", 8, 12), 5, 31, OP.logical_shift_right, OP.bitwise_and)
+        ts(A("iw", 20, 24), A("iw", 8, 12), 1, 3584, OP.logical_shift_right, OP.bitwise_and)
+        ts(A("iw", 24, 28), A("iw", 12, 16), 224, None, OP.bitwise_and)
+        tt(A("wa", 4, 8), A("iw", 24, 28), A("iw", 4, 8), OP.not_equal)
+        tt(A("wa", 8, 12), A("iw", 16, 20), A("iw", 20, 24), OP.add)
+        tt(A("wa", 12, 16), A("wa", 0, 4), A("wa", 4, 8), OP.mult)
+        tt(A("wa", 16, 20), A("wa", 12, 16), A("wa", 8, 12), OP.add)
+        cp("v", A("wo", 0, 4), A("wa", 16, 20))
 
     def turned():
-        for c in range(2):
-            cp("s", A("Z", 8 * c, 256, 16), A("L1", c, 32, 2))
+        ts(A("e1", 0, 16), A("r2", 0, 16), A("fb", 1, 2), None, OP.is_equal)
+        ts(A("n1", 0, 16), A("r2", 0, 16), A("fb", 1, 2), None, OP.not_equal)
+        ts(A("gm1", 0, 16), A("rc", 0, 16), A("fb", 1, 2), BIG, OP.is_equal, OP.mult)
         ts(A("ul", 0, 8), A("one", 0, 8), A("fb", 4, 5), 0.125, OP.mult, OP.mult)
-        turn(A("Wn", 0, 256), A("Z", 0, 256))
         pick("ua", 0, 128, "uq", 128, A("ul", 0, 8))
-        ts(A("lo1", 0, 3), A("lo0", 0, 3), 8.0, None, OP.mult)
-        masks(1)
-
-    def table(dst):
-        for h in range(4):
-            pick(dst, 64 * h, 64 * h + 64, "W0", P + K, A("ml0", 4 * h, 4 * h + 4))
+        gate.append(dealt[0])
+        for c in range(2):
+            tt(A("Z", 32 + 8 * c, NB, 16), A("L1", c, 32, 2), A("n1", 0, 16), OP.mult)
+        tt(A("pz", 0, 16), A("L1", 0, 32, 2), A("e1", 0, 16), OP.mult)
+        del gate[:]
+        for h in range(2):
+            act(A("pj", 8 * h, 8 * h + 8), A("pz", h, 16, 2), AF.Copy, total=A("Z", 16 * h, 16 * h + 1))
+        turn(A("Wn", 0, NB), A("Z", 0, NB))
 
     def finish(t):
-        n = lambda s: s + str(t)
         if t == 0:
             places()
-            act(A("ng", 1, 2), A("fb", 3, 4), AF.Copy, scale=-1.0)
-            act(A("sd", 0, 256), A("x16", 0, 256), AF.Sign)
+            tables()
         else:
-            table("W1")
             quant("wq", 0, 128, "wt", 0)
-        lanes(t)
         if own == t:
             rebuild(t)
         if t == 0:
             turned()
-        newcols(t)
         newlist(t)
         lists(t)
         if t == 0 and own:
@@ -617,27 +630,30 @@ def rank_program(g, core, T, topo):
             owner_v()
             owner_t()
         others = [o for o in range(NO) if 2 * o + t != rank]
+        c = P + K * t
         for s in ("", "s"):
-            landed([A(n("W") + s, P + KO * o, P + KO * o + KO) for o in others], "new%d" % t + s, len(others) * full,
+            landed([A("W" + s, c + KO * o, c + KO * o + KO) for o in others], "new%d" % t + s, len(others) * full,
                    (1.2 if s else 0.7) + (0.0 if own == t else 4.5))
 
-    judge(0, "tA", A("L0", 0, 32))
+    judge(0, "L0")
+    dealt = [sent[-1]]
     finish(0)
-    table("tB")
-    mm(A("pc", 0, 128), "ua", 0, "W0", P + K - 128, P + K)
+    mm(A("pc", 0, 128), "ua", 0, "W", P + K - 128, P + K)
     cp("v", A("cv", 0, K), A("pc", 128 - K, 128))
-    scatter(A("Wn", 0, N * P), A("wo", 0, 4), A("cv", 0, K))
-    turn(A("Tn", 0, 256), A("Wn", 0, 256))
-    judge(1, "tB", A("Tn", 0, 256))
+    scatter(A("Wn", 0, 4096), A("wo", 0, 4), A("cv", 0, K))
+    turn(A("Tn", 0, NB), A("Wn", 0, NB))
+    judge(1, "Tn")
     finish(1)
     for h in range(2):
-        mm(A("py", 512 * h, 512 * h + 128), "wq", 0, "W1", 128 * h, 128 * h + 128)
+        mm(A("py", 512 * h, 512 * h + 128), "wq", 0, "W", 128 * h, 128 * h + 128)
         cp("s", A("ya", 128 * h, 128 * h + 128), A("py", 512 * h, 512 * h + 128))
-    pick2("F", 128, "W1", P + K, "ml1", 8)
-    mm(A("pc", 0, 128), "wq", 0, "W1", P + K - 128, P + K)
-    cp("v", A("ya", P, P + K), A("pc", 128 - K, 128))
+    mm(A("pc", 512, 640), "wq", 0, "W", P + K - 128, P + K)
+    cp("s", A("ya", P, P + K), A("pc", 640 - K, 640))
+    pick2("F", 128, "W", P + 2 * K, "ml", 8)
+    mm(A("pc", 0, 128), "wq", 0, "W", P, P + 2 * K)
+    cp("v", A("ya", P + K, P + 2 * K), A("pc", 128 - K, 128))
     for h, e in ((0, "v"), (1, "s")):
-        gather(e, A("yb", 128 * h, 128 * h + 128), A("ya", 0, P + K), A("ml1", 8 * h, 8 * h + 8))
+        gather(e, A("yb", 128 * h, 128 * h + 128), A("ya", 0, P + 2 * K), A("ml", 8 * h, 8 * h + 8))
     for h in range(2):
         dma("y", None, A("F", 128 * h, 128 * h + 128), "st_c", 32, out_ap=T.oc[:, 512 * h:512 * h + 512],
             in_ap=T.F[:, 128 * h:128 * h + 128].bitcast(dt.uint8))

@@ -3,7 +3,6 @@ from concourse.mybir import dt, AluOpType, AxisListType, ActivationFunctionType
 
 OP = AluOpType
 AF = ActivationFunctionType
-X = AxisListType.X
 N, P, K, NO, KO = 8, 256, 64, 4, 16
 BIG = 1e29
 STEP = 1.0 - 2.0 ** -24
@@ -11,8 +10,10 @@ TINY = 2.0 ** -118
 FR = 2.0 ** -7
 FZ = 2.0 ** -15
 HALF = 127.5 / 256
-CY, HAND, LOAD = 1.04e-3, 0.16, 1.3
 NB = 32 * (N + 1)
+CY, HAND, LOAD, MARGIN, SLACK, EXTRA = 1.04e-3, 0.19, 0.65, 0.07, 0.4, 0.05
+LU, LA, LB = 0.8, 0.95, 1.15
+LC0, LC1, LD0, LD1, LAGN, LN0, LN1, LW = 2.0, 1.2, 0.6, 0.9, 1.3, 0.5, 1.2, 4.5
 
 F4 = "float8_e4m3fn_x4"
 SCRATCH = {}
@@ -36,21 +37,19 @@ def _parts(buf, *parts):
     _sb(buf, c)
 
 
-for _n, _w in (("tbt", 4 * P + 4 * N), ("ut", 512), ("wt", 512), ("ee", 528), ("zt", 512)):
+for _n, _w in (("tbt", 4 * P + 4 * N), ("ut", 512), ("wt", 512), ("ee", 528), ("zt", 528)):
     _sb(_n, _w, "bfloat16")
-_parts("con", ("rc", 40), ("hm", 32), ("jc", 1), ("hx", 32), ("hy", 32), ("rf", 40), ("fb", 8), ("sd32", 32),
+_parts("con", ("hm", 32), ("hx", 32), ("hy", 32), ("rf", 40), ("fb", 10), ("sd32", 32),
        ("sp", 16), ("one", 32), ("frc", 32), ("oc", 8), ("klc", 16), ("ng", 4), ("eq0", 32), ("dm0", 32),
-       ("gm0", 16), ("gm1", 16), ("lof", 4), ("vj0", 32), ("vj1", 32), ("pr", 64), ("l16", 64), ("t3", 64), ("t4", 64), ("t5", 64),
-       ("t6", 64), ("t7", 64), ("t8", 64), ("mc", 4), ("jm", 8), ("wa", 24), ("r8", 40), ("r2", 16), ("e1", 16), ("n1", 16),
+       ("gm0", 16), ("gm1", 16), ("lof", 8), ("vj0", 32), ("vj1", 32), ("pr", 64), ("l16", 64), ("t3", 64), ("t4", 64), ("t5", 64),
+       ("t6", 64), ("t7", 64), ("t8", 64), ("mc", 4), ("wa", 24), ("r8", 40), ("r2", 16), ("e1", 16), ("n1", 16),
        ("pz", 16), ("pj", 16), ("sr", 32), ("sq", 32), ("vz", 32), ("hz", 32))
-for _n, _w in (("nat", 528), ("x16", 288), ("xa", 272), ("xm", 272), ("md", 68), ("Mu", 272), ("M", 272), ("mm", P),
+for _n, _w in (("nat", 512), ("x16", 288), ("xa", 272), ("xm", 272), ("md", 68), ("Mu", 272), ("Mn", 272), ("M", 272), ("mm", P),
                ("sd", 256), ("dpat", 128), ("yb", 256), ("ya", P + 2 * K), ("lt", 64), ("wt01", 64), ("tab", 128),
-               ("Z", NB), ("Wn", 4096), ("Tn", NB), ("cv", K)):
+               ("Wn", 4096), ("Tn", NB), ("cv", 128), ("Ln", 144)):
     _sb(_n, _w)
-_sb("pi", 2, "int32")
-_sb("ib", 8, "int32")
-_sb("iw", 28, "int32")
-_sb("iz", 8, "int32")
+for _n, _w in (("ib", 11), ("iw", 48), ("iz", 8), ("ic", 20)):
+    _sb(_n, _w, "int32")
 for _n, _w in (("cl", 2), ("lo0", 4), ("sl", 2), ("zl", 2), ("gl", 2), ("ul", 8), ("wo", 4), ("oz", 4), ("os0", 4), ("ml", 16)):
     _sb(_n, _w, "uint16")
 for _n, _w in (("tR", P), ("F", P), ("uq", 128), ("ua", 128), ("wq", 128), ("eq", 512), ("W", P + 2 * K)):
@@ -58,8 +57,8 @@ for _n, _w in (("tR", P), ("F", P), ("uq", 128), ("ua", 128), ("wq", 128), ("eq"
 for _t in "01":
     _parts("jd" + _t, ("d1" + _t, 32), ("so" + _t, 32), ("du" + _t, 64), ("lw" + _t, 32), ("px" + _t, 16), ("tl" + _t, 64),
            ("tt" + _t, 160), ("jf" + _t, 4), ("fr" + _t, 4), ("zz" + _t, 16), ("lf" + _t, 16),
-           ("zo" + _t, 8), ("wg" + _t, 64), ("wb" + _t, 64), ("wc" + _t, 64), ("wd" + _t, 64), ("we" + _t, 64),
-           ("wf" + _t, 64), ("th" + _t, 136), ("cm" + _t, 256), ("cs" + _t, 128), ("ca" + _t, 2), ("ls" + _t, 2), ("rl" + _t, 256),
+           ("zo" + _t, 8), ("wb" + _t, 64), ("wc" + _t, 64), ("wd" + _t, 64), ("we" + _t, 64),
+           ("wf" + _t, 64), ("th" + _t, 136), ("cm" + _t, 256), ("cs" + _t, 128), ("ca" + _t, 4), ("ls" + _t, 2), ("rl" + _t, 256),
            ("cj" + _t, 256), ("lj" + _t, 16), ("bi" + _t, 64))
     for _n, _w in (("L", 32), ("S", 256), ("Lz", 64), ("val", 32), ("D", 272), ("xb", 40), ("bk", 64), ("lk", 64)):
         _sb(_n + _t, _w)
@@ -68,13 +67,14 @@ for _t in "01":
     _sb("h" + _t, 512, "bfloat16")
     for _n, _w in (("slot", K), ("land", 256), ("ord", 128), ("new", 128)):
         _mx(_n + _t, _w)
+VIEW["Z"] = VIEW["rl0"]
 SCRATCH["pc"] = ("psum", [128, 1024], "float32")
 SCRATCH["dec"] = ("psum", [128, 2048], "float32")
 SCRATCH["py"] = ("psum", [128, 1024], "float32")
 PSUM = ("pc", "dec", "py")
 
-SEMAPHORES = ["qv", "qs", "qt", "qg", "out", "ld_u", "ld_a", "ld_b", "ld_w", "st_c", "st_s", "st_y",
-              "st_b0", "st_b1", "ck0", "ck1", "col0", "col0s", "col1", "col1s", "new0", "new0s", "new1", "new1s"]
+SEMAPHORES = ["qv", "qs", "qt", "qg", "out", "ld_u", "ld_a", "ld_b", "ld_w", "st_c", "st_s", "st_y", "st_b0", "st_b1",
+              "ck0", "ck1", "ckn", "col0", "col0s", "col1", "col1s", "new0", "new0s", "new1", "new1s"]
 
 
 def rank_program(g, core, T, topo):
@@ -121,7 +121,7 @@ def rank_program(g, core, T, topo):
         for r in outs:
             wrote.setdefault(r[0], []).append((r[1], r[2], r[3], tok))
 
-    jobs, jw, jr, sent, gate = [], {}, {}, [], []
+    jobs, jw, jr, sent, gate, chain, holds = [], {}, {}, [], [], [], set()
 
     def job(e, outs, ins, run, cost, lag, after=()):
         need = set(after) | set(gate)
@@ -135,7 +135,7 @@ def rank_program(g, core, T, topo):
                 table.setdefault(r[0], []).append((r[1], r[2], r[3], k))
         return k
 
-    def op(e, outs, ins, call, cost=None):
+    def op(e, outs, ins, call, cost=None, lag=HAND):
         def run():
             order(e, ins, outs)
             inst = call()
@@ -143,9 +143,9 @@ def rank_program(g, core, T, topo):
             inst.then_inc(T.sem["q" + e], 1)
             final["q" + e] = count[e]
             note(ins, outs, ("q" + e, count[e], e))
-        job(e, outs, ins, run, max(64, max(r[5] for r in outs[:1] + ins[:1])) * CY if cost is None else cost, HAND)
+        job(e, outs, ins, run, max(64, max(r[5] for r in outs[:1] + ins[:1])) * CY if cost is None else cost, lag)
 
-    def dma(e, out, in_, sem, total, out_ap=None, in_ap=None, behind=None):
+    def dma(e, out, in_, sem, total, out_ap=None, in_ap=None, behind=None, lag=LOAD):
         ins, outs = [in_] if in_ else [], [out] if out else []
 
         def run():
@@ -155,24 +155,35 @@ def rank_program(g, core, T, topo):
             eng[e].dma_start(o, i).then_inc(T.sem[sem], 16)
             final[sem] = total
             note(ins, outs, (sem, total, "dma"))
-        job(e, outs, ins + ([behind] if behind else []), run, 0.1, LOAD)
+        job(e, outs, ins + ([behind] if behind else []), run, 0.1, lag)
+
+    def hold(ref, before):
+        holds.add(job(None, [ref], list(before), lambda: None, 0.0, 0.0))
 
     def emit():
         tail = [0.0] * len(jobs)
         for k in range(len(jobs) - 1, -1, -1):
             tail[k] += jobs[k][2] + jobs[k][3]
             for d in jobs[k][4]:
-                tail[d] = max(tail[d], tail[k])
-        busy, start = {}, {}
+                tail[d] = max(tail[d], tail[k] - (jobs[d][3] if k in holds and jobs[d][0] else 0.0))
+        busy, start, soon = {}, {}, []
+
+        def done(k, d):
+            return jobs[d][2] + (0.0 if k in holds and jobs[d][0] else jobs[d][3])
+
+        for k in range(len(jobs)):
+            soon.append(max([soon[d] + done(k, d) for d in jobs[k][4]], default=0.0))
+        whole = max(a + b for a, b in zip(soon, tail))
         for k in sorted(range(len(jobs)), key=lambda k: (-tail[k], k)):
             e, run, cost, lag, need = jobs[k]
-            t = max([start[d] + jobs[d][2] + jobs[d][3] for d in need], default=0.0)
+            side = soon[k] + tail[k] < whole - SLACK
+            t = max([start[d] + done(k, d) + (EXTRA if side and jobs[d][0] else 0.0) for d in need], default=0.0)
             if e:
-                for a, b in sorted(busy.setdefault(e, [])):
-                    if t + cost <= a + 1e-9:
+                for a, b, hot in sorted(busy.setdefault(e, [])):
+                    if t + cost + (MARGIN if hot and side else 0.0) <= a + 1e-9:
                         break
                     t = max(t, b)
-                busy[e].append((t, t + cost))
+                busy[e].append((t, t + cost, not side))
             start[k] = t
         for k in sorted(start, key=lambda k: (start[k], k)):
             jobs[k][1]()
@@ -220,9 +231,18 @@ def rank_program(g, core, T, topo):
     def turn(out, a):
         op("v", [out], [a], lambda: g.vector.transpose(out[4], a[4]))
 
+    def own_call(out, ins, call, cost):
+        gate.extend(chain)
+        op("g", [out], ins, call, cost, 0.0)
+        chain[:] = [len(jobs) - 1]
+        del gate[:]
+
     def iota(out, pat, base, cm, flag=True):
         kw = {"allow_small_or_imprecise_dtypes": True} if flag else {}
-        op("g", [out], [], lambda: g.iota(out[4], pat, base, cm, **kw), 0.16 + 2 * CY * out[5])
+        own_call(out, [], lambda: g.iota(out[4], pat, base, cm, **kw), 0.16 + 2 * CY * out[5])
+
+    def spot(out, a, base):
+        own_call(out, [a], lambda: g.affine_select(out[4], a[4], [[1, out[5]]], OP.not_equal, 1.0, base, -4), 0.21 + 2 * CY * out[5])
 
     def by(out):
         return 0.07 + 1.5 * CY * out[5]
@@ -235,6 +255,9 @@ def rank_program(g, core, T, topo):
 
     def gather_tt(out, win, off, b, o):
         op("v", [out], [win, off, b], lambda: g.vector.tensor_tensor(out[4], win[4].indirect(off[4]), b[4], o), by(out))
+
+    def gather_ts(out, win, off, x, b):
+        op("v", [out], [win, off, b], lambda: g.vector.tensor_scalar(out[4], win[4].indirect(off[4]), x, b[4], OP.mult, OP.add), by(out))
 
     def scatter(win, off, val):
         op("v", [win], [val, off], lambda: g.vector.tensor_copy(win[4].indirect(off[4]), val[4]), 0.06 + 3.5 * CY * val[5])
@@ -251,10 +274,10 @@ def rank_program(g, core, T, topo):
         pickc(dst, c0, c1, src, n, off)
         picks("s", dst, c0, c1, src, n, off)
 
-    def pick2(dst, n1, src, n, off, k):
+    def pick2(dst, n1, src, n, off, k, who):
         for h in range(2):
             pickc(dst, n1 * h, n1 * h + n1, src, n, A(off, k * h, k * h + k))
-        for h, e in ((0, "s"), (1, "v")):
+        for h, e in enumerate(who):
             picks(e, dst, n1 * h, n1 * h + n1, src, n, A(off, k * h, k * h + k))
 
     def quant(dst, c0, c1, tile, at):
@@ -265,13 +288,17 @@ def rank_program(g, core, T, topo):
         l, ls, r, rs = A(lhs, a, a + 128), A(lhs + "s", a, a + 128), A(rhs, b0, b1), A(rhs + "s", b0, b1)
         op("t", [out], [l, ls, r, rs], lambda: g.tensor.matmul_mx(out[4], l[4], ls[4], r[4], rs[4], True, True), 144 * 1.5 * CY)
 
-    def around(buf, src, step, end, places):
+    def around(buf, src, step, end, places, who, unturned=None):
         k = 0
         for x, c in places:
             for a in ((0, 2) if x == 2 else range(4)):
                 w = 64 if x == 2 else 32
                 b = a ^ x
-                cp("sv"[k & 1], A(buf, c, end, step, 32 * a, 32 * a + w), A(buf, src, end, step, 32 * b, 32 * b + w))
+                o = A(buf, c, end, step, 32 * a, 32 * a + w)
+                if who[k] == "t":
+                    turn(o, A(unturned, 0, 64, 1, 32 * b, 32 * b + w))
+                else:
+                    cp(who[k], o, A(buf, src, end, step, 32 * b, 32 * b + w))
                 k += 1
 
     peers = [c for c in T.cores if c != core]
@@ -283,9 +310,9 @@ def rank_program(g, core, T, topo):
     def raw(r, codes):
         return r[4].bitcast(dt.uint8) if codes else r[4]
 
-    def spread(ref, sem, codes=False):
+    def spread(ref, sem, codes=False, behind=()):
         def run():
-            order("g", [ref], [])
+            order("g", [ref] + list(behind), [])
             m = topo.mask(core, peers[0])
             for c in peers:
                 m &= topo.mask(core, c)
@@ -293,7 +320,7 @@ def rank_program(g, core, T, topo):
                                                   srcs=[raw(ref, codes)], dsts=[raw(ref, codes) for _ in peers])],
                                local_sem=T.sem["out"])
             final["out"] = final.get("out", 0) + bin(m).count("1")
-        sent.append(job("g", [], [ref], run, 0.5, 0.0, sent[-1:]))
+        sent.append(job("g", [], [ref] + list(behind), run, 0.5, 0.0, sent[-1:]))
 
     full = len(topo.engines(core, peers[0]))
 
@@ -302,6 +329,23 @@ def rank_program(g, core, T, topo):
             note([], refs, (sem, total, "remote"))
             final[sem] = total
         job(None, refs, [], run, 0.0, lag, sent[-1:])
+
+    def checks(parts):
+        srcs = [A("L0", 28 + 2 * h, 30 + 2 * h) for h in sorted({p[0] for p in parts})]
+
+        def run():
+            order("g", srcs, [])
+            tr = []
+            for h, a, b, e0, e1 in parts:
+                to = [(rank + k) % N for k in range(a, b)]
+                es = topo.engines(core, T.cores[to[0]])[e0 * full // 4:e1 * full // 4]
+                at = [14 * h + 2 * (rank - (rank > r)) for r in to]
+                tr.append(RemoteDMATransfer(dst_ids=[dest(T.cores[r]) for r in to], dma_engine_mask=sum(1 << e for e in es),
+                                            remote_sem=T.sem["ck0"], srcs=[A("L0", 28 + 2 * h, 30 + 2 * h)[4]],
+                                            dsts=[A("L0", x, x + 2)[4] for x in at]))
+                final["out"] = final.get("out", 0) + len(es)
+            g.remote_dma_fused(tr, local_sem=T.sem["out"])
+        sent.append(job("g", [], srcs, run, 0.5, 0.0, sent[-1:] + chain))
 
     def deal(t, codes):
         s = "" if codes else "s"
@@ -327,75 +371,97 @@ def rank_program(g, core, T, topo):
     o_ = rank // 2
     a0 = KO * o_
 
-    dma("y", A("tbt", 0, 512), None, "ld_a", 16, in_ap=T.tb[:, 0:512])
-    dma("s", A("ut", 0, 8), None, "ld_u", 16, in_ap=T.u[:, 0:8])
-    dma("s", A("tbt", 512, 1024), None, "ld_b", 16, in_ap=T.tb[:, 512:1024])
+    dma("y", A("tbt", 0, 512), None, "ld_a", 16, in_ap=T.tb[:, 0:512], lag=LA)
+    dma("s", A("ut", 0, 8), None, "ld_u", 16, in_ap=T.u[:, 0:8], lag=LU)
+    dma("s", A("tbt", 512, 1024), None, "ld_b", 16, in_ap=T.tb[:, 512:1024], lag=LB)
     dma("y", A("wt", 0, 512), None, "ld_w", 16, in_ap=T.w[:], behind=A("tbt", 512, 1024))
 
-    iota(A("pi", 0, 2), [[1, 2]], 0, 1, False)
-    iota(A("nat", 0, 128), [[1, 128]], 0, 0)
-    iota(A("rc", 0, 40), [[0, 5], [1, 8]], 0, 0)
-    iota(A("hm", 0, 32), [[0, 2], [1, 2], [0, 8]], 0, 0)
-    iota(A("jc", 0, 1), [[1, 1]], 0, 1)
+    iota(A("ib", 9, 11), [[1, 2]], 0, 1, False)
     iota(A("lt", 0, 64), [[0, 8], [1, 8]], 0, 0)
+    iota(A("nat", 0, 128), [[1, 128]], 0, 0)
     iota(A("pr", 0, 64), [[16, 8], [0, 8]], 0, 0)
-    iota(A("hx", 0, 32), [[128, 2], [1, 16]], 0, 0)
+
+    def ones(h):
+        fill(A("zt", h, h + 264), 0.0)
+        spot(A("ee", h, h + 264), A("zt", h, h + 264), h - 4)
+
     fill(A("ut", 8, 512), 0.0)
+    if own == 0:
+        ones(0)
     fill(A("one", 0, 32), 1.0)
     fill(A("frc", 0, 32), FR)
-    for col, (src, bits) in enumerate(((0, 7), (1, 7), (0, 31), (0, 15), (0, 8), (0, 112), (0, 64), (0, 32))):
-        ts(A("ib", col, col + 1), A("pi", src, src + 1), bits, None, OP.bitwise_and)
-    cp("v", A("fb", 0, 8), A("ib", 0, 8))
+    ts(A("ib", 0, 2), A("ib", 9, 11), 7, None, OP.bitwise_and)
+    for col, bits in enumerate((31, 15, 8, 112, 64, 32, 1)):
+        ts(A("ib", col + 2, col + 3), A("ib", 9, 10), bits, None, OP.bitwise_and)
+    cp("v", A("fb", 0, 10), A("ib", 0, 10))
 
-    ts(A("eq0", 0, 32), A("rc", 0, 32), A("fb", 0, 1), -1.0, OP.is_equal, OP.mult)
-    ts(A("gm0", 0, 16), A("rc", 0, 16), A("fb", 0, 1), BIG, OP.is_equal, OP.mult)
+    ts(A("eq0", 0, 32), A("lt", 0, 32), A("fb", 0, 1), -1.0, OP.is_equal, OP.mult)
+    ts(A("gm0", 0, 16), A("lt", 0, 16), A("fb", 0, 1), BIG, OP.is_equal, OP.mult)
+    const(A("hm", 0, 32), 0.0, A("lt", 0, 32))
+    for h in (8, 24):
+        const(A("hm", h, h + 8), 1.0, A("lt", 0, 8))
     tt(A("dm0", 0, 32), A("eq0", 0, 32), A("hm", 0, 32), OP.add)
+    ts(A("gm1", 0, 2), A("fb", 0, 2), 0.0, -FR, OP.is_equal, OP.mult)
+    hold(A("uq", 0, 128), [A("ib", 0, 9)])
     quant("uq", 0, 128, "ut", 0)
     act(A("nat", 128, 256), A("nat", 0, 128), AF.Identity, bias=128.0)
+    const(A("Ln", 0, 144), 0.0, A("nat", 0, 144))
     act(A("nat", 256, 512), A("nat", 0, 256), AF.Identity, bias=256.0)
-    act(A("nat", 512, 528), A("nat", 0, 16), AF.Identity, bias=512.0)
-    act(A("ng", 0, 1), A("jc", 0, 1), AF.Identity, bias=4.0, scale=4.0)
-
-    def share(t, bank, e):
-        for h in range(2):
-            cp(e, A("L%d" % t, 4 * rank + 2 * h, 4 * rank + 2 * h + 2), A(bank, 512 * h, 512 * h + 2))
-        spread(A("L%d" % t, 4 * rank, 4 * rank + 4), "ck%d" % t)
-        landed([A("L%d" % t, 4 * r, 4 * r + 4) for r in range(N) if r != rank], "ck%d" % t, 7 * full, 1.2 if t else 2.4)
 
     for h in range(2):
         quant("W", 128 * h, 128 * h + 128, "tbt", 512 * h)
         mm(A("pc", 512 * h, 512 * h + 128), "W", 128 * h, "uq", 0, 128)
-    share(0, "pc", "v")
+        cp("v", A("L0", 28 + 2 * h, 30 + 2 * h), A("pc", 512 * h, 512 * h + 2))
+    checks([(0, 1, 4, 0, 1)])
+    checks([(0, 4, N, 1, 2), (1, 1, N, 2, 4)])
+    landed([A("L0", 0, 28)], "ck0", 7 * 3 * full // 4, LC0)
+    chain[:] = sent[-1:]
 
-    iota(A("D0", 0, 272), [[0, 272]], 0, 0)
-    iota(A("x16", 0, 288), [[0, 18], [1, 16]], 0, 0)
-    iota(A("D1", 0, 272), [[0, 272]], 0, 0)
-    iota(A("Z", 0, NB), [[0, NB]], 0, 0)
-    iota(A("r2", 0, 16), [[1, 8], [0, 2]], 0, 0)
+    if own == 0:
+        ones(264)
+    iota(A("hx", 0, 32), [[128, 2], [1, 16]], 0, 0)
     iota(A("sr", 0, 16), [[0, 4], [8, 2], [24, 2]], 7, 0)
     iota(A("sr", 16, 32), [[0, 4], [8, 2], [-16, 2]], 23, 0)
+    iota(A("D0", 0, 96), [[0, 96]], 0, 0)
+    iota(A("x16", 0, 288), [[0, 18], [1, 16]], 0, 0)
+    iota(A("r2", 0, 16), [[1, 8], [0, 2]], 0, 0)
+    if own:
+        ones(0)
+        ones(264)
+    iota(A("D1", 0, 96), [[0, 96]], 0, 0)
     const(A("sr", 4, 5), 7.0 + 8 * (o_ >> 1) + 24 * (o_ & 1), A("one", 0, 1))
     const(A("sr", 20, 21), 23.0 + 8 * (o_ >> 1) - 16 * (o_ & 1), A("one", 0, 1))
     turn(A("sq", 0, 32), A("sr", 0, 32))
     cp("v", A("sl", 0, 2), A("sq", 0, 2))
-    ts(A("lo0", 0, 1), A("fb", 0, 1), 4.0, None, OP.mult)
-    ts(A("lo0", 1, 2), A("fb", 0, 1), 4.0, 2.0, OP.mult, OP.add)
+    act(A("lof", 0, 1), A("fb", 0, 1), AF.Sign, bias=-float(rank))
+    act(A("lof", 1, 2), A("lof", 0, 1), AF.Relu, scale=2.0)
+    act(A("lof", 2, 3), A("lof", 0, 1), AF.Abs)
+    act(A("lof", 3, 4), A("fb", 0, 1), AF.Identity, bias=28.0 - 2 * rank, scale=2.0)
+    act(A("lof", 4, 5), A("lof", 2, 3), AF.Identity, bias=A("lof", 3, 4), scale=2.0 * rank - 28)
+    act(A("lof", 5, 6), A("lof", 2, 3), AF.Identity, bias=2.0, scale=12.0)
+    act(A("lof", 6, 7), A("lof", 2, 3), AF.Identity, bias=0.25, scale=1.5)
+    act(A("lof", 7, 8), A("fb", 4, 5), AF.Identity, bias=1.0, scale=A("lof", 6, 7))
+    ts(A("lo0", 0, 1), A("lof", 4, 5), A("lof", 1, 2), None, OP.subtract)
+    ts(A("lo0", 1, 2), A("lof", 4, 5), A("lof", 1, 2), A("lof", 5, 6), OP.subtract, OP.add)
+    ts(A("lo0", 2, 3), A("lof", 4, 5), A("lof", 1, 2), A("lof", 7, 8), OP.subtract, OP.add)
     if rank:
         cp("s", A("tbt", 4 * P, 4 * P + 4 * N), A("tbt", 0, 4 * N))
         for h in range(2):
             quant("tR", 128 * h, 128 * h + 128, "tbt", 4 * rank + 512 * h)
     for h in range(2):
         mm(A("py", 512 * h, 512 * h + 128), "tR" if rank else "W", 128 * h, "uq", 0, 128)
-    act(A("lof", 0, 1), A("fb", 4, 5), AF.Identity, bias=1.0, scale=0.25)
-    act(A("lof", 1, 2), A("fb", 0, 1), AF.Identity, bias=A("lof", 0, 1), scale=4.0)
     cp("s", A("sd32", 0, 32), A("one", 0, 32))
     const(A("sd32", 0, 32, 16), 0.0, A("nat", 0, 2))
     const(A("r8", 0, 40), 1.0, A("nat", 0, 40))
     const(A("r8", 0, 40, 8), 0.0, A("nat", 0, 5))
     const(A("sp", 0, 16), 0.0, A("nat", 0, 16))
     const(A("sp", 0, 16, 8), -BIG, A("nat", 0, 2))
-    act(A("rf", 0, 40), A("rc", 0, 40), AF.Copy, scale=8.0 * FR)
-    share(1, "py", "s")
+    act(A("rf", 0, 40), A("lt", 0, 40), AF.Copy, scale=8.0 * FR)
+    const(A("rf", 0, 40, 8), FR, A("nat", 0, 5))
+    for h in range(2):
+        cp("s", A("L1", 4 * rank + 2 * h, 4 * rank + 2 * h + 2), A("py", 512 * h, 512 * h + 2))
+    spread(A("L1", 4 * rank, 4 * rank + 4), "ck1", False, [A("Ln", 0, 144)])
+    landed([A("L1", 4 * r, 4 * r + 4) for r in range(N) if r != rank], "ck1", 7 * full, LC1)
 
     def owner():
         act(A("oc", 0, 1), A("fb", 0, 1), AF.Identity, bias=-16.0, scale=16.0)
@@ -403,10 +469,9 @@ def rank_program(g, core, T, topo):
         act(A("oc", 2, 3), A("fb", 0, 1), AF.Relu, bias=1.0, scale=-1.0)
         act(A("oc", 3, 4), A("fb", 4, 5), AF.Copy, scale=0.125)
         act(A("oc", 4, 5), A("fb", 4, 5), AF.Identity, bias=1.0, scale=-0.125)
-        act(A("oc", 5, 6), A("fb", 4, 5), AF.Identity, bias=-HALF, scale=8.0)
-        act(A("oc", 6, 7), A("fb", 4, 5), AF.Identity, bias=7.0)
-        act(A("klc", 0, 8), A("nat", 0, 8), AF.Copy, scale=A("oc", 4, 5))
-        act(A("klc", 8, 16), A("nat", 8, 16), AF.Copy, scale=A("oc", 3, 4))
+        act(A("oc", 5, 6), A("fb", 8, 9), AF.Copy, scale=64.0 * FR / FZ)
+        act(A("klc", 0, 16, 2), A("nat", 0, 16, 2), AF.Copy, scale=A("oc", 4, 5))
+        act(A("klc", 1, 16, 2), A("nat", 1, 16, 2), AF.Copy, scale=A("oc", 3, 4))
         act(A("l16", 0, 64), A("lt", 0, 64), AF.Copy, scale=16.0)
         act(A("t4", 0, 64), A("pr", 0, 64), AF.Identity, bias=A("oc", 1, 2), scale=A("oc", 2, 3))
         const(A("dpat", 0, 128), 1.0, A("nat", 0, 128))
@@ -414,13 +479,10 @@ def rank_program(g, core, T, topo):
         const(A("dpat", 1, 128, 8), -1.0, A("nat", 0, 16))
 
     def owner_v():
-        fill(A("zt", 0, 512), 0.0)
-        for h in range(0, 528, 132):
-            ts(A("ee", h, h + 132), A("nat", h, h + 132), A("ng", 0, 1), None, OP.is_equal)
         quant("land%d" % own, 128, 256, "zt", 0)
         for b in range(4):
             quant("eq", 128 * b, 128 * b + 128, "ee", 4 - b)
-        ts(A("cl", 0, 1), A("fb", 0, 1), 16.0, A("oc", 6, 7), OP.mult, OP.add)
+        ts(A("cl", 0, 1), A("fb", 3, 4), 8.0, 7.0, OP.mult, OP.add)
 
     def owner_t():
         ts(A("t3", 0, 64), A("pr", 0, 64), A("oc", 0, 1), 16.0, OP.is_le, OP.mult)
@@ -431,18 +493,21 @@ def rank_program(g, core, T, topo):
         act(A("tab", 0, 64), A("t8", 0, 64), AF.Copy, scale=A("oc", 4, 5))
         act(A("tab", 64, 128), A("t8", 0, 64), AF.Copy, scale=A("oc", 3, 4))
 
-    cp("v", A("lo0", 2, 3), A("lof", 1, 2))
-    ts(A("gl", 0, 1), A("fb", 2, 3), 0.0, None, OP.add)
-    ts(A("gl", 1, 2), A("fb", 2, 3), 32.0, None, OP.add)
+    ts(A("gl", 0, 2), A("nat", 0, 33, 32), A("fb", 2, 3), None, OP.add)
     if own == 0:
         owner()
         owner_v()
+        ts(A("ul", 0, 8), A("one", 0, 8), A("fb", 8, 9), None, OP.mult)
+        pick("ua", 0, 128, "uq", 128, A("ul", 0, 8))
     ts(A("md", 0, 64, 2), A("nat", 0, 32), A("fb", 2, 3), STEP, OP.is_ge, OP.max)
     act(A("md", 65, 66), A("fb", 7, 8), AF.Identity, bias=1.0, scale=(STEP - 1.0) / 32)
     act(A("md", 64, 65), A("fb", 6, 7), AF.Identity, bias=1.0, scale=(STEP - 1.0) / 64)
     act(A("md", 1, 64, 2), A("one", 0, 32), AF.Copy, scale=A("md", 65, 66))
     ts(A("hy", 0, 32), A("hx", 0, 32), A("fb", 5, 6), None, OP.add)
     tt(A("vj0", 0, 32), A("hy", 0, 32), A("rf", 0, 32), OP.add)
+    act(A("hz", 0, 32), A("hy", 0, 32), AF.Copy, scale=FZ)
+    tt(A("vz", 0, 32), A("hz", 0, 32), A("rf", 1, 33), OP.add)
+    ts(A("zl", 0, 2), A("hx", 0, 32, 16), A("fb", 9, 10), None, OP.add)
     if own == 0:
         owner_t()
     ts(A("wt01", 0, 64), A("lt", 0, 64), float(rank), None, OP.is_equal)
@@ -457,43 +522,51 @@ def rank_program(g, core, T, topo):
             scan(A(so, 0, 32), A("sd32", 0, 32), A(d1, 0, 32), OP.mult, OP.subtract)
         else:
             for h in range(2):
-                scan(A(so, 16 * h + 8, 16 * h + 16), A("one", 0, 8), A(i, 32 + 16 * h, NB, 32), OP.mult, OP.subtract,
-                     A(i, 16 * h, 16 * h + 1))
-                act(A(lw, 8 * h, 8 * h + 8), A(i, 40 + 16 * h, NB, 32), AF.Abs)
+                scan(A(so, 16 * h + 8, 16 * h + 16), A("one", 0, 8), A(i, 46 + 2 * h, NB, 32), OP.mult, OP.subtract,
+                     A(i, 14 + 2 * h, 15 + 2 * h))
+                act(A(lw, 16 + 8 * h, 24 + 8 * h), A(i, 47 + 2 * h, NB, 32), AF.Abs)
         for h in range(2):
             act(A(du, 32 * h, 32 * h + 32), A("one", 0, 32), AF.Abs, bias=TINY, scale=A(so, 16 * h + 15, 16 * h + 16))
-        tt(A(lw, 16, 32), A(lw, 0, 16), A(n("gm"), 0, 16), OP.subtract)
+        if t == 0:
+            tt(A(lw, 16, 32), A(lw, 0, 16), A(n("gm"), 0, 16), OP.subtract)
         scan(A(px, 0, 16), A("sp", 0, 16), A(lw, 16, 32), OP.add, OP.max)
         turn(A(S, 0, 256, 4), A(du, 0, 64))
         for h in range(2):
             act(A(th, 68 * h, 68 * h + 65), A("md", 0, 65), AF.Copy, scale=A(du, 32 * h, 32 * h + 1))
-        around(S, 0, 4, 256, ((1, 2), (2, 1), (3, 3)))
+        around(S, 0, 4, 256, ((1, 2), (2, 1), (3, 3)), "tttttttsss", du)
         for h in range(2):
             act(A(n("lj"), 8 * h, 8 * h + 8), A(px, 8 * h, 8 * h + 8), AF.Sign, bias=A(px, 8 * h + 7, 8 * h + 8), scale=-1.0,
                 total=A(ls, h, h + 1))
         for h in range(2):
-            ts(A(tl, 32 * h, 32 * h + 32), A("frc", 0, 32), A(ls, h, h + 1), None, OP.mult)
+            act(A(tl, 32 * h, 32 * h + 32), A("frc", 0, 32), AF.Relu, bias=A("gm1", t, t + 1), scale=A(ls, h, h + 1))
         turn(A(n("Lz"), 0, 64), A(tl, 0, 64))
         gather_tt(A(n("val"), 0, 32), A(n("Lz"), 0, 64), A("gl", 0, 2), A("vj%d" % t, 0, 32), OP.add)
-        for h in range(2):
-            act(A(rl, 128 * h, 128 * h + 128), A(S, 128 - 128 * h, 256 - 128 * h), AF.Sign, bias=A(du, 32 * h, 32 * h + 1), scale=-1.0)
-        for h in range(2):
-            act(A(cj, 128 * h, 128 * h + 128), A(rl, 128 * h, 128 * h + 128), AF.Relu, scale=2.0 * h - 1.0, total=A(ca, h, h + 1))
+        for b in range(2):
+            for h in range(2):
+                act(A(rl, 128 * h + 64 * b, 128 * h + 64 * b + 64), A(S, 128 - 128 * h + b, 256 - 128 * h, 2), AF.Sign,
+                    bias=A(du, 32 * h, 32 * h + 1), scale=-1.0)
+        for b in range(2):
+            for h in range(2):
+                c = 128 * h + 64 * b
+                act(A(cj, c, c + 64), A(rl, c, c + 64), AF.Relu, scale=2.0 * h - 1.0, total=A(ca, 2 * h + b, 2 * h + b + 1))
         for h in range(2):
             c = 128 * h
             tt(A(cm, c, c + 64), A(S, c, c + 128, 2), A(th, 68 * h, 68 * h + 64), OP.is_gt)
             ts(A(cm, c + 64, c + 128), A(S, c + 1, c + 128, 2), A(th, 68 * h + 64, 68 * h + 65), None, OP.is_gt)
             scan(A(cs, 64 * h, 64 * h + 64), A(cm, c, c + 64), A(cm, c + 64, c + 128), OP.add, OP.add, float(c))
         for h, o in ((0, OP.add), (1, OP.subtract)):
-            ts(A(R, h, h + 1), A(cs, 64 * h + 63, 64 * h + 64), A(ca, h, h + 1), None, o)
+            ts(A(R, h, h + 1), A(cs, 64 * h + 63, 64 * h + 64), A(ca, 2 * h, 2 * h + 1), A(ca, 2 * h + 1, 2 * h + 2), o, o)
         scatter(A(n("D"), 16, 272), A(R, 0, 2), A(n("val"), 0, 32))
         tr, xb, of, lf = n("tt"), n("xb"), n("of"), n("lf")
         turn(A(tr, 64, 160), A(n("D"), 0, 96))
         turn(A(tr, 0, 64), A(n("D"), 16, 80))
-        around(tr, 0, 16, 160, ((1, 4), (2, 8), (3, 12)))
+        around(tr, 0, 16, 160, ((1, 4), (2, 8), (3, 12)), "svsvsvsvsv")
         scan(A(xb, 0, 40), A("r8", 0, 40), A(tr, 0, 160, 4), OP.mult, OP.add)
         gather("v", A(of, 0, 16), A(xb, 0, 40), A("sl", 0, 1))
         gather("s", A(lf, 0, 16), A(xb, 0, 40), A("sl", 0, 1))
+        if own == t:
+            gather_ts(A("ic", 0, 16), A(xb, 0, 40), A("sl", 0, 1), 1.0 / FZ, A("oc", 5, 6))
+            hold(A(n("slot"), 0, K), [A("ic", 0, 16)])
         pick(n("slot"), 0, K, "W", P + K * t, A(of, 0, 4))
         deal(t, True)
         deal(t, False)
@@ -502,9 +575,10 @@ def rank_program(g, core, T, topo):
             pick(n("land"), KO * rank, KO * rank + KO, "W", P + K * t, A(of, 4, 5))
         tt(A(n("fr"), 0, 4), A(lf, 0, 4), A(n("jf"), 0, 4), OP.subtract)
         if own == t:
-            ts(A(n("lc"), 0, 1), A(n("fr"), o_, o_ + 1), 1.0 / FR, A("oc", 5, 6), OP.mult, OP.add)
+            ts(A("ic", 16, 17), A("ic", 4, 5), 8, 127, OP.logical_shift_right, OP.bitwise_and)
+            cp("v", A(n("lc"), 0, 1), A("ic", 16, 17))
             gather_tt(A(n("zz"), 0, 16), A("tab", 0, 128), A(n("lc"), 0, 1), A("klc", 0, 16), OP.add)
-            tt(A(n("zo"), 0, 8), A(n("zz"), 0, 8), A(n("zz"), 8, 16), OP.add)
+            tt(A(n("zo"), 0, 8), A(n("zz"), 0, 16, 2), A(n("zz"), 1, 16, 2), OP.add)
             cp("v", A(n("oi"), 0, 8), A(n("zo"), 0, 8))
         ts(A(n("cd"), 0, 4), A(n("fr"), 0, 4), 1.0 / FR, -HALF, OP.mult, OP.add)
         if t == 0:
@@ -524,18 +598,29 @@ def rank_program(g, core, T, topo):
         dma("y", None, A(n("bk"), 0, 64, 1, 0, 1), "st_b%d" % t, 32, out_ap=T.bs[2 * t:2 * t + 1, :])
         dma("y", None, A(n("lk"), 0, 64, 1, 0, 1), "st_b%d" % t, 32, out_ap=T.bs[2 * t + 1:2 * t + 2, :])
 
+    def arrive():
+        others = [o for o in range(NO) if 2 * o != rank]
+        landed([A("Ln", 32 * o + 16, 32 * o + 20) for o in others], "ckn", len(others) * full, LAGN + (LW if own else 0.0))
+
     def rebuild(t):
         n = lambda s: s + str(t)
         c = P + K * t + a0
         for s in ("", "s"):
             landed([A(n("land") + s, KO * r, KO * r + KO) for r in range(N) if r != rank], "col%d" % t + s, 7 * (full // NO),
-                   0.9 if s else 0.6)
-        pick2(n("ord"), 64, n("land"), 256, n("oi"), 4)
+                   LD1 if s else LD0)
+        pick2(n("ord"), 64, n("land"), 256, n("oi"), 4, "sv")
         for b in range(4):
             mm(A("dec", 512 * b, 512 * b + 128), "eq", 128 * b, n("ord"), 0, 128)
+        if t:
+            hold(A("h1", 0, 512), [A("we1", 0, 64)])
         for b in range(4):
             scan(A(n("h"), b, 512, 4), A("dpat", 0, 128), A("dec", 512 * b, 512 * b + 128), OP.mult, OP.subtract)
         quant(n("new"), 0, 128, n("h"), 0)
+        if t == 0:
+            mm(A("pc", 0, 128), "ua", 0, "new0", 0, 128)
+            turn(A("Ln", 32 * o_ + 16, 32 * o_ + 48), A("pc", 3, 128, 4))
+            spread(A("Ln", 32 * o_ + 16, 32 * o_ + 20), "ckn")
+            arrive()
         pick("W", c, c + KO, n("new"), 128, A("cl", 0, 1))
         spread(A("W", c, c + KO), "new%d" % t, True)
         spread(A("Ws", c, c + KO), "new%ds" % t)
@@ -543,114 +628,139 @@ def rank_program(g, core, T, topo):
     def tables():
         c = (rank - 8) % 16
         act(A("ng", 1, 2), A("fb", 3, 4), AF.Copy, scale=-1.0)
-        act(A("Mu", 0, 272), A("nat", 0, 272), AF.Identity, bias=rank - 8.0)
+        act(A("Mn", 0, 272), A("nat", 0, 272), AF.Identity, bias=rank - 8.0)
         act(A("xa", 0, 272), A("x16", c, c + 272), AF.Abs, bias=A("ng", 1, 2))
         act(A("xm", 0, 272), A("xa", 0, 272), AF.Relu, bias=1.0, scale=-1.0)
         for h in range(0, 272, 68):
-            tt(A("M", h, h + 68), A("xm", h, h + 68), A("Mu", h, h + 68), OP.mult)
-        act(A("sd", 0, 256), A("x16", 0, 256), AF.Sign)
+            tt(A("M", h, h + 68), A("xm", h, h + 68), A("Mn", h, h + 68), OP.mult)
+        act(A("sd", 0, P), A("x16", rank, rank + P), AF.Sign)
 
-    def newlist(t):
+    def newcols(t):
         n = lambda s: s + str(t)
-        old, lo, hi, off = (A("bi1", 0, 64), 8, 264, A("oz", 0, 4)) if t else (A("bk0", 0, 64), 0, 272, A("os0", 0, 4))
+        old = A("bi1", 0, 64) if t else A("bk0", 0, 64)
         tt(A(n("wb"), 0, 64), A("nat", P + K * t, P + K * t + K), old, OP.subtract)
         tt(A(n("wc"), 0, 64), A(n("wd"), 0, 64), A(n("wb"), 0, 64), OP.mult)
         tt(A(n("we"), 0, 64), A(n("wc"), 0, 64), old, OP.add)
+
+    def entries():
+        act(A("Mu", 0, 272), A("nat", 0, 272), AF.Identity, bias=rank - 8.0)
+        scatter(A("Mu", 0, 272), A("os0", 0, 4), A("we0", 0, 64))
+        if rank:
+            cp("s", A("Mu", 264 - rank, 264), A("Mu", 8 - rank, 8))
+        gather_tt(A("vj1", 0, 32), A("Mu", 8, 264), A("zl", 0, 2), A("vz", 0, 32), OP.add)
+
+    def newlist(t):
+        n = lambda s: s + str(t)
+        lo, hi, off = (8, 264, A("oz", 0, 4)) if t else (0, 272, A("os0", 0, 4))
         gather_tt(A(n("wf"), 0, 64), A("xm", lo, hi), off, A(n("we"), 0, 64), OP.mult)
-        if t == 0:
-            scatter(A("Mu", lo, hi), off, A("we0", 0, 64))
-            if rank:
-                cp("s", A("Mu", 264 - rank, 264), A("Mu", 8 - rank, 8))
-            act(A("hz", 0, 32), A("hy", 0, 32), AF.Copy, scale=FZ)
-            tt(A("vz", 0, 32), A("hz", 0, 32), A("rf", 1, 33), OP.add)
-            ts(A("zl", 0, 1), A("jc", 0, 1), 0.0, None, OP.add)
-            ts(A("zl", 1, 2), A("jc", 0, 1), 128.0, None, OP.add)
-            gather_tt(A("vj1", 0, 32), A("Mu", 8, 264), A("zl", 0, 2), A("vz", 0, 32), OP.add)
         scatter(A("M", lo, hi), off, A(n("wf"), 0, 64))
         if t == 0:
             if rank:
                 cp("s", A("M", 264 - rank, 264), A("M", 8 - rank, 8))
             return
-        c = -rank % P
-        scan(A("mm", 0, P - c), A("sd", 0, P - c), A("M", 8 + c, 8 + P), OP.mult, OP.add)
-        if c:
-            scan(A("mm", P - c, P), A("sd", P - c, P), A("M", 8, 8 + c), OP.mult, OP.add, A("mm", P - c - 1, P - c))
-        cp("v", A("ml", 0, 16), A("mm", 15, 256, 16))
+        scan(A("mm", 0, P), A("sd", 0, P), A("M", 8, 8 + P), OP.mult, OP.add)
+        first = 1 if rank else 0
+        cp("v", A("ml", first, 16), A("mm", 15 - rank + 16 * first, P, 16))
+        if rank:
+            ts(A("ml", 0, 1), A("mm", 15 - rank, 16 - rank), A("mm", P - 1, P), None, OP.add)
 
     def places():
-        act(A("mc", 0, 1), A("fb", 5, 6), AF.Identity, bias=8192.0, scale=-256.0)
-        act(A("mc", 1, 2), A("fb", 6, 7), AF.Identity, bias=A("mc", 0, 1), scale=224.0)
-        act(A("mc", 2, 3), A("fb", 7, 8), AF.Identity, bias=A("mc", 1, 2), scale=224.0)
-        act(A("mc", 3, 4), A("mc", 2, 3), AF.Identity, bias=32.0)
-        act(A("jm", 0, 4), A("jf0", 0, 4), AF.Identity, bias=A("mc", 2, 3), scale=32.0)
-        act(A("jm", 4, 8), A("jf0", 0, 4), AF.Identity, bias=A("mc", 3, 4), scale=32.0)
-        ts(A("iw", 0, 4), A("fr0", 0, 4), 32.0 / FR, None, OP.mult)
-        ts(A("iw", 4, 8), A("iw", 0, 4), 224, None, OP.bitwise_and)
-        tt(A("iw", 8, 12), A("jm", 0, 4), A("iw", 4, 8), OP.subtract)
-        tt(A("iw", 12, 16), A("jm", 4, 8), A("iw", 4, 8), OP.subtract)
-        ts(A("wa", 0, 4), A("iw", 4, 8), 32.0, None, OP.add)
-        ts(A("iw", 16, 20), A("iw", 8, 12), 5, 31, OP.logical_shift_right, OP.bitwise_and)
-        ts(A("iw", 20, 24), A("iw", 8, 12), 1, 3584, OP.logical_shift_right, OP.bitwise_and)
-        ts(A("iw", 24, 28), A("iw", 12, 16), 224, None, OP.bitwise_and)
-        tt(A("wa", 4, 8), A("iw", 24, 28), A("iw", 4, 8), OP.not_equal)
-        tt(A("wa", 8, 12), A("iw", 16, 20), A("iw", 20, 24), OP.add)
-        tt(A("wa", 12, 16), A("wa", 0, 4), A("wa", 4, 8), OP.mult)
-        tt(A("wa", 16, 20), A("wa", 12, 16), A("wa", 8, 12), OP.add)
-        cp("v", A("wo", 0, 4), A("wa", 16, 20))
+        act(A("mc", 0, 1), A("fb", 5, 6), AF.Identity, bias=8192.0 * 128, scale=-256.0 * 128)
+        act(A("mc", 1, 2), A("fb", 6, 7), AF.Identity, bias=A("mc", 0, 1), scale=224.0 * 128)
+        act(A("mc", 2, 3), A("fb", 7, 8), AF.Identity, bias=A("mc", 1, 2), scale=224.0 * 128)
+        lf = A("lf0", 0, 4)
+        ts(A("iw", 0, 4), lf, 32.0 / FR, A("mc", 2, 3), OP.mult, OP.add)
+        ts(A("iw", 4, 8), lf, 256.0 / FR, 128.0 * 4352, OP.mult, OP.add)
+        ts(A("iw", 8, 12), lf, 512.0 / FR, None, OP.mult)
+        ts(A("iw", 12, 16), A("iw", 0, 4), 224, None, OP.bitwise_and)
+        ts(A("iw", 16, 20), A("iw", 0, 4), 7, 65504, OP.logical_shift_right, OP.bitwise_and)
+        ts(A("iw", 20, 24), A("iw", 4, 8), 7, 130816, OP.logical_shift_right, OP.bitwise_and)
+        ts(A("iw", 24, 28), A("iw", 8, 12), 3584, None, OP.bitwise_and)
+        tt(A("iw", 28, 32), A("iw", 16, 20), A("iw", 12, 16), OP.subtract)
+        tt(A("iw", 32, 36), A("iw", 20, 24), A("iw", 24, 28), OP.subtract)
+        ts(A("wa", 0, 4), A("iw", 12, 16), 32.0, None, OP.add)
+        ts(A("iw", 36, 40), A("iw", 28, 32), 5, 31, OP.logical_shift_right, OP.bitwise_and)
+        ts(A("iw", 40, 44), A("iw", 28, 32), 1, 3584, OP.logical_shift_right, OP.bitwise_and)
+        ts(A("iw", 44, 48), A("iw", 32, 36), 1792, None, OP.bitwise_and)
+        tt(A("wa", 4, 8), A("iw", 36, 40), A("iw", 40, 44), OP.add)
+        tt(A("wa", 8, 12), A("wa", 0, 4), A("iw", 44, 48), OP.min)
+        tt(A("wa", 12, 16), A("wa", 4, 8), A("wa", 8, 12), OP.add)
+        cp("v", A("wo", 0, 4), A("wa", 12, 16))
 
     def turned():
         ts(A("e1", 0, 16), A("r2", 0, 16), A("fb", 1, 2), None, OP.is_equal)
         ts(A("n1", 0, 16), A("r2", 0, 16), A("fb", 1, 2), None, OP.not_equal)
-        ts(A("gm1", 0, 16), A("rc", 0, 16), A("fb", 1, 2), BIG, OP.is_equal, OP.mult)
-        ts(A("ul", 0, 8), A("one", 0, 8), A("fb", 4, 5), 0.125, OP.mult, OP.mult)
-        pick("ua", 0, 128, "uq", 128, A("ul", 0, 8))
-        gate.append(dealt[0])
-        for c in range(2):
-            tt(A("Z", 32 + 8 * c, NB, 16), A("L1", c, 32, 2), A("n1", 0, 16), OP.mult)
+        for c in range(4):
+            tt(A("Z", 46 + c, NB, 32), A("L1", c, 32, 4), A("n1", 0, 16, 2), OP.mult)
         tt(A("pz", 0, 16), A("L1", 0, 32, 2), A("e1", 0, 16), OP.mult)
-        del gate[:]
         for h in range(2):
-            act(A("pj", 8 * h, 8 * h + 8), A("pz", h, 16, 2), AF.Copy, total=A("Z", 16 * h, 16 * h + 1))
+            act(A("pj", 8 * h, 8 * h + 8), A("pz", h, 16, 2), AF.Copy, total=A("Z", 14 + 2 * h, 15 + 2 * h))
         turn(A("Wn", 0, NB), A("Z", 0, NB))
 
-    def finish(t):
-        if t == 0:
-            places()
-            tables()
-        else:
-            quant("wq", 0, 128, "wt", 0)
-        if own == t:
-            rebuild(t)
-        if t == 0:
-            turned()
-        newlist(t)
-        lists(t)
-        if t == 0 and own:
-            owner()
-            owner_v()
-            owner_t()
+    def products(parts):
+        for h in parts:
+            if h < 2:
+                mm(A("py", 512 * h, 512 * h + 128), "wq", 0, "W", 128 * h, 128 * h + 128)
+                cp("s", A("ya", 128 * h, 128 * h + 128), A("py", 512 * h, 512 * h + 128))
+            else:
+                mm(A("pc", 512, 640), "wq", 0, "W", P + K - 128, P + K)
+                cp("s", A("ya", P, P + K), A("pc", 640 - K, 640))
+
+    def newcomers(t):
         others = [o for o in range(NO) if 2 * o + t != rank]
         c = P + K * t
         for s in ("", "s"):
             landed([A("W" + s, c + KO * o, c + KO * o + KO) for o in others], "new%d" % t + s, len(others) * full,
-                   (1.2 if s else 0.7) + (0.0 if own == t else 4.5))
+                   (LN1 if s else LN0) + (0.0 if own == t else LW + (1 - t)))
 
+    if own:
+        owner()
+        owner_v()
+        owner_t()
+    else:
+        hold(A("L0", 0, 28), [A("eq", 0, 512), A("tab", 0, 128), A("tR", 0, P)])
     judge(0, "L0")
-    dealt = [sent[-1]]
-    finish(0)
-    mm(A("pc", 0, 128), "ua", 0, "W", P + K - 128, P + K)
-    cp("v", A("cv", 0, K), A("pc", 128 - K, 128))
-    scatter(A("Wn", 0, 4096), A("wo", 0, 4), A("cv", 0, K))
+    places()
+    gate[:] = sent[-1:]
+    turned()
+    if own:
+        tables()
+        quant("wq", 0, 128, "wt", 0)
+        products((0, 1))
+    del gate[:]
+    if own == 0:
+        rebuild(0)
+    else:
+        arrive()
+    newcols(0)
+    entries()
+    lists(0)
+    if own:
+        newlist(0)
+    newcomers(0)
+    hold(A("Ln", 0, 144), [A("vj1", 0, 32), A("wo", 0, 4), A("Wn", 0, NB)])
+    turn(A("cv", 0, 128), A("Ln", 2, 130))
+    scatter(A("Wn", 0, 4096), A("wo", 0, 4), A("cv", 1, 128, 2))
     turn(A("Tn", 0, NB), A("Wn", 0, NB))
     judge(1, "Tn")
-    finish(1)
-    for h in range(2):
-        mm(A("py", 512 * h, 512 * h + 128), "wq", 0, "W", 128 * h, 128 * h + 128)
-        cp("s", A("ya", 128 * h, 128 * h + 128), A("py", 512 * h, 512 * h + 128))
-    mm(A("pc", 512, 640), "wq", 0, "W", P + K - 128, P + K)
-    cp("s", A("ya", P, P + K), A("pc", 640 - K, 640))
-    pick2("F", 128, "W", P + 2 * K, "ml", 8)
+    gate[:] = sent[-1:]
+    if own:
+        products((2,))
+    else:
+        tables()
+        newlist(0)
+        quant("wq", 0, 128, "wt", 0)
+        products((0, 1, 2))
+    del gate[:]
+    newcols(1)
+    if own:
+        rebuild(1)
+    newlist(1)
+    lists(1)
+    newcomers(1)
+    pick2("F", 128, "W", P + 2 * K, "ml", 8, "ss")
     mm(A("pc", 0, 128), "wq", 0, "W", P, P + 2 * K)
+    hold(A("ya", P + K, P + 2 * K), [A("F", 0, P)])
     cp("v", A("ya", P + K, P + 2 * K), A("pc", 128 - K, 128))
     for h, e in ((0, "v"), (1, "s")):
         gather(e, A("yb", 128 * h, 128 * h + 128), A("ya", 0, P + 2 * K), A("ml", 8 * h, 8 * h + 8))

from concourse.bass import DstId, RemoteDMATransfer
from concourse.mybir import dt, AluOpType, AxisListType, ActivationFunctionType

OP = AluOpType
AF = ActivationFunctionType
N, P, K, NO, KO = 8, 256, 64, 4, 16
BIG = 1e29
STEP = 1.0 - 2.0 ** -24
TINY = 2.0 ** -118
FR = 2.0 ** -7
FZ = 2.0 ** -15
HALF = 127.5 / 256
NB = 32 * (N + 1)
CY, HAND, LOAD, MARGIN, SLACK, EXTRA = 1.04e-3, 0.19, 0.65, 0.07, 0.4, 0.05
LU, LA, LB = 0.8, 0.95, 1.15
LC0, LC1, LD0, LD1, LAGN, LN0, LN1, LW = 2.0, 1.2, 0.6, 0.9, 1.3, 0.5, 1.2, 4.5

F4 = "float8_e4m3fn_x4"
SCRATCH = {}
VIEW = {}


def _sb(name, n, ty="float32"):
    SCRATCH[name] = ("sbuf", [128, n], ty)


def _mx(name, n):
    _sb(name, n, F4)
    _sb(name + "s", n, "uint8")


def _parts(buf, *parts):
    c = 0
    for name, n in parts:
        VIEW[name] = (buf, c)
        c += n + -n % 4
    _sb(buf, c)


for _n, _w in (("tbt", 4 * P + 4 * N), ("ut", 512), ("wt", 512), ("ee", 528), ("zt", 528)):
    _sb(_n, _w, "bfloat16")
_parts("con", ("hm", 32), ("hx", 32), ("hy", 32), ("rf", 40), ("fb", 10), ("sd32", 32),
       ("sp", 16), ("one", 32), ("frc", 32), ("oc", 8), ("klc", 16), ("ng", 4), ("eq0", 32), ("dm0", 32),
       ("gm0", 16), ("gm1", 16), ("lof", 8), ("vj0", 32), ("vj1", 32), ("pr", 64), ("l16", 64), ("t3", 64), ("t4", 64), ("t5", 64),
       ("t6", 64), ("t7", 64), ("t8", 64), ("mc", 4), ("wa", 24), ("r8", 40), ("r2", 16), ("e1", 16), ("n1", 16),
       ("pz", 16), ("pj", 16), ("sr", 32), ("sq", 32), ("vz", 32), ("hz", 32))
for _n, _w in (("nat", 512), ("x16", 288), ("xa", 272), ("xm", 272), ("md", 68), ("Mu", 272), ("Mn", 272), ("M", 272), ("mm", P),
               ("sd", 256), ("dpat", 128), ("yb", 256), ("ya", P + 2 * K), ("lt", 64), ("wt01", 64), ("tab", 128),
               ("Wn", 4096), ("Tn", NB), ("cv", 128), ("Ln", 144)):
    _sb(_n, _w)
for _n, _w in (("ib", 11), ("iw", 48), ("iz", 8), ("ic", 20)):
    _sb(_n, _w, "int32")
for _n, _w in (("cl", 2), ("lo0", 4), ("sl", 2), ("zl", 2), ("gl", 2), ("ul", 8), ("wo", 4), ("oz", 4), ("os0", 4), ("ml", 16)):
    _sb(_n, _w, "uint16")
for _n, _w in (("tR", P), ("F", P), ("uq", 128), ("ua", 128), ("wq", 128), ("eq", 512), ("W", P + 2 * K)):
    _mx(_n, _w)
for _t in "01":
    _parts("jd" + _t, ("d1" + _t, 32), ("so" + _t, 32), ("du" + _t, 64), ("lw" + _t, 32), ("px" + _t, 16), ("tl" + _t, 64),
           ("tt" + _t, 160), ("jf" + _t, 4), ("fr" + _t, 4), ("zz" + _t, 16), ("lf" + _t, 16),
           ("zo" + _t, 8), ("wb" + _t, 64), ("wc" + _t, 64), ("wd" + _t, 64), ("we" + _t, 64),
           ("wf" + _t, 64), ("th" + _t, 136), ("cm" + _t, 256), ("cs" + _t, 128), ("ca" + _t, 4), ("ls" + _t, 2), ("rl" + _t, 256),
           ("cj" + _t, 256), ("lj" + _t, 16), ("bi" + _t, 64))
    for _n, _w in (("L", 32), ("S", 256), ("Lz", 64), ("val", 32), ("D", 272), ("xb", 40), ("bk", 64), ("lk", 64)):
        _sb(_n + _t, _w)
    for _n, _w in (("R", 2), ("of", 16), ("cd", 4), ("lc", 2), ("oi", 8)):
        _sb(_n + _t, _w, "uint16")
    _sb("h" + _t, 512, "bfloat16")
    for _n, _w in (("slot", K), ("land", 256), ("ord", 128), ("new", 128)):
        _mx(_n + _t, _w)
VIEW["Z"] = VIEW["rl0"]
SCRATCH["pc"] = ("psum", [128, 1024], "float32")
SCRATCH["dec"] = ("psum", [128, 2048], "float32")
SCRATCH["py"] = ("psum", [128, 1024], "float32")
PSUM = ("pc", "dec", "py")

SEMAPHORES = ["qv", "qs", "qt", "qg", "out", "ld_u", "ld_a", "ld_b", "ld_w", "st_c", "st_s", "st_y", "st_b0", "st_b1",
              "ck0", "ck1", "ckn", "col0", "col0s", "col1", "col1s", "new0", "new0s", "new1", "new1s"]


def rank_program(g, core, T, topo):
    rank = T.rank_of(core)
    if rank is None:
        return
    eng = {"v": g.vector, "s": g.scalar, "t": g.tensor, "g": g, "y": g.sync}
    count = {"v": 0, "s": 0, "t": 0, "g": 0}
    seen = {e: {} for e in eng}
    wrote, read = {}, {}
    final = {}

    def A(name, c0, c1, st=1, p0=0, p1=128):
        if name in VIEW:
            name, c = VIEW[name]
            c0, c1 = c0 + c, c1 + c
        ap = T[name][p0:p1, c0:c1] if st == 1 else T[name][p0:p1, c0:c1:st]
        cols = frozenset(c // 512 for c in range(c0, c1, st)) if name in PSUM else frozenset(range(c0, c1, st))
        return (name, p0, p1, cols, ap, len(range(c0, c1, st)))

    def hits(table, r):
        for (p0, p1, cols, tok) in table.get(r[0], ()):
            if p0 < r[2] and r[1] < p1 and not cols.isdisjoint(r[3]):
                yield tok

    def wait(e, sem, val):
        if seen[e].get(sem, 0) < val:
            eng[e].wait_ge(T.sem[sem], val)
            seen[e][sem] = val

    def order(e, ins, outs):
        need = {}
        for rs, table, same in ((ins, wrote, True), (outs, wrote, True), (outs, read, False)):
            for r in rs:
                for sem, val, src in hits(table, r):
                    if src != e or (same and r[0] not in PSUM) or rs is ins:
                        need[sem] = max(need.get(sem, 0), val)
        for sem, val in need.items():
            wait(e, sem, val)

    def note(ins, outs, tok):
        for r in ins:
            read.setdefault(r[0], []).append((r[1], r[2], r[3], tok))
        for r in outs:
            wrote.setdefault(r[0], []).append((r[1], r[2], r[3], tok))

    jobs, jw, jr, sent, gate, chain, holds = [], {}, {}, [], [], [], set()

    def job(e, outs, ins, run, cost, lag, after=()):
        need = set(after) | set(gate)
        for rs, table in ((ins, jw), (outs, jw), (outs, jr)):
            for r in rs:
                need.update(hits(table, r))
        k = len(jobs)
        jobs.append((e, run, cost, lag, need))
        for rs, table in ((ins, jr), (outs, jw)):
            for r in rs:
                table.setdefault(r[0], []).append((r[1], r[2], r[3], k))
        return k

    def op(e, outs, ins, call, cost=None, lag=HAND):
        def run():
            order(e, ins, outs)
            inst = call()
            count[e] += 1
            inst.then_inc(T.sem["q" + e], 1)
            final["q" + e] = count[e]
            note(ins, outs, ("q" + e, count[e], e))
        job(e, outs, ins, run, max(64, max(r[5] for r in outs[:1] + ins[:1])) * CY if cost is None else cost, lag)

    def dma(e, out, in_, sem, total, out_ap=None, in_ap=None, behind=None, lag=LOAD):
        ins, outs = [in_] if in_ else [], [out] if out else []

        def run():
            order(e, ins + ([behind] if behind else []), outs)
            o = out_ap if out_ap is not None else out[4]
            i = in_ap if in_ap is not None else in_[4]
            eng[e].dma_start(o, i).then_inc(T.sem[sem], 16)
            final[sem] = total
            note(ins, outs, (sem, total, "dma"))
        job(e, outs, ins + ([behind] if behind else []), run, 0.1, lag)

    def hold(ref, before):
        holds.add(job(None, [ref], list(before), lambda: None, 0.0, 0.0))

    def emit():
        tail = [0.0] * len(jobs)
        for k in range(len(jobs) - 1, -1, -1):
            tail[k] += jobs[k][2] + jobs[k][3]
            for d in jobs[k][4]:
                tail[d] = max(tail[d], tail[k] - (jobs[d][3] if k in holds and jobs[d][0] else 0.0))
        busy, start, soon = {}, {}, []

        def done(k, d):
            return jobs[d][2] + (0.0 if k in holds and jobs[d][0] else jobs[d][3])

        for k in range(len(jobs)):
            soon.append(max([soon[d] + done(k, d) for d in jobs[k][4]], default=0.0))
        whole = max(a + b for a, b in zip(soon, tail))
        for k in sorted(range(len(jobs)), key=lambda k: (-tail[k], k)):
            e, run, cost, lag, need = jobs[k]
            side = soon[k] + tail[k] < whole - SLACK
            t = max([start[d] + done(k, d) + (EXTRA if side and jobs[d][0] else 0.0) for d in need], default=0.0)
            if e:
                for a, b, hot in sorted(busy.setdefault(e, [])):
                    if t + cost + (MARGIN if hot and side else 0.0) <= a + 1e-9:
                        break
                    t = max(t, b)
                busy[e].append((t, t + cost, not side))
            start[k] = t
        for k in sorted(start, key=lambda k: (start[k], k)):
            jobs[k][1]()

    def tt(out, a, b, o):
        op("v", [out], [a, b], lambda: g.vector.tensor_tensor(out[4], a[4], b[4], o), max(64, 2 * out[5]) * CY)

    def ts(out, a, s1, s2, o0, o1=None):
        ins = [a] + [s for s in (s1, s2) if isinstance(s, tuple)]
        v1 = s1[4] if isinstance(s1, tuple) else s1
        v2 = s2[4] if isinstance(s2, tuple) else s2
        if o1 is None:
            op("v", [out], ins, lambda: g.vector.tensor_scalar(out[4], a[4], v1, None, o0))
        else:
            op("v", [out], ins, lambda: g.vector.tensor_scalar(out[4], a[4], v1, v2, o0, o1))

    def act(out, a, f, bias=None, scale=None, total=None):
        ins = [a] + [s for s in (bias, scale) if isinstance(s, tuple)]
        kw = {}
        if bias is not None:
            kw["bias"] = bias[4] if isinstance(bias, tuple) else bias
        if scale is not None:
            kw["scale"] = scale[4] if isinstance(scale, tuple) else scale
        if total is not None:
            kw["accum_out"] = total[4]
        op("s", [out] if total is None else [out, total], ins, lambda: g.scalar.activation(out[4], a[4], f, **kw))

    def cp(e, out, a):
        if e == "v":
            op("v", [out], [a], lambda: g.vector.tensor_copy(out[4], a[4]))
        else:
            act(out, a, AF.Copy)

    def fill(out, x):
        op("v", [out], [], lambda: g.vector.memset(out[4], x), max(64, out[5] // 2) * CY)

    def const(out, x, like):
        act(out, like, AF.Identity, bias=x, scale=0.0)

    def scan(out, d0, d1, o0, o1, first=0.0):
        col = isinstance(first, tuple)
        op("v", [out], [d0, d1] + ([first] if col else []),
           lambda: g.vector.tensor_tensor_scan(out[4], d0[4], d1[4], first[4] if col else first, o0, o1))

    def turn(out, a):
        op("v", [out], [a], lambda: g.vector.transpose(out[4], a[4]))

    def own_call(out, ins, call, cost):
        gate.extend(chain)
        op("g", [out], ins, call, cost, 0.0)
        chain[:] = [len(jobs) - 1]
        del gate[:]

    def iota(out, pat, base, cm, flag=True):
        kw = {"allow_small_or_imprecise_dtypes": True} if flag else {}
        own_call(out, [], lambda: g.iota(out[4], pat, base, cm, **kw), 0.16 + 2 * CY * out[5])

    def spot(out, a, base):
        own_call(out, [a], lambda: g.affine_select(out[4], a[4], [[1, out[5]]], OP.not_equal, 1.0, base, -4), 0.21 + 2 * CY * out[5])

    def by(out):
        return 0.07 + 1.5 * CY * out[5]

    def gather(e, out, win, off, f=AF.Copy):
        if e == "v":
            op("v", [out], [win, off], lambda: g.vector.tensor_copy(out[4], win[4].indirect(off[4])), by(out))
        else:
            op("s", [out], [win, off], lambda: g.scalar.activation(out[4], win[4].indirect(off[4]), f), by(out))

    def gather_tt(out, win, off, b, o):
        op("v", [out], [win, off, b], lambda: g.vector.tensor_tensor(out[4], win[4].indirect(off[4]), b[4], o), by(out))

    def gather_ts(out, win, off, x, b):
        op("v", [out], [win, off, b], lambda: g.vector.tensor_scalar(out[4], win[4].indirect(off[4]), x, b[4], OP.mult, OP.add), by(out))

    def scatter(win, off, val):
        op("v", [win], [val, off], lambda: g.vector.tensor_copy(win[4].indirect(off[4]), val[4]), 0.06 + 3.5 * CY * val[5])

    def pickc(dst, c0, c1, src, n, off):
        o, i = A(dst, c0, c1), A(src, 0, n)
        op("v", [o], [i, off], lambda: g.vector.tensor_copy(o[4].bitcast(dt.uint32), i[4].bitcast(dt.uint32).indirect(off[4])),
           by(o))

    def picks(e, dst, c0, c1, src, n, off):
        gather(e, A(dst + "s", c0, c1), A(src + "s", 0, n), off)

    def pick(dst, c0, c1, src, n, off):
        pickc(dst, c0, c1, src, n, off)
        picks("s", dst, c0, c1, src, n, off)

    def pick2(dst, n1, src, n, off, k, who):
        for h in range(2):
            pickc(dst, n1 * h, n1 * h + n1, src, n, A(off, k * h, k * h + k))
        for h, e in enumerate(who):
            picks(e, dst, n1 * h, n1 * h + n1, src, n, A(off, k * h, k * h + k))

    def quant(dst, c0, c1, tile, at):
        o, s, i = A(dst, c0, c1), A(dst + "s", c0, c1), A(tile, at, at + 4 * (c1 - c0))
        op("v", [o, s], [i], lambda: g.vector.quantize_mx(o[4], s[4], i[4]), 0.015 + 0.27 * CY * i[5])

    def mm(out, lhs, a, rhs, b0, b1):
        l, ls, r, rs = A(lhs, a, a + 128), A(lhs + "s", a, a + 128), A(rhs, b0, b1), A(rhs + "s", b0, b1)
        op("t", [out], [l, ls, r, rs], lambda: g.tensor.matmul_mx(out[4], l[4], ls[4], r[4], rs[4], True, True), 144 * 1.5 * CY)

    def around(buf, src, step, end, places, who, unturned=None):
        k = 0
        for x, c in places:
            for a in ((0, 2) if x == 2 else range(4)):
                w = 64 if x == 2 else 32
                b = a ^ x
                o = A(buf, c, end, step, 32 * a, 32 * a + w)
                if who[k] == "t":
                    turn(o, A(unturned, 0, 64, 1, 32 * b, 32 * b + w))
                else:
                    cp(who[k], o, A(buf, src, end, step, 32 * b, 32 * b + w))
                k += 1

    peers = [c for c in T.cores if c != core]

    def dest(c):
        rid, pid, _s = topo.addr(c)
        return DstId(rid=rid, pnc=pid)

    def raw(r, codes):
        return r[4].bitcast(dt.uint8) if codes else r[4]

    def spread(ref, sem, codes=False, behind=()):
        def run():
            order("g", [ref] + list(behind), [])
            m = topo.mask(core, peers[0])
            for c in peers:
                m &= topo.mask(core, c)
            g.remote_dma_fused([RemoteDMATransfer(dst_ids=[dest(c) for c in peers], dma_engine_mask=m, remote_sem=T.sem[sem],
                                                  srcs=[raw(ref, codes)], dsts=[raw(ref, codes) for _ in peers])],
                               local_sem=T.sem["out"])
            final["out"] = final.get("out", 0) + bin(m).count("1")
        sent.append(job("g", [], [ref] + list(behind), run, 0.5, 0.0, sent[-1:]))

    full = len(topo.engines(core, peers[0]))

    def landed(refs, sem, total, lag):
        def run():
            note([], refs, (sem, total, "remote"))
            final[sem] = total
        job(None, refs, [], run, 0.0, lag, sent[-1:])

    def checks(parts):
        srcs = [A("L0", 28 + 2 * h, 30 + 2 * h) for h in sorted({p[0] for p in parts})]

        def run():
            order("g", srcs, [])
            tr = []
            for h, a, b, e0, e1 in parts:
                to = [(rank + k) % N for k in range(a, b)]
                es = topo.engines(core, T.cores[to[0]])[e0 * full // 4:e1 * full // 4]
                at = [14 * h + 2 * (rank - (rank > r)) for r in to]
                tr.append(RemoteDMATransfer(dst_ids=[dest(T.cores[r]) for r in to], dma_engine_mask=sum(1 << e for e in es),
                                            remote_sem=T.sem["ck0"], srcs=[A("L0", 28 + 2 * h, 30 + 2 * h)[4]],
                                            dsts=[A("L0", x, x + 2)[4] for x in at]))
                final["out"] = final.get("out", 0) + len(es)
            g.remote_dma_fused(tr, local_sem=T.sem["out"])
        sent.append(job("g", [], srcs, run, 0.5, 0.0, sent[-1:] + chain))

    def deal(t, codes):
        s = "" if codes else "s"

        def run():
            tr = []
            for o in range(NO):
                c = T.cores[2 * o + t]
                if c == core:
                    continue
                es = topo.engines(core, c)
                w = len(es) // NO
                src = A("slot%d" % t + s, KO * o, KO * o + KO)
                order("g", [src], [])
                d = A("land%d" % t + s, KO * rank, KO * rank + KO)
                tr.append(RemoteDMATransfer(dst_ids=[dest(c)], dma_engine_mask=sum(1 << e for e in es[w * o:w * o + w]),
                                            remote_sem=T.sem["col%d" % t + s], srcs=[raw(src, codes)], dsts=[raw(d, codes)]))
                final["out"] = final.get("out", 0) + w
            g.remote_dma_fused(tr, local_sem=T.sem["out"])
        sent.append(job("g", [], [A("slot%d" % t + s, 0, K)], run, 0.4, 0.0, sent[-1:]))

    own = rank % 2
    o_ = rank // 2
    a0 = KO * o_

    dma("y", A("tbt", 0, 512), None, "ld_a", 16, in_ap=T.tb[:, 0:512], lag=LA)
    dma("s", A("ut", 0, 8), None, "ld_u", 16, in_ap=T.u[:, 0:8], lag=LU)
    dma("s", A("tbt", 512, 1024), None, "ld_b", 16, in_ap=T.tb[:, 512:1024], lag=LB)
    dma("y", A("wt", 0, 512), None, "ld_w", 16, in_ap=T.w[:], behind=A("tbt", 512, 1024))

    iota(A("ib", 9, 11), [[1, 2]], 0, 1, False)
    iota(A("lt", 0, 64), [[0, 8], [1, 8]], 0, 0)
    iota(A("nat", 0, 128), [[1, 128]], 0, 0)
    iota(A("pr", 0, 64), [[16, 8], [0, 8]], 0, 0)

    def ones(h):
        fill(A("zt", h, h + 264), 0.0)
        spot(A("ee", h, h + 264), A("zt", h, h + 264), h - 4)

    fill(A("ut", 8, 512), 0.0)
    if own == 0:
        ones(0)
    fill(A("one", 0, 32), 1.0)
    fill(A("frc", 0, 32), FR)
    ts(A("ib", 0, 2), A("ib", 9, 11), 7, None, OP.bitwise_and)
    for col, bits in enumerate((31, 15, 8, 112, 64, 32, 1)):
        ts(A("ib", col + 2, col + 3), A("ib", 9, 10), bits, None, OP.bitwise_and)
    cp("v", A("fb", 0, 10), A("ib", 0, 10))

    ts(A("eq0", 0, 32), A("lt", 0, 32), A("fb", 0, 1), -1.0, OP.is_equal, OP.mult)
    ts(A("gm0", 0, 16), A("lt", 0, 16), A("fb", 0, 1), BIG, OP.is_equal, OP.mult)
    const(A("hm", 0, 32), 0.0, A("lt", 0, 32))
    for h in (8, 24):
        const(A("hm", h, h + 8), 1.0, A("lt", 0, 8))
    tt(A("dm0", 0, 32), A("eq0", 0, 32), A("hm", 0, 32), OP.add)
    ts(A("gm1", 0, 2), A("fb", 0, 2), 0.0, -FR, OP.is_equal, OP.mult)
    hold(A("uq", 0, 128), [A("ib", 0, 9)])
    quant("uq", 0, 128, "ut", 0)
    act(A("nat", 128, 256), A("nat", 0, 128), AF.Identity, bias=128.0)
    const(A("Ln", 0, 144), 0.0, A("nat", 0, 144))
    act(A("nat", 256, 512), A("nat", 0, 256), AF.Identity, bias=256.0)

    for h in range(2):
        quant("W", 128 * h, 128 * h + 128, "tbt", 512 * h)
        mm(A("pc", 512 * h, 512 * h + 128), "W", 128 * h, "uq", 0, 128)
        cp("v", A("L0", 28 + 2 * h, 30 + 2 * h), A("pc", 512 * h, 512 * h + 2))
    checks([(0, 1, 4, 0, 1)])
    checks([(0, 4, N, 1, 2), (1, 1, N, 2, 4)])
    landed([A("L0", 0, 28)], "ck0", 7 * 3 * full // 4, LC0)
    chain[:] = sent[-1:]

    if own == 0:
        ones(264)
    iota(A("hx", 0, 32), [[128, 2], [1, 16]], 0, 0)
    iota(A("sr", 0, 16), [[0, 4], [8, 2], [24, 2]], 7, 0)
    iota(A("sr", 16, 32), [[0, 4], [8, 2], [-16, 2]], 23, 0)
    iota(A("D0", 0, 96), [[0, 96]], 0, 0)
    iota(A("x16", 0, 288), [[0, 18], [1, 16]], 0, 0)
    iota(A("r2", 0, 16), [[1, 8], [0, 2]], 0, 0)
    if own:
        ones(0)
        ones(264)
    iota(A("D1", 0, 96), [[0, 96]], 0, 0)
    const(A("sr", 4, 5), 7.0 + 8 * (o_ >> 1) + 24 * (o_ & 1), A("one", 0, 1))
    const(A("sr", 20, 21), 23.0 + 8 * (o_ >> 1) - 16 * (o_ & 1), A("one", 0, 1))
    turn(A("sq", 0, 32), A("sr", 0, 32))
    cp("v", A("sl", 0, 2), A("sq", 0, 2))
    act(A("lof", 0, 1), A("fb", 0, 1), AF.Sign, bias=-float(rank))
    act(A("lof", 1, 2), A("lof", 0, 1), AF.Relu, scale=2.0)
    act(A("lof", 2, 3), A("lof", 0, 1), AF.Abs)
    act(A("lof", 3, 4), A("fb", 0, 1), AF.Identity, bias=28.0 - 2 * rank, scale=2.0)
    act(A("lof", 4, 5), A("lof", 2, 3), AF.Identity, bias=A("lof", 3, 4), scale=2.0 * rank - 28)
    act(A("lof", 5, 6), A("lof", 2, 3), AF.Identity, bias=2.0, scale=12.0)
    act(A("lof", 6, 7), A("lof", 2, 3), AF.Identity, bias=0.25, scale=1.5)
    act(A("lof", 7, 8), A("fb", 4, 5), AF.Identity, bias=1.0, scale=A("lof", 6, 7))
    ts(A("lo0", 0, 1), A("lof", 4, 5), A("lof", 1, 2), None, OP.subtract)
    ts(A("lo0", 1, 2), A("lof", 4, 5), A("lof", 1, 2), A("lof", 5, 6), OP.subtract, OP.add)
    ts(A("lo0", 2, 3), A("lof", 4, 5), A("lof", 1, 2), A("lof", 7, 8), OP.subtract, OP.add)
    if rank:
        cp("s", A("tbt", 4 * P, 4 * P + 4 * N), A("tbt", 0, 4 * N))
        for h in range(2):
            quant("tR", 128 * h, 128 * h + 128, "tbt", 4 * rank + 512 * h)
    for h in range(2):
        mm(A("py", 512 * h, 512 * h + 128), "tR" if rank else "W", 128 * h, "uq", 0, 128)
    cp("s", A("sd32", 0, 32), A("one", 0, 32))
    const(A("sd32", 0, 32, 16), 0.0, A("nat", 0, 2))
    const(A("r8", 0, 40), 1.0, A("nat", 0, 40))
    const(A("r8", 0, 40, 8), 0.0, A("nat", 0, 5))
    const(A("sp", 0, 16), 0.0, A("nat", 0, 16))
    const(A("sp", 0, 16, 8), -BIG, A("nat", 0, 2))
    act(A("rf", 0, 40), A("lt", 0, 40), AF.Copy, scale=8.0 * FR)
    const(A("rf", 0, 40, 8), FR, A("nat", 0, 5))
    for h in range(2):
        cp("s", A("L1", 4 * rank + 2 * h, 4 * rank + 2 * h + 2), A("py", 512 * h, 512 * h + 2))
    spread(A("L1", 4 * rank, 4 * rank + 4), "ck1", False, [A("Ln", 0, 144)])
    landed([A("L1", 4 * r, 4 * r + 4) for r in range(N) if r != rank], "ck1", 7 * full, LC1)

    def owner():
        act(A("oc", 0, 1), A("fb", 0, 1), AF.Identity, bias=-16.0, scale=16.0)
        act(A("oc", 1, 2), A("fb", 0, 1), AF.Relu, bias=-16.0, scale=16.0)
        act(A("oc", 2, 3), A("fb", 0, 1), AF.Relu, bias=1.0, scale=-1.0)
        act(A("oc", 3, 4), A("fb", 4, 5), AF.Copy, scale=0.125)
        act(A("oc", 4, 5), A("fb", 4, 5), AF.Identity, bias=1.0, scale=-0.125)
        act(A("oc", 5, 6), A("fb", 8, 9), AF.Copy, scale=64.0 * FR / FZ)
        act(A("klc", 0, 16, 2), A("nat", 0, 16, 2), AF.Copy, scale=A("oc", 4, 5))
        act(A("klc", 1, 16, 2), A("nat", 1, 16, 2), AF.Copy, scale=A("oc", 3, 4))
        act(A("l16", 0, 64), A("lt", 0, 64), AF.Copy, scale=16.0)
        act(A("t4", 0, 64), A("pr", 0, 64), AF.Identity, bias=A("oc", 1, 2), scale=A("oc", 2, 3))
        const(A("dpat", 0, 128), 1.0, A("nat", 0, 128))
        const(A("dpat", 0, 128, 8), 0.0, A("nat", 0, 16))
        const(A("dpat", 1, 128, 8), -1.0, A("nat", 0, 16))

    def owner_v():
        quant("land%d" % own, 128, 256, "zt", 0)
        for b in range(4):
            quant("eq", 128 * b, 128 * b + 128, "ee", 4 - b)
        ts(A("cl", 0, 1), A("fb", 3, 4), 8.0, 7.0, OP.mult, OP.add)

    def owner_t():
        ts(A("t3", 0, 64), A("pr", 0, 64), A("oc", 0, 1), 16.0, OP.is_le, OP.mult)
        tt(A("t5", 0, 64), A("t3", 0, 64), A("t4", 0, 64), OP.add)
        tt(A("t6", 0, 64), A("t5", 0, 64), A("l16", 0, 64), OP.is_equal)
        act(A("t7", 0, 64), A("t6", 0, 64), AF.Copy, scale=128.0)
        tt(A("t8", 0, 64), A("t5", 0, 64), A("t7", 0, 64), OP.add)
        act(A("tab", 0, 64), A("t8", 0, 64), AF.Copy, scale=A("oc", 4, 5))
        act(A("tab", 64, 128), A("t8", 0, 64), AF.Copy, scale=A("oc", 3, 4))

    ts(A("gl", 0, 2), A("nat", 0, 33, 32), A("fb", 2, 3), None, OP.add)
    if own == 0:
        owner()
        owner_v()
        ts(A("ul", 0, 8), A("one", 0, 8), A("fb", 8, 9), None, OP.mult)
        pick("ua", 0, 128, "uq", 128, A("ul", 0, 8))
    ts(A("md", 0, 64, 2), A("nat", 0, 32), A("fb", 2, 3), STEP, OP.is_ge, OP.max)
    act(A("md", 65, 66), A("fb", 7, 8), AF.Identity, bias=1.0, scale=(STEP - 1.0) / 32)
    act(A("md", 64, 65), A("fb", 6, 7), AF.Identity, bias=1.0, scale=(STEP - 1.0) / 64)
    act(A("md", 1, 64, 2), A("one", 0, 32), AF.Copy, scale=A("md", 65, 66))
    ts(A("hy", 0, 32), A("hx", 0, 32), A("fb", 5, 6), None, OP.add)
    tt(A("vj0", 0, 32), A("hy", 0, 32), A("rf", 0, 32), OP.add)
    act(A("hz", 0, 32), A("hy", 0, 32), AF.Copy, scale=FZ)
    tt(A("vz", 0, 32), A("hz", 0, 32), A("rf", 1, 33), OP.add)
    ts(A("zl", 0, 2), A("hx", 0, 32, 16), A("fb", 9, 10), None, OP.add)
    if own == 0:
        owner_t()
    ts(A("wt01", 0, 64), A("lt", 0, 64), float(rank), None, OP.is_equal)

    def judge(t, i):
        n = lambda s: s + str(t)
        d1, so, du, S, lw, px, tl = n("d1"), n("so"), n("du"), n("S"), n("lw"), n("px"), n("tl")
        th, cm, cs, cj, rl, ca, ls, R = n("th"), n("cm"), n("cs"), n("cj"), n("rl"), n("ca"), n("ls"), n("R")
        if t == 0:
            gather_tt(A(d1, 0, 32), A(i, 0, 32), A("lo0", 0, 2), A("dm0", 0, 32), OP.mult)
            gather("s", A(lw, 0, 16), A(i, 0, 32), A("lo0", 2, 3), AF.Abs)
            scan(A(so, 0, 32), A("sd32", 0, 32), A(d1, 0, 32), OP.mult, OP.subtract)
        else:
            for h in range(2):
                scan(A(so, 16 * h + 8, 16 * h + 16), A("one", 0, 8), A(i, 46 + 2 * h, NB, 32), OP.mult, OP.subtract,
                     A(i, 14 + 2 * h, 15 + 2 * h))
                act(A(lw, 16 + 8 * h, 24 + 8 * h), A(i, 47 + 2 * h, NB, 32), AF.Abs)
        for h in range(2):
            act(A(du, 32 * h, 32 * h + 32), A("one", 0, 32), AF.Abs, bias=TINY, scale=A(so, 16 * h + 15, 16 * h + 16))
        if t == 0:
            tt(A(lw, 16, 32), A(lw, 0, 16), A(n("gm"), 0, 16), OP.subtract)
        scan(A(px, 0, 16), A("sp", 0, 16), A(lw, 16, 32), OP.add, OP.max)
        turn(A(S, 0, 256, 4), A(du, 0, 64))
        for h in range(2):
            act(A(th, 68 * h, 68 * h + 65), A("md", 0, 65), AF.Copy, scale=A(du, 32 * h, 32 * h + 1))
        around(S, 0, 4, 256, ((1, 2), (2, 1), (3, 3)), "tttttttsss", du)
        for h in range(2):
            act(A(n("lj"), 8 * h, 8 * h + 8), A(px, 8 * h, 8 * h + 8), AF.Sign, bias=A(px, 8 * h + 7, 8 * h + 8), scale=-1.0,
                total=A(ls, h, h + 1))
        for h in range(2):
            act(A(tl, 32 * h, 32 * h + 32), A("frc", 0, 32), AF.Relu, bias=A("gm1", t, t + 1), scale=A(ls, h, h + 1))
        turn(A(n("Lz"), 0, 64), A(tl, 0, 64))
        gather_tt(A(n("val"), 0, 32), A(n("Lz"), 0, 64), A("gl", 0, 2), A("vj%d" % t, 0, 32), OP.add)
        for b in range(2):
            for h in range(2):
                act(A(rl, 128 * h + 64 * b, 128 * h + 64 * b + 64), A(S, 128 - 128 * h + b, 256 - 128 * h, 2), AF.Sign,
                    bias=A(du, 32 * h, 32 * h + 1), scale=-1.0)
        for b in range(2):
            for h in range(2):
                c = 128 * h + 64 * b
                act(A(cj, c, c + 64), A(rl, c, c + 64), AF.Relu, scale=2.0 * h - 1.0, total=A(ca, 2 * h + b, 2 * h + b + 1))
        for h in range(2):
            c = 128 * h
            tt(A(cm, c, c + 64), A(S, c, c + 128, 2), A(th, 68 * h, 68 * h + 64), OP.is_gt)
            ts(A(cm, c + 64, c + 128), A(S, c + 1, c + 128, 2), A(th, 68 * h + 64, 68 * h + 65), None, OP.is_gt)
            scan(A(cs, 64 * h, 64 * h + 64), A(cm, c, c + 64), A(cm, c + 64, c + 128), OP.add, OP.add, float(c))
        for h, o in ((0, OP.add), (1, OP.subtract)):
            ts(A(R, h, h + 1), A(cs, 64 * h + 63, 64 * h + 64), A(ca, 2 * h, 2 * h + 1), A(ca, 2 * h + 1, 2 * h + 2), o, o)
        scatter(A(n("D"), 16, 272), A(R, 0, 2), A(n("val"), 0, 32))
        tr, xb, of, lf = n("tt"), n("xb"), n("of"), n("lf")
        turn(A(tr, 64, 160), A(n("D"), 0, 96))
        turn(A(tr, 0, 64), A(n("D"), 16, 80))
        around(tr, 0, 16, 160, ((1, 4), (2, 8), (3, 12)), "svsvsvsvsv")
        scan(A(xb, 0, 40), A("r8", 0, 40), A(tr, 0, 160, 4), OP.mult, OP.add)
        gather("v", A(of, 0, 16), A(xb, 0, 40), A("sl", 0, 1))
        gather("s", A(lf, 0, 16), A(xb, 0, 40), A("sl", 0, 1))
        if own == t:
            gather_ts(A("ic", 0, 16), A(xb, 0, 40), A("sl", 0, 1), 1.0 / FZ, A("oc", 5, 6))
            hold(A(n("slot"), 0, K), [A("ic", 0, 16)])
        pick(n("slot"), 0, K, "W", P + K * t, A(of, 0, 4))
        deal(t, True)
        deal(t, False)
        cp("v", A(n("jf"), 0, 4), A(of, 0, 4))
        if own == t:
            pick(n("land"), KO * rank, KO * rank + KO, "W", P + K * t, A(of, 4, 5))
        tt(A(n("fr"), 0, 4), A(lf, 0, 4), A(n("jf"), 0, 4), OP.subtract)
        if own == t:
            ts(A("ic", 16, 17), A("ic", 4, 5), 8, 127, OP.logical_shift_right, OP.bitwise_and)
            cp("v", A(n("lc"), 0, 1), A("ic", 16, 17))
            gather_tt(A(n("zz"), 0, 16), A("tab", 0, 128), A(n("lc"), 0, 1), A("klc", 0, 16), OP.add)
            tt(A(n("zo"), 0, 8), A(n("zz"), 0, 16, 2), A(n("zz"), 1, 16, 2), OP.add)
            cp("v", A(n("oi"), 0, 8), A(n("zo"), 0, 8))
        ts(A(n("cd"), 0, 4), A(n("fr"), 0, 4), 1.0 / FR, -HALF, OP.mult, OP.add)
        if t == 0:
            ts(A("os0", 0, 4), A("jf0", 0, 4), 8.0 - rank, None, OP.add)
            gather("s", A("bk0", 0, 64), A("nat", 0, P), A(of, 0, 4))
        else:
            ts(A("iz", 0, 4), A("fr1", 0, 4), 1.0 / FZ, None, OP.mult)
            ts(A("iz", 4, 8), A("iz", 0, 4), 255, None, OP.bitwise_and)
            cp("v", A("oz", 0, 4), A("iz", 4, 8))
            gather("s", A("bk1", 0, 64), A("nat", 0, P), A("oz", 0, 4))
            gather("s", A("bi1", 0, 64), A("nat", 0, P + K), A(of, 0, 4))
        gather("s", A(n("wd"), 0, 64), A("wt01", 0, 64), A(n("cd"), 0, 4))

    def lists(t):
        n = lambda s: s + str(t)
        gather("s", A(n("lk"), 0, 64), A("lt", 0, 64), A(n("cd"), 0, 4))
        dma("y", None, A(n("bk"), 0, 64, 1, 0, 1), "st_b%d" % t, 32, out_ap=T.bs[2 * t:2 * t + 1, :])
        dma("y", None, A(n("lk"), 0, 64, 1, 0, 1), "st_b%d" % t, 32, out_ap=T.bs[2 * t + 1:2 * t + 2, :])

    def arrive():
        others = [o for o in range(NO) if 2 * o != rank]
        landed([A("Ln", 32 * o + 16, 32 * o + 20) for o in others], "ckn", len(others) * full, LAGN + (LW if own else 0.0))

    def rebuild(t):
        n = lambda s: s + str(t)
        c = P + K * t + a0
        for s in ("", "s"):
            landed([A(n("land") + s, KO * r, KO * r + KO) for r in range(N) if r != rank], "col%d" % t + s, 7 * (full // NO),
                   LD1 if s else LD0)
        pick2(n("ord"), 64, n("land"), 256, n("oi"), 4, "sv")
        for b in range(4):
            mm(A("dec", 512 * b, 512 * b + 128), "eq", 128 * b, n("ord"), 0, 128)
        if t:
            hold(A("h1", 0, 512), [A("we1", 0, 64)])
        for b in range(4):
            scan(A(n("h"), b, 512, 4), A("dpat", 0, 128), A("dec", 512 * b, 512 * b + 128), OP.mult, OP.subtract)
        quant(n("new"), 0, 128, n("h"), 0)
        if t == 0:
            mm(A("pc", 0, 128), "ua", 0, "new0", 0, 128)
            turn(A("Ln", 32 * o_ + 16, 32 * o_ + 48), A("pc", 3, 128, 4))
            spread(A("Ln", 32 * o_ + 16, 32 * o_ + 20), "ckn")
            arrive()
        pick("W", c, c + KO, n("new"), 128, A("cl", 0, 1))
        spread(A("W", c, c + KO), "new%d" % t, True)
        spread(A("Ws", c, c + KO), "new%ds" % t)

    def tables():
        c = (rank - 8) % 16
        act(A("ng", 1, 2), A("fb", 3, 4), AF.Copy, scale=-1.0)
        act(A("Mn", 0, 272), A("nat", 0, 272), AF.Identity, bias=rank - 8.0)
        act(A("xa", 0, 272), A("x16", c, c + 272), AF.Abs, bias=A("ng", 1, 2))
        act(A("xm", 0, 272), A("xa", 0, 272), AF.Relu, bias=1.0, scale=-1.0)
        for h in range(0, 272, 68):
            tt(A("M", h, h + 68), A("xm", h, h + 68), A("Mn", h, h + 68), OP.mult)
        act(A("sd", 0, P), A("x16", rank, rank + P), AF.Sign)

    def newcols(t):
        n = lambda s: s + str(t)
        old = A("bi1", 0, 64) if t else A("bk0", 0, 64)
        tt(A(n("wb"), 0, 64), A("nat", P + K * t, P + K * t + K), old, OP.subtract)
        tt(A(n("wc"), 0, 64), A(n("wd"), 0, 64), A(n("wb"), 0, 64), OP.mult)
        tt(A(n("we"), 0, 64), A(n("wc"), 0, 64), old, OP.add)

    def entries():
        act(A("Mu", 0, 272), A("nat", 0, 272), AF.Identity, bias=rank - 8.0)
        scatter(A("Mu", 0, 272), A("os0", 0, 4), A("we0", 0, 64))
        if rank:
            cp("s", A("Mu", 264 - rank, 264), A("Mu", 8 - rank, 8))
        gather_tt(A("vj1", 0, 32), A("Mu", 8, 264), A("zl", 0, 2), A("vz", 0, 32), OP.add)

    def newlist(t):
        n = lambda s: s + str(t)
        lo, hi, off = (8, 264, A("oz", 0, 4)) if t else (0, 272, A("os0", 0, 4))
        gather_tt(A(n("wf"), 0, 64), A("xm", lo, hi), off, A(n("we"), 0, 64), OP.mult)
        scatter(A("M", lo, hi), off, A(n("wf"), 0, 64))
        if t == 0:
            if rank:
                cp("s", A("M", 264 - rank, 264), A("M", 8 - rank, 8))
            return
        scan(A("mm", 0, P), A("sd", 0, P), A("M", 8, 8 + P), OP.mult, OP.add)
        first = 1 if rank else 0
        cp("v", A("ml", first, 16), A("mm", 15 - rank + 16 * first, P, 16))
        if rank:
            ts(A("ml", 0, 1), A("mm", 15 - rank, 16 - rank), A("mm", P - 1, P), None, OP.add)

    def places():
        act(A("mc", 0, 1), A("fb", 5, 6), AF.Identity, bias=8192.0 * 128, scale=-256.0 * 128)
        act(A("mc", 1, 2), A("fb", 6, 7), AF.Identity, bias=A("mc", 0, 1), scale=224.0 * 128)
        act(A("mc", 2, 3), A("fb", 7, 8), AF.Identity, bias=A("mc", 1, 2), scale=224.0 * 128)
        lf = A("lf0", 0, 4)
        ts(A("iw", 0, 4), lf, 32.0 / FR, A("mc", 2, 3), OP.mult, OP.add)
        ts(A("iw", 4, 8), lf, 256.0 / FR, 128.0 * 4352, OP.mult, OP.add)
        ts(A("iw", 8, 12), lf, 512.0 / FR, None, OP.mult)
        ts(A("iw", 12, 16), A("iw", 0, 4), 224, None, OP.bitwise_and)
        ts(A("iw", 16, 20), A("iw", 0, 4), 7, 65504, OP.logical_shift_right, OP.bitwise_and)
        ts(A("iw", 20, 24), A("iw", 4, 8), 7, 130816, OP.logical_shift_right, OP.bitwise_and)
        ts(A("iw", 24, 28), A("iw", 8, 12), 3584, None, OP.bitwise_and)
        tt(A("iw", 28, 32), A("iw", 16, 20), A("iw", 12, 16), OP.subtract)
        tt(A("iw", 32, 36), A("iw", 20, 24), A("iw", 24, 28), OP.subtract)
        ts(A("wa", 0, 4), A("iw", 12, 16), 32.0, None, OP.add)
        ts(A("iw", 36, 40), A("iw", 28, 32), 5, 31, OP.logical_shift_right, OP.bitwise_and)
        ts(A("iw", 40, 44), A("iw", 28, 32), 1, 3584, OP.logical_shift_right, OP.bitwise_and)
        ts(A("iw", 44, 48), A("iw", 32, 36), 1792, None, OP.bitwise_and)
        tt(A("wa", 4, 8), A("iw", 36, 40), A("iw", 40, 44), OP.add)
        tt(A("wa", 8, 12), A("wa", 0, 4), A("iw", 44, 48), OP.min)
        tt(A("wa", 12, 16), A("wa", 4, 8), A("wa", 8, 12), OP.add)
        cp("v", A("wo", 0, 4), A("wa", 12, 16))

    def turned():
        ts(A("e1", 0, 16), A("r2", 0, 16), A("fb", 1, 2), None, OP.is_equal)
        ts(A("n1", 0, 16), A("r2", 0, 16), A("fb", 1, 2), None, OP.not_equal)
        for c in range(4):
            tt(A("Z", 46 + c, NB, 32), A("L1", c, 32, 4), A("n1", 0, 16, 2), OP.mult)
        tt(A("pz", 0, 16), A("L1", 0, 32, 2), A("e1", 0, 16), OP.mult)
        for h in range(2):
            act(A("pj", 8 * h, 8 * h + 8), A("pz", h, 16, 2), AF.Copy, total=A("Z", 14 + 2 * h, 15 + 2 * h))
        turn(A("Wn", 0, NB), A("Z", 0, NB))

    def products(parts):
        for h in parts:
            if h < 2:
                mm(A("py", 512 * h, 512 * h + 128), "wq", 0, "W", 128 * h, 128 * h + 128)
                cp("s", A("ya", 128 * h, 128 * h + 128), A("py", 512 * h, 512 * h + 128))
            else:
                mm(A("pc", 512, 640), "wq", 0, "W", P + K - 128, P + K)
                cp("s", A("ya", P, P + K), A("pc", 640 - K, 640))

    def newcomers(t):
        others = [o for o in range(NO) if 2 * o + t != rank]
        c = P + K * t
        for s in ("", "s"):
            landed([A("W" + s, c + KO * o, c + KO * o + KO) for o in others], "new%d" % t + s, len(others) * full,
                   (LN1 if s else LN0) + (0.0 if own == t else LW + (1 - t)))

    if own:
        owner()
        owner_v()
        owner_t()
    else:
        hold(A("L0", 0, 28), [A("eq", 0, 512), A("tab", 0, 128), A("tR", 0, P)])
    judge(0, "L0")
    places()
    gate[:] = sent[-1:]
    turned()
    if own:
        tables()
        quant("wq", 0, 128, "wt", 0)
        products((0, 1))
    del gate[:]
    if own == 0:
        rebuild(0)
    else:
        arrive()
    newcols(0)
    entries()
    lists(0)
    if own:
        newlist(0)
    newcomers(0)
    hold(A("Ln", 0, 144), [A("vj1", 0, 32), A("wo", 0, 4), A("Wn", 0, NB)])
    turn(A("cv", 0, 128), A("Ln", 2, 130))
    scatter(A("Wn", 0, 4096), A("wo", 0, 4), A("cv", 1, 128, 2))
    turn(A("Tn", 0, NB), A("Wn", 0, NB))
    judge(1, "Tn")
    gate[:] = sent[-1:]
    if own:
        products((2,))
    else:
        tables()
        newlist(0)
        quant("wq", 0, 128, "wt", 0)
        products((0, 1, 2))
    del gate[:]
    newcols(1)
    if own:
        rebuild(1)
    newlist(1)
    lists(1)
    newcomers(1)
    pick2("F", 128, "W", P + 2 * K, "ml", 8, "ss")
    mm(A("pc", 0, 128), "wq", 0, "W", P, P + 2 * K)
    hold(A("ya", P + K, P + 2 * K), [A("F", 0, P)])
    cp("v", A("ya", P + K, P + 2 * K), A("pc", 128 - K, 128))
    for h, e in ((0, "v"), (1, "s")):
        gather(e, A("yb", 128 * h, 128 * h + 128), A("ya", 0, P + 2 * K), A("ml", 8 * h, 8 * h + 8))
    for h in range(2):
        dma("y", None, A("F", 128 * h, 128 * h + 128), "st_c", 32, out_ap=T.oc[:, 512 * h:512 * h + 512],
            in_ap=T.F[:, 128 * h:128 * h + 128].bitcast(dt.uint8))
    for k in range(4):
        dma("y", None, A("Fs", 0, P, 1, 32 * k, 32 * k + 4), "st_s", 64, out_ap=T.osc[4 * k:4 * k + 4, :])
    dma("y", None, A("yb", 0, 128), "st_y", 32, out_ap=T.y[:, 0:128])
    dma("s", None, A("yb", 128, 256), "st_y", 32, out_ap=T.y[:, 128:256])
    emit()
    for sem, val in final.items():
        wait("g", sem, val)
